import numpy as np
import ml_dtypes


def mxq(x, axis, fmt="e4m3"):
    dtype, down = {"e4m3": (ml_dtypes.float8_e4m3fn, 7), "e5m2": (ml_dtypes.float8_e5m2, 14)}[fmt]
    v = np.moveaxis(np.asarray(x, np.float32).astype(ml_dtypes.bfloat16).astype(np.float64), axis, -1)
    blocks = v.reshape(v.shape[:-1] + (-1, 32))
    amax = np.abs(blocks).max(-1, keepdims=True)
    byte = np.maximum(np.where(amax > 0, np.frexp(amax)[1] - 1 + 127, 0) - down, 1)
    scale = np.exp2(byte - 127.0)
    codes = (blocks / scale).astype(np.float32).astype(dtype).astype(np.float64)
    return np.moveaxis((codes * scale).reshape(v.shape), -1, axis)


WIDE = False


def mx_kscale(k):
    if not WIDE:
        return np.ones(k)
    levels = np.array([10, -10, 5, -5, 0])
    if k % 512:
        return np.exp2(np.random.permutation(np.resize(levels, k // 32))).repeat(32)
    a = np.empty((k // 512, 16))
    for p in range(k // 512):
        a[p, :8] = np.random.permutation(np.resize(levels, 8))
        for g in range(8):
            far = levels[np.abs(levels - a[p, g]) >= 10]
            a[p, g + 8] = far[np.random.randint(len(far))]
    return np.exp2(a.ravel()).repeat(32)


def f64(x):
    return np.asarray(x).astype(np.float64)


def striped(idx):
    return np.tile(idx.reshape(-1, 16).T, (8, 1)).astype(np.uint16)


def unstriped(offs):
    return offs[:16].T.reshape(-1).astype(np.int64)


E2M1 = np.array([0.0, 0.5, 1.0, 1.5, 2.0, 3.0, 4.0, 6.0, -0.0, -0.5, -1.0, -1.5, -2.0, -3.0, -4.0, -6.0])


def pack_weight(w, fmt):
    k, n = w.shape
    w = f64(np.asarray(w, np.float32).astype(ml_dtypes.bfloat16)).reshape(k // 32, 32, n)
    amax = np.abs(w).max(1)
    if fmt == "e4m3":
        byte = np.frexp(amax)[1] - 1 + 127 - 7
    else:
        mant, ex = np.frexp(amax / 6.0)
        byte = np.where(mant > 0.5, ex, ex - 1) + 127
    byte = np.clip(np.where(amax > 0, byte, 1), 1, 254)
    scaled = (w * np.exp2(127.0 - byte)[:, None, :]).reshape(k, n).astype(np.float32)
    by_word = np.ascontiguousarray(scaled.reshape(k // 512, 128, 4, n).transpose(0, 1, 3, 2))
    if fmt == "e4m3":
        words = by_word.astype(ml_dtypes.float8_e4m3fn).view(np.uint8)
    else:
        c = by_word.astype(ml_dtypes.float4_e2m1fn).view(np.uint8) & 0xF
        words = (c[..., 0::2] | (c[..., 1::2] << 4)).reshape(k // 512, 128, 2 * n)
    return np.ascontiguousarray(words), np.ascontiguousarray(byte.astype(np.uint8).reshape(k // 512, 16, n))


def unpack_weight(words, scales, fmt):
    g, _, n = scales.shape
    words = np.ascontiguousarray(words).reshape(g, 128, n, -1)
    if fmt == "e4m3":
        vals = words.view(ml_dtypes.float8_e4m3fn).astype(np.float64)
    else:
        nib = np.empty((g, 128, n, 4), np.uint8)
        nib[..., 0::2] = words & 0xF
        nib[..., 1::2] = words >> 4
        vals = E2M1[nib]
    vals = vals * np.repeat(np.exp2(scales.astype(np.float64) - 127.0), 8, axis=1)[..., None]
    return vals.transpose(0, 1, 3, 2).reshape(g * 512, n)


def relu2(v):
    return np.maximum(v, 0.0) ** 2


K, T, S, H, N = 512, 1024, 512, 512, 512


def setup_inputs():
    n = np.random.standard_normal
    s = mx_kscale(K)
    u = mx_kscale(H)
    hard = np.random.permutation(T)[:S]
    x = pack_weight(n((K, T)) * s[:, None], "e4m3")
    w1 = pack_weight(n((K, H)) / np.sqrt(K) / s[:, None] * u, "e2m1")
    w2 = pack_weight(n((H, N)) / np.sqrt(H) / u[:, None] ** 2, "e2m1")
    return {
        "x_words": x[0],
        "x_scales": x[1],
        "w": (n((K, N)) / np.sqrt(K) / s[:, None]).astype(np.float32),
        "w1_words": w1[0],
        "w1_scales": w1[1],
        "w2_words": w2[0],
        "w2_scales": w2[1],
        "offs": striped(hard),
    }


def reference(x_words, x_scales, w, w1_words, w1_scales, w2_words, w2_scales, offs):
    wq = mxq(f64(w), 0, "e4m3")
    w1 = unpack_weight(w1_words, w1_scales, "e2m1")
    w2 = unpack_weight(w2_words, w2_scales, "e2m1")
    idx = unstriped(offs)
    x = unpack_weight(x_words, x_scales, "e4m3")
    out = wq.T @ x
    h = relu2(w1.T @ x[:, idx])
    out[:, idx] = w2.T @ mxq(h, 0, "e4m3")
    return out

@@ -1,0 +1,229 @@
+from contextlib import ExitStack
+
+import concourse.mybir as mybir
+
+K, T, S, H, N = 512, 1024, 512, 512, 512
+FLOPS = 2 * K * N * T + 2 * K * H * S + 2 * H * N * S
+
+F32 = mybir.dt.float32
+BF16 = mybir.dt.bfloat16
+I32 = mybir.dt.int32
+U32 = mybir.dt.uint32
+U16 = mybir.dt.uint16
+U8 = mybir.dt.uint8
+FP8X4 = mybir.dt.float8_e4m3fn_x4
+FP4X4 = mybir.dt.float4_e2m1fn_x4
+ACT = mybir.ActivationFunctionType
+ALU = mybir.AluOpType
+
+P = 128
+PACK = 4
+BANK = 512
+CHUNK = 128
+CHUNKS = S // CHUNK
+BLOCKS = N // P
+LIST_COLS = CHUNK // 16
+
+
+def load_scale_rows(nc, plane, rows):
+    for q in range(4):
+        nc.sync.dma_start(out=plane[32 * q : 32 * q + 4, :].bitcast(I32), in_=rows[4 * q : 4 * q + 4, :].bitcast(I32))
+
+
+def tile_moe_cas_mlp_relu2_kernel(tc, x_words, x_scales, w, w1_words, w1_scales, w2_words, w2_scales, offs, out):
+    nc = tc.nc
+    with ExitStack() as ctx:
+        keep = ctx.enter_context(tc.tile_pool(name="keep", bufs=1))
+        psum = ctx.enter_context(tc.psum_pool(name="psum", bufs=1))
+
+        offsets = keep.tile([P, S // 16], U16, name="offsets")
+        x_codes = keep.tile([P, T], U32, name="x_codes", align_bytes=64)
+        x_plane = keep.tile([P, T], U8, name="x_plane", align_bytes=64)
+        w1_raw = keep.tile([P, 2 * H], U8, name="w1_raw", align_bytes=64)
+        w1_raw_plane = keep.tile([P, H], U8, name="w1_raw_plane", tag="w1_raw_plane", align_bytes=64)
+        w1_codes = keep.tile([P, 2 * H], U8, name="w1_codes", align_bytes=64)
+        w1_plane = keep.tile([P, H], U8, name="w1_plane", align_bytes=64)
+        w2_codes = keep.tile([P, 2 * N], U8, name="w2_codes", align_bytes=64)
+        w2_plane = keep.tile([P, N], U8, name="w2_plane", align_bytes=64)
+        light_raw = [keep.tile([P, PACK, P], F32, name="light_raw%d" % b) for b in range(BLOCKS)]
+        light_codes = keep.tile([P, N], U32, name="light_codes", align_bytes=64)
+        light_plane = keep.tile([P, N], U8, name="light_plane", align_bytes=64)
+        windows = [keep.tile([P, T], F32, name="window%d" % b) for b in range(BLOCKS)]
+        slot_plane = keep.tile([P, S], U8, name="slot_plane", align_bytes=64)
+        h_codes = keep.tile([P, S], U32, name="h_codes", align_bytes=64)
+        h_plane = keep.tile([P, S], U8, name="h_plane", align_bytes=64)
+
+        nc.vector.memset(w1_raw_plane[:].bitcast(I32), 0)
+        nc.vector.memset(x_plane[:].bitcast(I32), 0)
+        nc.vector.memset(w2_plane[:].bitcast(I32), 0)
+
+        w_rows = w.rearrange("(p j) n -> p j n", j=PACK)
+
+        def load_light(b):
+            nc.sync.dma_start(out=light_raw[b][:], in_=w_rows[:, :, b * P : (b + 1) * P])
+
+        def load_words(tile, words):
+            nc.sync.dma_start(out=tile[:].bitcast(I32), in_=words.bitcast(I32))
+
+        nc.sync.dma_start(offsets[:], offs)
+        load_words(w1_raw, w1_words[0])
+        load_scale_rows(nc, w1_raw_plane, w1_scales[0])
+        load_words(x_codes, x_words[0].rearrange("p t d -> p (t d)"))
+        load_scale_rows(nc, x_plane, x_scales[0])
+        load_light(0)
+        load_words(w2_codes, w2_words[0])
+        load_scale_rows(nc, w2_plane, w2_scales[0])
+        load_light(1)
+        load_light(2)
+        load_light(3)
+
+        def copy(engine, dst, src):
+            if engine == "v":
+                nc.vector.tensor_copy(out=dst, in_=src)
+            else:
+                nc.scalar.copy(out=dst, in_=src)
+
+        def cast_light(b, engine, tag):
+            grouped = keep.tile([P, P, PACK], BF16, name="grouped", tag=tag, align_bytes=64)
+            dst = grouped[:].rearrange("p (c i) j -> p c j i", i=4)
+            src = light_raw[b][:].rearrange("p j (c i) -> p c j i", i=4)
+            copy(engine, dst, src)
+            cols = slice(b * P, (b + 1) * P)
+            nc.vector.quantize_mx(
+                out=light_codes[:, cols].bitcast(FP8X4),
+                scales=light_plane[:, cols],
+                in_=grouped[:].rearrange("p n j -> p (n j)"),
+            )
+
+        def light_layer(b, half, engine, bank="light", bufs=2):
+            cols = slice(b * P, (b + 1) * P)
+            tokens = slice(half * BANK, (half + 1) * BANK)
+            acc = psum.tile([P, BANK], F32, name="light_acc", tag=bank, bufs=bufs)
+            nc.tensor.matmul_mx(
+                out=acc[:],
+                lhsT=light_codes[:, cols].bitcast(FP8X4),
+                lhsT_scale=light_plane[:, cols],
+                rhs=x_codes[:, tokens].bitcast(FP8X4),
+                rhs_scale=x_plane[:, tokens],
+                start=True,
+                stop=True,
+            )
+            copy(engine, windows[b][:, tokens], acc[:])
+
+        def entries(first, last):
+            return offsets[:, first * LIST_COLS : last * LIST_COLS]
+
+        slot_codes = {}
+
+        def gather_words(first, last, tag):
+            words = keep.tile([P, (last - first) * CHUNK], U32, name="slot_codes", tag=tag, align_bytes=64)
+            nc.vector.tensor_copy(words[:], x_codes[:].indirect(entries(first, last)))
+            for c in range(first, last):
+                slot_codes.setdefault(c, words[:, (c - first) * CHUNK : (c - first + 1) * CHUNK])
+
+        def gather_scales(first, last):
+            nc.vector.tensor_copy(slot_plane[:, first * CHUNK : last * CHUNK], x_plane[:].indirect(entries(first, last)))
+
+        def hidden(c, relu_engine, square_engine, bank, bufs, relu_tag):
+            acc = psum.tile([P, PACK, CHUNK], F32, name="h_acc", tag=bank, bufs=bufs)
+            for t in range(PACK):
+                nc.tensor.matmul_mx(
+                    out=acc[:, t, :],
+                    lhsT=w1_codes[:, 2 * t * P : 2 * (t + 1) * P].bitcast(FP4X4),
+                    lhsT_scale=w1_plane[:, t * P : (t + 1) * P],
+                    rhs=slot_codes[c].bitcast(FP8X4),
+                    rhs_scale=slot_plane[:, c * CHUNK : (c + 1) * CHUNK],
+                    start=True,
+                    stop=True,
+                )
+            r = keep.tile([P, CHUNK, PACK], F32, name="relu", tag=relu_tag, align_bytes=64)
+            h = keep.tile([P, CHUNK * PACK], BF16, name="h", tag="h%d" % c, align_bytes=64)
+            flat = r[:].rearrange("p s t -> p (s t)")
+            if relu_engine == "v":
+                nc.vector.tensor_scalar_max(r[:], acc[:].rearrange("p t s -> p s t"), 0.0)
+            else:
+                nc.scalar.activation(out=r[:], in_=acc[:].rearrange("p t s -> p s t"), func=ACT.Relu)
+            if square_engine == "v":
+                nc.vector.tensor_tensor(h[:], flat, flat, ALU.mult)
+            else:
+                nc.scalar.activation(out=h[:], in_=flat, func=ACT.Square)
+            slots = slice(c * CHUNK, (c + 1) * CHUNK)
+            nc.vector.quantize_mx(out=h_codes[:, slots].bitcast(FP8X4), scales=h_plane[:, slots], in_=h[:])
+
+        def second_product(blocks, first, last, bank):
+            slots = slice(first * CHUNK, last * CHUNK)
+            acc = psum.tile([P, len(blocks), slots.stop - slots.start], F32, name="z_acc", tag=bank)
+            for n, b in enumerate(blocks):
+                nc.tensor.matmul_mx(
+                    out=acc[:, n, :],
+                    lhsT=w2_codes[:, 2 * b * P : 2 * (b + 1) * P].bitcast(FP4X4),
+                    lhsT_scale=w2_plane[:, b * P : (b + 1) * P],
+                    rhs=h_codes[:, slots].bitcast(FP8X4),
+                    rhs_scale=h_plane[:, slots],
+                    start=True,
+                    stop=True,
+                )
+            return acc
+
+        def leave(acc, tag, engine="s"):
+            z = keep.tile(list(acc.shape), F32, name="z", tag=tag, align_bytes=64)
+            copy(engine, z[:], acc)
+            return z
+
+        def scatter(b, first, last, z):
+            nc.vector.tensor_copy(windows[b][:].indirect(entries(first, last)), z)
+
+        def part(acc, first, last):
+            return acc[:, first * CHUNK : last * CHUNK]
+
+        def store(b):
+            nc.sync.dma_start(out=out[b * P : (b + 1) * P, :], in_=windows[b][:])
+
+        def permute_w1():
+            nc.vector.tensor_copy(
+                out=w1_codes[:].bitcast(U16).rearrange("p (t m) -> p t m", t=PACK),
+                in_=w1_raw[:].bitcast(U16).rearrange("p (m t) -> p t m", t=PACK),
+            )
+            nc.vector.tensor_copy(
+                out=w1_plane[:].rearrange("p (t m) -> p t m", t=PACK),
+                in_=w1_raw_plane[:].rearrange("p (m t) -> p t m", t=PACK),
+            )
+
+        permute_w1()
+        gather_words(0, 1, "s0")
+        gather_scales(0, 1)
+        gather_words(1, 2, "s1")
+        gather_scales(1, 2)
+        cast_light(0, "s", "g0")
+        hidden(0, "s", "v", "pa", 1, "r0")
+        light_layer(0, 0, "s")
+        light_layer(0, 1, "s")
+        scatter(0, 0, 1, leave(second_product([0], 0, 1, "za")[:, 0, :], "z00")[:])
+        gather_scales(2, 4)
+        gather_words(2, 4, "g0")
+        hidden(1, "s", "v", "pb", 1, "r1")
+        scatter(0, 1, 2, leave(second_product([0], 1, 2, "zb")[:, 0, :], "z01")[:])
+        hidden(2, "s", "s", "pc", 1, "r2")
+        scatter(0, 2, 3, leave(second_product([0], 2, 3, "pa")[:, 0, :], "z02")[:])
+        hidden(3, "s", "s", "za", 1, "r3")
+        scatter(0, 3, 4, leave(second_product([0], 3, 4, "pb")[:, 0, :], "z03")[:])
+        store(0)
+        cast_light(1, "v", "g1")
+        light_layer(1, 0, "s")
+        light_layer(1, 1, "s")
+        a1 = second_product([1], 0, 4, "zb")[:, 0, :]
+        scatter(1, 0, 1, leave(part(a1, 0, 1), "z1a")[:])
+        cast_light(2, "s", "r3")
+        scatter(1, 1, 4, leave(part(a1, 1, 4), "z1b")[:])
+        store(1)
+        light_layer(2, 0, "s")
+        light_layer(2, 1, "s")
+        a2 = second_product([2], 0, 4, "pc")[:, 0, :]
+        scatter(2, 0, 1, leave(part(a2, 0, 1), "z2a")[:])
+        cast_light(3, "s", "r3")
+        scatter(2, 1, 4, leave(part(a2, 1, 4), "z2b")[:])
+        store(2)
+        light_layer(3, 0, "s")
+        light_layer(3, 1, "s")
+        scatter(3, 0, 4, leave(second_product([3], 0, 4, "za")[:, 0, :], "z3")[:])
+        store(3)

@@ -71,9 +71,9 @@ def tile_moe_cas_mlp_relu2_kernel(tc, x_words, x_scales, w, w1_words, w1_scales,
         load_words(x_codes, x_words[0].rearrange("p t d -> p (t d)"))
         load_scale_rows(nc, x_plane, x_scales[0])
         load_light(0)
+        load_light(1)
         load_words(w2_codes, w2_words[0])
         load_scale_rows(nc, w2_plane, w2_scales[0])
-        load_light(1)
         load_light(2)
         load_light(3)
 
@@ -124,7 +124,7 @@ def tile_moe_cas_mlp_relu2_kernel(tc, x_words, x_scales, w, w1_words, w1_scales,
         def gather_scales(first, last):
             nc.vector.tensor_copy(slot_plane[:, first * CHUNK : last * CHUNK], x_plane[:].indirect(entries(first, last)))
 
-        def hidden(c, relu_engine, square_engine, bank, bufs, relu_tag):
+        def hidden(c, relu_engine, square_engine, bank, bufs, relu_tag, h_tag=None):
             acc = psum.tile([P, PACK, CHUNK], F32, name="h_acc", tag=bank, bufs=bufs)
             for t in range(PACK):
                 nc.tensor.matmul_mx(
@@ -137,7 +137,7 @@ def tile_moe_cas_mlp_relu2_kernel(tc, x_words, x_scales, w, w1_words, w1_scales,
                     stop=True,
                 )
             r = keep.tile([P, CHUNK, PACK], F32, name="relu", tag=relu_tag, align_bytes=64)
-            h = keep.tile([P, CHUNK * PACK], BF16, name="h", tag="h%d" % c, align_bytes=64)
+            h = keep.tile([P, CHUNK * PACK], BF16, name="h", tag=h_tag or "h%d" % c, align_bytes=64)
             flat = r[:].rearrange("p s t -> p (s t)")
             if relu_engine == "v":
                 nc.vector.tensor_scalar_max(r[:], acc[:].rearrange("p t s -> p s t"), 0.0)
@@ -195,35 +195,38 @@ def tile_moe_cas_mlp_relu2_kernel(tc, x_words, x_scales, w, w1_words, w1_scales,
         gather_words(1, 2, "s1")
         gather_scales(1, 2)
         cast_light(0, "s", "g0")
+        cast_light(1, "s", "g1")
         hidden(0, "s", "v", "pa", 1, "r0")
+        hidden(1, "s", "v", "pb", 1, "r1", "h0")
         light_layer(0, 0, "s")
         light_layer(0, 1, "s")
-        scatter(0, 0, 1, leave(second_product([0], 0, 1, "za")[:, 0, :], "z00")[:])
+        z = leave(second_product([0, 1], 0, 1, "za")[:], "z0")
+        scatter(0, 0, 1, z[:, 0, :])
+        light_layer(1, 0, "v")
+        light_layer(1, 1, "s")
+        scatter(1, 0, 1, z[:, 1, :])
         gather_scales(2, 4)
         gather_words(2, 4, "g0")
-        hidden(1, "s", "v", "pb", 1, "r1")
-        scatter(0, 1, 2, leave(second_product([0], 1, 2, "zb")[:, 0, :], "z01")[:])
         hidden(2, "s", "s", "pc", 1, "r2")
-        scatter(0, 2, 3, leave(second_product([0], 2, 3, "pa")[:, 0, :], "z02")[:])
+        z = leave(second_product([0, 1], 1, 2, "zb")[:], "z1")
+        scatter(0, 1, 2, z[:, 0, :])
+        scatter(1, 1, 2, z[:, 1, :])
         hidden(3, "s", "s", "za", 1, "r3")
-        scatter(0, 3, 4, leave(second_product([0], 3, 4, "pb")[:, 0, :], "z03")[:])
+        cast_light(2, "s", "r2")
+        z = leave(second_product([0, 1], 2, 3, "pa")[:], "z2")
+        scatter(0, 2, 3, z[:, 0, :])
+        scatter(1, 2, 3, z[:, 1, :])
+        cast_light(3, "s", "r3")
+        z = leave(second_product([0, 1], 3, 4, "pb")[:], "z3")
+        scatter(0, 3, 4, z[:, 0, :])
         store(0)
-        cast_light(1, "v", "g1")
-        light_layer(1, 0, "s")
-        light_layer(1, 1, "s")
-        a1 = second_product([1], 0, 4, "zb")[:, 0, :]
-        scatter(1, 0, 1, leave(part(a1, 0, 1), "z1a")[:])
-        cast_light(2, "s", "r3")
-        scatter(1, 1, 4, leave(part(a1, 1, 4), "z1b")[:])
+        scatter(1, 3, 4, z[:, 1, :])
         store(1)
         light_layer(2, 0, "s")
         light_layer(2, 1, "s")
-        a2 = second_product([2], 0, 4, "pc")[:, 0, :]
-        scatter(2, 0, 1, leave(part(a2, 0, 1), "z2a")[:])
-        cast_light(3, "s", "r3")
-        scatter(2, 1, 4, leave(part(a2, 1, 4), "z2b")[:])
+        scatter(2, 0, 4, leave(second_product([2], 0, 4, "pc")[:, 0, :], "z4")[:])
         store(2)
         light_layer(3, 0, "s")
         light_layer(3, 1, "s")
-        scatter(3, 0, 4, leave(second_product([3], 0, 4, "za")[:, 0, :], "z3")[:])
+        scatter(3, 0, 4, leave(second_product([3], 0, 4, "zb")[:, 0, :], "z5")[:])
         store(3)

@@ -23,6 +23,9 @@ CHUNK = 128
 CHUNKS = S // CHUNK
 BLOCKS = N // P
 LIST_COLS = CHUNK // 16
+RUN = 4
+EARLY_BLOCKS = (0, 1)
+LIGHT_BANKS = 2
 
 
 def load_scale_rows(nc, plane, rows):
@@ -40,7 +43,7 @@ def tile_moe_cas_mlp_relu2_kernel(tc, x_words, x_scales, w, w1_words, w1_scales,
         x_codes = keep.tile([P, T], U32, name="x_codes", align_bytes=64)
         x_plane = keep.tile([P, T], U8, name="x_plane", align_bytes=64)
         w1_raw = keep.tile([P, 2 * H], U8, name="w1_raw", align_bytes=64)
-        w1_raw_plane = keep.tile([P, H], U8, name="w1_raw_plane", tag="w1_raw_plane", align_bytes=64)
+        w1_raw_plane = keep.tile([P, H], U8, name="w1_raw_plane", align_bytes=64)
         w1_codes = keep.tile([P, 2 * H], U8, name="w1_codes", align_bytes=64)
         w1_plane = keep.tile([P, H], U8, name="w1_plane", align_bytes=64)
         w2_codes = keep.tile([P, 2 * N], U8, name="w2_codes", align_bytes=64)
@@ -70,114 +73,12 @@ def tile_moe_cas_mlp_relu2_kernel(tc, x_words, x_scales, w, w1_words, w1_scales,
         load_scale_rows(nc, w1_raw_plane, w1_scales[0])
         load_words(x_codes, x_words[0].rearrange("p t d -> p (t d)"))
         load_scale_rows(nc, x_plane, x_scales[0])
-        load_light(0)
-        load_light(1)
+        for b in EARLY_BLOCKS:
+            load_light(b)
         load_words(w2_codes, w2_words[0])
         load_scale_rows(nc, w2_plane, w2_scales[0])
-        load_light(2)
-        load_light(3)
-
-        def copy(engine, dst, src):
-            if engine == "v":
-                nc.vector.tensor_copy(out=dst, in_=src)
-            else:
-                nc.scalar.copy(out=dst, in_=src)
-
-        def cast_light(b, engine, tag):
-            grouped = keep.tile([P, P, PACK], BF16, name="grouped", tag=tag, align_bytes=64)
-            dst = grouped[:].rearrange("p (c i) j -> p c j i", i=4)
-            src = light_raw[b][:].rearrange("p j (c i) -> p c j i", i=4)
-            copy(engine, dst, src)
-            cols = slice(b * P, (b + 1) * P)
-            nc.vector.quantize_mx(
-                out=light_codes[:, cols].bitcast(FP8X4),
-                scales=light_plane[:, cols],
-                in_=grouped[:].rearrange("p n j -> p (n j)"),
-            )
-
-        def light_layer(b, half, engine, bank="light", bufs=2):
-            cols = slice(b * P, (b + 1) * P)
-            tokens = slice(half * BANK, (half + 1) * BANK)
-            acc = psum.tile([P, BANK], F32, name="light_acc", tag=bank, bufs=bufs)
-            nc.tensor.matmul_mx(
-                out=acc[:],
-                lhsT=light_codes[:, cols].bitcast(FP8X4),
-                lhsT_scale=light_plane[:, cols],
-                rhs=x_codes[:, tokens].bitcast(FP8X4),
-                rhs_scale=x_plane[:, tokens],
-                start=True,
-                stop=True,
-            )
-            copy(engine, windows[b][:, tokens], acc[:])
-
-        def entries(first, last):
-            return offsets[:, first * LIST_COLS : last * LIST_COLS]
-
-        slot_codes = {}
-
-        def gather_words(first, last, tag):
-            words = keep.tile([P, (last - first) * CHUNK], U32, name="slot_codes", tag=tag, align_bytes=64)
-            nc.vector.tensor_copy(words[:], x_codes[:].indirect(entries(first, last)))
-            for c in range(first, last):
-                slot_codes.setdefault(c, words[:, (c - first) * CHUNK : (c - first + 1) * CHUNK])
-
-        def gather_scales(first, last):
-            nc.vector.tensor_copy(slot_plane[:, first * CHUNK : last * CHUNK], x_plane[:].indirect(entries(first, last)))
-
-        def hidden(c, relu_engine, square_engine, bank, bufs, relu_tag, h_tag=None):
-            acc = psum.tile([P, PACK, CHUNK], F32, name="h_acc", tag=bank, bufs=bufs)
-            for t in range(PACK):
-                nc.tensor.matmul_mx(
-                    out=acc[:, t, :],
-                    lhsT=w1_codes[:, 2 * t * P : 2 * (t + 1) * P].bitcast(FP4X4),
-                    lhsT_scale=w1_plane[:, t * P : (t + 1) * P],
-                    rhs=slot_codes[c].bitcast(FP8X4),
-                    rhs_scale=slot_plane[:, c * CHUNK : (c + 1) * CHUNK],
-                    start=True,
-                    stop=True,
-                )
-            r = keep.tile([P, CHUNK, PACK], F32, name="relu", tag=relu_tag, align_bytes=64)
-            h = keep.tile([P, CHUNK * PACK], BF16, name="h", tag=h_tag or "h%d" % c, align_bytes=64)
-            flat = r[:].rearrange("p s t -> p (s t)")
-            if relu_engine == "v":
-                nc.vector.tensor_scalar_max(r[:], acc[:].rearrange("p t s -> p s t"), 0.0)
-            else:
-                nc.scalar.activation(out=r[:], in_=acc[:].rearrange("p t s -> p s t"), func=ACT.Relu)
-            if square_engine == "v":
-                nc.vector.tensor_tensor(h[:], flat, flat, ALU.mult)
-            else:
-                nc.scalar.activation(out=h[:], in_=flat, func=ACT.Square)
-            slots = slice(c * CHUNK, (c + 1) * CHUNK)
-            nc.vector.quantize_mx(out=h_codes[:, slots].bitcast(FP8X4), scales=h_plane[:, slots], in_=h[:])
-
-        def second_product(blocks, first, last, bank):
-            slots = slice(first * CHUNK, last * CHUNK)
-            acc = psum.tile([P, len(blocks), slots.stop - slots.start], F32, name="z_acc", tag=bank)
-            for n, b in enumerate(blocks):
-                nc.tensor.matmul_mx(
-                    out=acc[:, n, :],
-                    lhsT=w2_codes[:, 2 * b * P : 2 * (b + 1) * P].bitcast(FP4X4),
-                    lhsT_scale=w2_plane[:, b * P : (b + 1) * P],
-                    rhs=h_codes[:, slots].bitcast(FP8X4),
-                    rhs_scale=h_plane[:, slots],
-                    start=True,
-                    stop=True,
-                )
-            return acc
-
-        def leave(acc, tag, engine="s"):
-            z = keep.tile(list(acc.shape), F32, name="z", tag=tag, align_bytes=64)
-            copy(engine, z[:], acc)
-            return z
-
-        def scatter(b, first, last, z):
-            nc.vector.tensor_copy(windows[b][:].indirect(entries(first, last)), z)
-
-        def part(acc, first, last):
-            return acc[:, first * CHUNK : last * CHUNK]
-
-        def store(b):
-            nc.sync.dma_start(out=out[b * P : (b + 1) * P, :], in_=windows[b][:])
+        for b in range(len(EARLY_BLOCKS), BLOCKS):
+            load_light(b)
 
         def permute_w1():
             nc.vector.tensor_copy(
@@ -189,44 +90,134 @@ def tile_moe_cas_mlp_relu2_kernel(tc, x_words, x_scales, w, w1_words, w1_scales,
                 in_=w1_raw_plane[:].rearrange("p (m t) -> p t m", t=PACK),
             )
 
+        def entries(first, last):
+            return offsets[:, first * LIST_COLS : last * LIST_COLS]
+
+        def gather_words(first, last, tag):
+            words = keep.tile([P, (last - first) * CHUNK], U32, name="slot_codes", tag=tag, align_bytes=64)
+            nc.vector.tensor_copy(words[:], x_codes[:].indirect(entries(first, last)))
+            return [words[:, c * CHUNK : (c + 1) * CHUNK] for c in range(last - first)]
+
+        def gather_scales(first, last):
+            nc.vector.tensor_copy(slot_plane[:, first * CHUNK : last * CHUNK], x_plane[:].indirect(entries(first, last)))
+
+        def quantize_light(b, tag):
+            grouped = keep.tile([P, P, PACK], BF16, name="grouped", tag=tag, align_bytes=64)
+            nc.scalar.copy(
+                out=grouped[:].rearrange("p (c i) j -> p c j i", i=RUN),
+                in_=light_raw[b][:].rearrange("p j (c i) -> p c j i", i=RUN),
+            )
+            cols = slice(b * P, (b + 1) * P)
+            nc.vector.quantize_mx(
+                out=light_codes[:, cols].bitcast(FP8X4),
+                scales=light_plane[:, cols],
+                in_=grouped[:].rearrange("p n j -> p (n j)"),
+            )
+
+        def light_product(b, half, copy_out):
+            cols = slice(b * P, (b + 1) * P)
+            tokens = slice(half * BANK, (half + 1) * BANK)
+            acc = psum.tile([P, BANK], F32, name="light_acc", tag="light", bufs=LIGHT_BANKS)
+            nc.tensor.matmul_mx(
+                out=acc[:],
+                lhsT=light_codes[:, cols].bitcast(FP8X4),
+                lhsT_scale=light_plane[:, cols],
+                rhs=x_codes[:, tokens].bitcast(FP8X4),
+                rhs_scale=x_plane[:, tokens],
+                start=True,
+                stop=True,
+            )
+            copy_out(out=windows[b][:, tokens], in_=acc[:])
+
+        def square_on_vector(h, relu):
+            nc.vector.tensor_tensor(h, relu, relu, ALU.mult)
+
+        def square_on_scalar(h, relu):
+            nc.scalar.activation(out=h, in_=relu, func=ACT.Square)
+
+        def hidden(c, words, square, bank, h_tag):
+            slots = slice(c * CHUNK, (c + 1) * CHUNK)
+            acc = psum.tile([P, PACK, CHUNK], F32, name="h_acc", tag=bank)
+            for t in range(PACK):
+                nc.tensor.matmul_mx(
+                    out=acc[:, t, :],
+                    lhsT=w1_codes[:, 2 * t * P : 2 * (t + 1) * P].bitcast(FP4X4),
+                    lhsT_scale=w1_plane[:, t * P : (t + 1) * P],
+                    rhs=words.bitcast(FP8X4),
+                    rhs_scale=slot_plane[:, slots],
+                    start=True,
+                    stop=True,
+                )
+            relu = keep.tile([P, CHUNK, PACK], F32, name="relu", tag="relu%d" % c, align_bytes=64)
+            h = keep.tile([P, CHUNK * PACK], BF16, name="h", tag=h_tag, align_bytes=64)
+            nc.scalar.activation(out=relu[:], in_=acc[:].rearrange("p t s -> p s t"), func=ACT.Relu)
+            square(h[:], relu[:].rearrange("p s t -> p (s t)"))
+            nc.vector.quantize_mx(out=h_codes[:, slots].bitcast(FP8X4), scales=h_plane[:, slots], in_=h[:])
+
+        def heavy_product(blocks, first, last, bank):
+            slots = slice(first * CHUNK, last * CHUNK)
+            shape = [P, len(blocks), slots.stop - slots.start]
+            acc = psum.tile(shape, F32, name="z_acc", tag=bank)
+            for place, b in enumerate(blocks):
+                nc.tensor.matmul_mx(
+                    out=acc[:, place, :],
+                    lhsT=w2_codes[:, 2 * b * P : 2 * (b + 1) * P].bitcast(FP4X4),
+                    lhsT_scale=w2_plane[:, b * P : (b + 1) * P],
+                    rhs=h_codes[:, slots].bitcast(FP8X4),
+                    rhs_scale=h_plane[:, slots],
+                    start=True,
+                    stop=True,
+                )
+            z = keep.tile(shape, F32, name="z", tag="z%d_%d" % (blocks[0], first), align_bytes=64)
+            nc.scalar.copy(out=z[:], in_=acc[:])
+            return z
+
+        def scatter(b, first, last, z):
+            nc.vector.tensor_copy(windows[b][:].indirect(entries(first, last)), z)
+
+        def store(b):
+            nc.sync.dma_start(out=out[b * P : (b + 1) * P, :], in_=windows[b][:])
+
         permute_w1()
-        gather_words(0, 1, "s0")
+        words = gather_words(0, 1, "words0")
         gather_scales(0, 1)
-        gather_words(1, 2, "s1")
+        words = words + gather_words(1, 2, "words1")
         gather_scales(1, 2)
-        cast_light(0, "s", "g0")
-        cast_light(1, "s", "g1")
-        hidden(0, "s", "v", "pa", 1, "r0")
-        hidden(1, "s", "v", "pb", 1, "r1", "h0")
-        light_layer(0, 0, "s")
-        light_layer(0, 1, "s")
-        z = leave(second_product([0, 1], 0, 1, "za")[:], "z0")
+        for b in EARLY_BLOCKS:
+            quantize_light(b, "grouped%d" % b)
+
+        hidden(0, words[0], square_on_vector, "bank_a", "h0")
+        hidden(1, words[1], square_on_vector, "bank_b", "h0")
+        light_product(0, 0, nc.scalar.copy)
+        light_product(0, 1, nc.scalar.copy)
+        z = heavy_product(EARLY_BLOCKS, 0, 1, "bank_c")
         scatter(0, 0, 1, z[:, 0, :])
-        light_layer(1, 0, "v")
-        light_layer(1, 1, "s")
+        light_product(1, 0, nc.vector.tensor_copy)
+        light_product(1, 1, nc.scalar.copy)
         scatter(1, 0, 1, z[:, 1, :])
-        gather_scales(2, 4)
-        gather_words(2, 4, "g0")
-        hidden(2, "s", "s", "pc", 1, "r2")
-        z = leave(second_product([0, 1], 1, 2, "zb")[:], "z1")
-        scatter(0, 1, 2, z[:, 0, :])
-        scatter(1, 1, 2, z[:, 1, :])
-        hidden(3, "s", "s", "za", 1, "r3")
-        cast_light(2, "s", "r2")
-        z = leave(second_product([0, 1], 2, 3, "pa")[:], "z2")
-        scatter(0, 2, 3, z[:, 0, :])
-        scatter(1, 2, 3, z[:, 1, :])
-        cast_light(3, "s", "r3")
-        z = leave(second_product([0, 1], 3, 4, "pb")[:], "z3")
-        scatter(0, 3, 4, z[:, 0, :])
-        store(0)
-        scatter(1, 3, 4, z[:, 1, :])
-        store(1)
-        light_layer(2, 0, "s")
-        light_layer(2, 1, "s")
-        scatter(2, 0, 4, leave(second_product([2], 0, 4, "pc")[:, 0, :], "z4")[:])
-        store(2)
-        light_layer(3, 0, "s")
-        light_layer(3, 1, "s")
-        scatter(3, 0, 4, leave(second_product([3], 0, 4, "zb")[:, 0, :], "z5")[:])
-        store(3)
+
+        gather_scales(2, CHUNKS)
+        words = words + gather_words(2, CHUNKS, "grouped0")
+
+        hidden(2, words[2], square_on_scalar, "bank_d", "h2")
+        z = heavy_product(EARLY_BLOCKS, 1, 2, "bank_e")
+        for b in EARLY_BLOCKS:
+            scatter(b, 1, 2, z[:, b, :])
+
+        hidden(3, words[3], square_on_scalar, "bank_c", "h3")
+        quantize_light(2, "relu2")
+        z = heavy_product(EARLY_BLOCKS, 2, 3, "bank_a")
+        for b in EARLY_BLOCKS:
+            scatter(b, 2, 3, z[:, b, :])
+
+        quantize_light(3, "relu3")
+        z = heavy_product(EARLY_BLOCKS, 3, CHUNKS, "bank_b")
+        for b in EARLY_BLOCKS:
+            scatter(b, 3, CHUNKS, z[:, b, :])
+            store(b)
+
+        for b, bank in ((2, "bank_d"), (3, "bank_e")):
+            for half in range(T // BANK):
+                light_product(b, half, nc.scalar.copy)
+            scatter(b, 0, CHUNKS, heavy_product((b,), 0, CHUNKS, bank)[:, 0, :])
+            store(b)

@@ -25,7 +25,6 @@ BLOCKS = N // P
 LIST_COLS = CHUNK // 16
 RUN = 4
 EARLY_BLOCKS = (0, 1)
-LIGHT_BANKS = 2
 
 
 def load_scale_rows(nc, plane, rows):
@@ -37,6 +36,7 @@ def tile_moe_cas_mlp_relu2_kernel(tc, x_words, x_scales, w, w1_words, w1_scales,
     nc = tc.nc
     with ExitStack() as ctx:
         keep = ctx.enter_context(tc.tile_pool(name="keep", bufs=1))
+        laid = ctx.enter_context(tc.tile_pool(name="laid", bufs=1))
         psum = ctx.enter_context(tc.psum_pool(name="psum", bufs=1))
 
         offsets = keep.tile([P, S // 16], U16, name="offsets")
@@ -48,10 +48,12 @@ def tile_moe_cas_mlp_relu2_kernel(tc, x_words, x_scales, w, w1_words, w1_scales,
         w1_plane = keep.tile([P, H], U8, name="w1_plane", align_bytes=64)
         w2_codes = keep.tile([P, 2 * N], U8, name="w2_codes", align_bytes=64)
         w2_plane = keep.tile([P, N], U8, name="w2_plane", align_bytes=64)
-        light_raw = [keep.tile([P, PACK, P], F32, name="light_raw%d" % b) for b in range(BLOCKS)]
+        early_raw = [keep.tile([P, PACK, P], F32, name="early_raw", tag="raw%d" % b, align_bytes=64) for b in EARLY_BLOCKS]
+        raw2 = laid.tile([P, PACK, P], F32, name="raw2", align_bytes=64, offset=4096)
+        raw3 = keep.tile([P, PACK, P], F32, name="raw3", align_bytes=64)
         light_codes = keep.tile([P, N], U32, name="light_codes", align_bytes=64)
         light_plane = keep.tile([P, N], U8, name="light_plane", align_bytes=64)
-        windows = [keep.tile([P, T], F32, name="window%d" % b) for b in range(BLOCKS)]
+        windows = {}
         slot_plane = keep.tile([P, S], U8, name="slot_plane", align_bytes=64)
         h_codes = keep.tile([P, S], U32, name="h_codes", align_bytes=64)
         h_plane = keep.tile([P, S], U8, name="h_plane", align_bytes=64)
@@ -63,7 +65,7 @@ def tile_moe_cas_mlp_relu2_kernel(tc, x_words, x_scales, w, w1_words, w1_scales,
         w_rows = w.rearrange("(p j) n -> p j n", j=PACK)
 
         def load_light(b):
-            nc.sync.dma_start(out=light_raw[b][:], in_=w_rows[:, :, b * P : (b + 1) * P])
+            nc.sync.dma_start(out=early_raw[b][:], in_=w_rows[:, :, b * P : (b + 1) * P])
 
         def load_words(tile, words):
             nc.sync.dma_start(out=tile[:].bitcast(I32), in_=words.bitcast(I32))
@@ -73,12 +75,12 @@ def tile_moe_cas_mlp_relu2_kernel(tc, x_words, x_scales, w, w1_words, w1_scales,
         load_scale_rows(nc, w1_raw_plane, w1_scales[0])
         load_words(x_codes, x_words[0].rearrange("p t d -> p (t d)"))
         load_scale_rows(nc, x_plane, x_scales[0])
-        for b in EARLY_BLOCKS:
-            load_light(b)
+        load_light(0)
+        load_light(1)
         load_words(w2_codes, w2_words[0])
         load_scale_rows(nc, w2_plane, w2_scales[0])
-        for b in range(len(EARLY_BLOCKS), BLOCKS):
-            load_light(b)
+        nc.sync.dma_start(out=raw2[:], in_=w_rows[:, :, 2 * P : 3 * P])
+        nc.sync.dma_start(out=raw3[:], in_=w_rows[:, :, 3 * P :])
 
         def permute_w1():
             nc.vector.tensor_copy(
@@ -101,23 +103,29 @@ def tile_moe_cas_mlp_relu2_kernel(tc, x_words, x_scales, w, w1_words, w1_scales,
         def gather_scales(first, last):
             nc.vector.tensor_copy(slot_plane[:, first * CHUNK : last * CHUNK], x_plane[:].indirect(entries(first, last)))
 
-        def quantize_light(b, tag):
-            grouped = keep.tile([P, P, PACK], BF16, name="grouped", tag=tag, align_bytes=64)
+        def cast_light(raw, width, tag, pool=keep, offset=None):
+            grouped = pool.tile([P, width, PACK], BF16, name="grouped", tag=tag, align_bytes=64, offset=offset)
             nc.scalar.copy(
                 out=grouped[:].rearrange("p (c i) j -> p c j i", i=RUN),
-                in_=light_raw[b][:].rearrange("p j (c i) -> p c j i", i=RUN),
+                in_=raw.rearrange("p j (c i) -> p c j i", i=RUN),
             )
-            cols = slice(b * P, (b + 1) * P)
+            return grouped
+
+        def quantize_light(first, last, grouped):
+            cols = slice(first * P, last * P)
             nc.vector.quantize_mx(
                 out=light_codes[:, cols].bitcast(FP8X4),
                 scales=light_plane[:, cols],
                 in_=grouped[:].rearrange("p n j -> p (n j)"),
             )
 
-        def light_product(b, half, copy_out):
+        def open_window(b, tag):
+            windows[b] = keep.tile([P, T], F32, name="window", tag=tag, align_bytes=64)
+
+        def light_product(b, half, bank, *copies):
             cols = slice(b * P, (b + 1) * P)
             tokens = slice(half * BANK, (half + 1) * BANK)
-            acc = psum.tile([P, BANK], F32, name="light_acc", tag="light", bufs=LIGHT_BANKS)
+            acc = psum.tile([P, BANK], F32, name="light_acc", tag=bank)
             nc.tensor.matmul_mx(
                 out=acc[:],
                 lhsT=light_codes[:, cols].bitcast(FP8X4),
@@ -127,7 +135,9 @@ def tile_moe_cas_mlp_relu2_kernel(tc, x_words, x_scales, w, w1_words, w1_scales,
                 start=True,
                 stop=True,
             )
-            copy_out(out=windows[b][:, tokens], in_=acc[:])
+            width = BANK // len(copies)
+            for first, copy_out in zip(range(0, BANK, width), copies):
+                copy_out(out=windows[b][:, half * BANK + first : half * BANK + first + width], in_=acc[:, first : first + width])
 
         def square_on_vector(h, relu):
             nc.vector.tensor_tensor(h, relu, relu, ALU.mult)
@@ -135,7 +145,7 @@ def tile_moe_cas_mlp_relu2_kernel(tc, x_words, x_scales, w, w1_words, w1_scales,
         def square_on_scalar(h, relu):
             nc.scalar.activation(out=h, in_=relu, func=ACT.Square)
 
-        def hidden(c, words, square, bank, h_tag):
+        def first_product(c, words, bank, relu):
             slots = slice(c * CHUNK, (c + 1) * CHUNK)
             acc = psum.tile([P, PACK, CHUNK], F32, name="h_acc", tag=bank)
             for t in range(PACK):
@@ -148,13 +158,24 @@ def tile_moe_cas_mlp_relu2_kernel(tc, x_words, x_scales, w, w1_words, w1_scales,
                     start=True,
                     stop=True,
                 )
-            relu = keep.tile([P, CHUNK, PACK], F32, name="relu", tag="relu%d" % c, align_bytes=64)
+            sums = acc[:].rearrange("p t s -> p s t")
+            nc.scalar.activation(out=relu, in_=sums, func=ACT.Relu)
+            return relu, sums
+
+        def relu_tile(chunks, tag):
+            relu = keep.tile([P, chunks, CHUNK, PACK], F32, name="relu", tag=tag, align_bytes=64)
+            return [relu[:, c] for c in range(chunks)]
+
+        def squared(relu, square, h_tag):
             h = keep.tile([P, CHUNK * PACK], BF16, name="h", tag=h_tag, align_bytes=64)
-            nc.scalar.activation(out=relu[:], in_=acc[:].rearrange("p t s -> p s t"), func=ACT.Relu)
-            square(h[:], relu[:].rearrange("p s t -> p (s t)"))
+            square(h[:], relu.rearrange("p s t -> p (s t)"))
+            return h
+
+        def quantize_hidden(c, h):
+            slots = slice(c * CHUNK, (c + 1) * CHUNK)
             nc.vector.quantize_mx(out=h_codes[:, slots].bitcast(FP8X4), scales=h_plane[:, slots], in_=h[:])
 
-        def heavy_product(blocks, first, last, bank):
+        def heavy_product(blocks, first, last, bank, copy_out, offset=None):
             slots = slice(first * CHUNK, last * CHUNK)
             shape = [P, len(blocks), slots.stop - slots.start]
             acc = psum.tile(shape, F32, name="z_acc", tag=bank)
@@ -168,8 +189,12 @@ def tile_moe_cas_mlp_relu2_kernel(tc, x_words, x_scales, w, w1_words, w1_scales,
                     start=True,
                     stop=True,
                 )
-            z = keep.tile(shape, F32, name="z", tag="z%d_%d" % (blocks[0], first), align_bytes=64)
-            nc.scalar.copy(out=z[:], in_=acc[:])
+            name = "z%d_%d" % (blocks[0], first)
+            if offset is None:
+                z = keep.tile(shape, F32, name=name, align_bytes=64)
+            else:
+                z = laid.tile(shape, F32, name=name, align_bytes=64, offset=offset)
+            copy_out(out=z[:], in_=acc[:])
             return z
 
         def scatter(b, first, last, z):
@@ -179,45 +204,63 @@ def tile_moe_cas_mlp_relu2_kernel(tc, x_words, x_scales, w, w1_words, w1_scales,
             nc.sync.dma_start(out=out[b * P : (b + 1) * P, :], in_=windows[b][:])
 
         permute_w1()
-        words = gather_words(0, 1, "words0")
+        words = gather_words(0, 2, "words01")
         gather_scales(0, 1)
-        words = words + gather_words(1, 2, "words1")
         gather_scales(1, 2)
         for b in EARLY_BLOCKS:
-            quantize_light(b, "grouped%d" % b)
-
-        hidden(0, words[0], square_on_vector, "bank_a", "h0")
-        hidden(1, words[1], square_on_vector, "bank_b", "h0")
-        light_product(0, 0, nc.scalar.copy)
-        light_product(0, 1, nc.scalar.copy)
-        z = heavy_product(EARLY_BLOCKS, 0, 1, "bank_c")
-        scatter(0, 0, 1, z[:, 0, :])
-        light_product(1, 0, nc.vector.tensor_copy)
-        light_product(1, 1, nc.scalar.copy)
-        scatter(1, 0, 1, z[:, 1, :])
-
+            quantize_light(b, b + 1, cast_light(early_raw[b][:], P, "grouped%d" % b))
         gather_scales(2, CHUNKS)
         words = words + gather_words(2, CHUNKS, "grouped0")
+        for b in (0, 2, 3):
+            open_window(b, "window%d" % b)
 
-        hidden(2, words[2], square_on_scalar, "bank_d", "h2")
-        z = heavy_product(EARLY_BLOCKS, 1, 2, "bank_e")
-        for b in EARLY_BLOCKS:
-            scatter(b, 1, 2, z[:, b, :])
+        relu0, sums0 = first_product(0, words[0], "bank_a", relu_tile(1, "relu0")[0])
+        relu1, sums1 = first_product(1, words[1], "bank_b", relu_tile(1, "relu1")[0])
+        h0 = squared(relu0, square_on_vector, "h0")
+        h1 = laid.tile([P, CHUNK, PACK], BF16, name="h1", align_bytes=64, offset=0)
+        low, high = slice(0, CHUNK // 2), slice(CHUNK // 2, CHUNK)
+        nc.vector.tensor_tensor(h1[:, low, :], sums1[:, low, :], relu1[:, low, :], ALU.mult)
+        quantize_hidden(0, h0)
+        open_window(1, "h0")
+        nc.vector.tensor_tensor(h1[:, high, :], sums1[:, high, :], relu1[:, high, :], ALU.mult)
+        light_product(0, 0, "light0", nc.scalar.copy)
+        light_product(0, 1, "light1", nc.scalar.copy)
+        light_product(1, 0, "bank_d", nc.vector.tensor_copy)
+        quantize_hidden(1, h1[:].rearrange("p s t -> p (s t)"))
+        z00 = heavy_product((0,), 0, 1, "bank_c", nc.scalar.copy)
+        light_product(1, 1, "bank_a", nc.vector.tensor_copy, nc.scalar.copy)
+        scatter(0, 0, 1, z00[:, 0, :])
+        z10 = heavy_product((1,), 0, 1, "bank_f", nc.scalar.copy)
+        scatter(1, 0, 1, z10[:, 0, :])
 
-        hidden(3, words[3], square_on_scalar, "bank_c", "h3")
-        quantize_light(2, "relu2")
-        z = heavy_product(EARLY_BLOCKS, 2, 3, "bank_a")
-        for b in EARLY_BLOCKS:
-            scatter(b, 2, 3, z[:, b, :])
+        relu2 = laid.tile([P, CHUNK, PACK], F32, name="relu2", align_bytes=64, offset=0)
+        first_product(2, words[2], "bank_b", relu2[:])
+        z01 = heavy_product((0,), 1, 2, "bank_e", nc.scalar.copy)
+        h2 = squared(relu2[:], square_on_scalar, "h2")
+        scatter(0, 1, 2, z01[:, 0, :])
+        quantize_hidden(2, h2)
+        z11 = heavy_product((1,), 1, 2, "light1", nc.scalar.copy, 0)
+        scatter(1, 1, 2, z11[:, 0, :])
 
-        quantize_light(3, "relu3")
-        z = heavy_product(EARLY_BLOCKS, 3, CHUNKS, "bank_b")
-        for b in EARLY_BLOCKS:
-            scatter(b, 3, CHUNKS, z[:, b, :])
-            store(b)
+        relu3 = laid.tile([P, CHUNK, PACK], F32, name="relu3", align_bytes=64, offset=1024)
+        first_product(3, words[3], "bank_c", relu3[:])
+        h3 = squared(relu3[:], square_on_scalar, "h3")
+        quantize_hidden(3, h3)
+        z02 = heavy_product((0,), 2, 3, "bank_e", nc.scalar.copy, 2048)
+        scatter(0, 2, 3, z02[:, 0, :])
+        quantize_light(2, 3, cast_light(raw2[:], P, "grouped2", laid, 2560))
+        z12 = heavy_product((1,), 2, 3, "bank_d", nc.scalar.copy, 4096)
+        scatter(1, 2, 3, z12[:, 0, :])
 
-        for b, bank in ((2, "bank_d"), (3, "bank_e")):
+        z = heavy_product(EARLY_BLOCKS, 3, CHUNKS, "bank_a", nc.scalar.copy, 5120)
+        scatter(0, 3, CHUNKS, z[:, 0, :])
+        store(0)
+        quantize_light(3, 4, cast_light(raw3[:], P, "h3"))
+        scatter(1, 3, CHUNKS, z[:, 1, :])
+        store(1)
+
+        for b, bank in ((2, "bank_b"), (3, "bank_f")):
             for half in range(T // BANK):
-                light_product(b, half, nc.scalar.copy)
-            scatter(b, 0, CHUNKS, heavy_product((b,), 0, CHUNKS, bank)[:, 0, :])
+                light_product(b, half, "light%d" % half, nc.scalar.copy)
+            scatter(b, 0, CHUNKS, heavy_product((b,), 0, CHUNKS, bank, nc.scalar.copy)[:, 0, :])
             store(b)

@@ -25,6 +25,18 @@ BLOCKS = N // P
 LIST_COLS = CHUNK // 16
 RUN = 4
 EARLY_BLOCKS = (0, 1)
+VECTOR_SHARE = 256
+
+KIB = 1024
+AT_H1 = 0
+AT_RELU2 = 0
+AT_Z11 = 0
+AT_RELU3 = KIB
+AT_Z02 = 2 * KIB
+AT_ROUNDED2 = 2 * KIB + KIB // 2
+AT_RAW2 = 4 * KIB
+AT_Z12 = 4 * KIB
+AT_Z3 = 5 * KIB
 
 
 def load_scale_rows(nc, plane, rows):
@@ -48,9 +60,12 @@ def tile_moe_cas_mlp_relu2_kernel(tc, x_words, x_scales, w, w1_words, w1_scales,
         w1_plane = keep.tile([P, H], U8, name="w1_plane", align_bytes=64)
         w2_codes = keep.tile([P, 2 * N], U8, name="w2_codes", align_bytes=64)
         w2_plane = keep.tile([P, N], U8, name="w2_plane", align_bytes=64)
-        early_raw = [keep.tile([P, PACK, P], F32, name="early_raw", tag="raw%d" % b, align_bytes=64) for b in EARLY_BLOCKS]
-        raw2 = laid.tile([P, PACK, P], F32, name="raw2", align_bytes=64, offset=4096)
-        raw3 = keep.tile([P, PACK, P], F32, name="raw3", align_bytes=64)
+        light_raw = [
+            keep.tile([P, PACK, P], F32, name="raw0", align_bytes=64),
+            keep.tile([P, PACK, P], F32, name="raw1", align_bytes=64),
+            laid.tile([P, PACK, P], F32, name="raw2", align_bytes=64, offset=AT_RAW2),
+            keep.tile([P, PACK, P], F32, name="raw3", align_bytes=64),
+        ]
         light_codes = keep.tile([P, N], U32, name="light_codes", align_bytes=64)
         light_plane = keep.tile([P, N], U8, name="light_plane", align_bytes=64)
         windows = {}
@@ -65,7 +80,7 @@ def tile_moe_cas_mlp_relu2_kernel(tc, x_words, x_scales, w, w1_words, w1_scales,
         w_rows = w.rearrange("(p j) n -> p j n", j=PACK)
 
         def load_light(b):
-            nc.sync.dma_start(out=early_raw[b][:], in_=w_rows[:, :, b * P : (b + 1) * P])
+            nc.sync.dma_start(out=light_raw[b][:], in_=w_rows[:, :, b * P : (b + 1) * P])
 
         def load_words(tile, words):
             nc.sync.dma_start(out=tile[:].bitcast(I32), in_=words.bitcast(I32))
@@ -75,12 +90,12 @@ def tile_moe_cas_mlp_relu2_kernel(tc, x_words, x_scales, w, w1_words, w1_scales,
         load_scale_rows(nc, w1_raw_plane, w1_scales[0])
         load_words(x_codes, x_words[0].rearrange("p t d -> p (t d)"))
         load_scale_rows(nc, x_plane, x_scales[0])
-        load_light(0)
-        load_light(1)
+        for b in EARLY_BLOCKS:
+            load_light(b)
         load_words(w2_codes, w2_words[0])
         load_scale_rows(nc, w2_plane, w2_scales[0])
-        nc.sync.dma_start(out=raw2[:], in_=w_rows[:, :, 2 * P : 3 * P])
-        nc.sync.dma_start(out=raw3[:], in_=w_rows[:, :, 3 * P :])
+        for b in range(len(EARLY_BLOCKS), BLOCKS):
+            load_light(b)
 
         def permute_w1():
             nc.vector.tensor_copy(
@@ -103,26 +118,23 @@ def tile_moe_cas_mlp_relu2_kernel(tc, x_words, x_scales, w, w1_words, w1_scales,
         def gather_scales(first, last):
             nc.vector.tensor_copy(slot_plane[:, first * CHUNK : last * CHUNK], x_plane[:].indirect(entries(first, last)))
 
-        def cast_light(raw, width, tag, pool=keep, offset=None):
-            grouped = pool.tile([P, width, PACK], BF16, name="grouped", tag=tag, align_bytes=64, offset=offset)
+        def quantize_light(b, pool, **place):
+            rounded = pool.tile([P, P, PACK], BF16, name="rounded%d" % b, align_bytes=64, **place)
             nc.scalar.copy(
-                out=grouped[:].rearrange("p (c i) j -> p c j i", i=RUN),
-                in_=raw.rearrange("p j (c i) -> p c j i", i=RUN),
+                out=rounded[:].rearrange("p (c i) j -> p c j i", i=RUN),
+                in_=light_raw[b][:].rearrange("p j (c i) -> p c j i", i=RUN),
             )
-            return grouped
-
-        def quantize_light(first, last, grouped):
-            cols = slice(first * P, last * P)
+            cols = slice(b * P, (b + 1) * P)
             nc.vector.quantize_mx(
                 out=light_codes[:, cols].bitcast(FP8X4),
                 scales=light_plane[:, cols],
-                in_=grouped[:].rearrange("p n j -> p (n j)"),
+                in_=rounded[:].rearrange("p n j -> p (n j)"),
             )
 
         def open_window(b, tag):
             windows[b] = keep.tile([P, T], F32, name="window", tag=tag, align_bytes=64)
 
-        def light_product(b, half, bank, *copies):
+        def light_product(b, half, bank):
             cols = slice(b * P, (b + 1) * P)
             tokens = slice(half * BANK, (half + 1) * BANK)
             acc = psum.tile([P, BANK], F32, name="light_acc", tag=bank)
@@ -135,15 +147,11 @@ def tile_moe_cas_mlp_relu2_kernel(tc, x_words, x_scales, w, w1_words, w1_scales,
                 start=True,
                 stop=True,
             )
-            width = BANK // len(copies)
-            for first, copy_out in zip(range(0, BANK, width), copies):
-                copy_out(out=windows[b][:, half * BANK + first : half * BANK + first + width], in_=acc[:, first : first + width])
+            return acc[:], windows[b][:, tokens]
 
-        def square_on_vector(h, relu):
-            nc.vector.tensor_tensor(h, relu, relu, ALU.mult)
-
-        def square_on_scalar(h, relu):
-            nc.scalar.activation(out=h, in_=relu, func=ACT.Square)
+        def light_on_scalar(b, half, bank):
+            sums, columns = light_product(b, half, bank)
+            nc.scalar.copy(out=columns, in_=sums)
 
         def first_product(c, words, bank, relu):
             slots = slice(c * CHUNK, (c + 1) * CHUNK)
@@ -159,29 +167,35 @@ def tile_moe_cas_mlp_relu2_kernel(tc, x_words, x_scales, w, w1_words, w1_scales,
                     stop=True,
                 )
             sums = acc[:].rearrange("p t s -> p s t")
-            nc.scalar.activation(out=relu, in_=sums, func=ACT.Relu)
-            return relu, sums
+            nc.scalar.activation(out=relu[:], in_=sums, func=ACT.Relu)
+            return sums
 
-        def relu_tile(chunks, tag):
-            relu = keep.tile([P, chunks, CHUNK, PACK], F32, name="relu", tag=tag, align_bytes=64)
-            return [relu[:, c] for c in range(chunks)]
+        def relu_tile(c, pool, **place):
+            return pool.tile([P, CHUNK, PACK], F32, name="relu%d" % c, align_bytes=64, **place)
 
-        def squared(relu, square, h_tag):
-            h = keep.tile([P, CHUNK * PACK], BF16, name="h", tag=h_tag, align_bytes=64)
-            square(h[:], relu.rearrange("p s t -> p (s t)"))
+        def h_tile(c, pool, **place):
+            return pool.tile([P, CHUNK, PACK], BF16, name="h%d" % c, align_bytes=64, **place)
+
+        def square_on_scalar(c, relu):
+            h = h_tile(c, keep)
+            nc.scalar.activation(out=h[:], in_=relu[:], func=ACT.Square)
             return h
 
         def quantize_hidden(c, h):
             slots = slice(c * CHUNK, (c + 1) * CHUNK)
-            nc.vector.quantize_mx(out=h_codes[:, slots].bitcast(FP8X4), scales=h_plane[:, slots], in_=h[:])
+            nc.vector.quantize_mx(
+                out=h_codes[:, slots].bitcast(FP8X4),
+                scales=h_plane[:, slots],
+                in_=h[:].rearrange("p s t -> p (s t)"),
+            )
 
-        def heavy_product(blocks, first, last, bank, copy_out, offset=None):
+        def heavy_product(blocks, first, last, bank, pool, **place):
             slots = slice(first * CHUNK, last * CHUNK)
             shape = [P, len(blocks), slots.stop - slots.start]
             acc = psum.tile(shape, F32, name="z_acc", tag=bank)
-            for place, b in enumerate(blocks):
+            for column, b in enumerate(blocks):
                 nc.tensor.matmul_mx(
-                    out=acc[:, place, :],
+                    out=acc[:, column, :],
                     lhsT=w2_codes[:, 2 * b * P : 2 * (b + 1) * P].bitcast(FP4X4),
                     lhsT_scale=w2_plane[:, b * P : (b + 1) * P],
                     rhs=h_codes[:, slots].bitcast(FP8X4),
@@ -189,12 +203,8 @@ def tile_moe_cas_mlp_relu2_kernel(tc, x_words, x_scales, w, w1_words, w1_scales,
                     start=True,
                     stop=True,
                 )
-            name = "z%d_%d" % (blocks[0], first)
-            if offset is None:
-                z = keep.tile(shape, F32, name=name, align_bytes=64)
-            else:
-                z = laid.tile(shape, F32, name=name, align_bytes=64, offset=offset)
-            copy_out(out=z[:], in_=acc[:])
+            z = pool.tile(shape, F32, name="z%d_%d" % (blocks[0], first), align_bytes=64, **place)
+            nc.scalar.copy(out=z[:], in_=acc[:])
             return z
 
         def scatter(b, first, last, z):
@@ -208,59 +218,61 @@ def tile_moe_cas_mlp_relu2_kernel(tc, x_words, x_scales, w, w1_words, w1_scales,
         gather_scales(0, 1)
         gather_scales(1, 2)
         for b in EARLY_BLOCKS:
-            quantize_light(b, b + 1, cast_light(early_raw[b][:], P, "grouped%d" % b))
+            quantize_light(b, keep)
         gather_scales(2, CHUNKS)
-        words = words + gather_words(2, CHUNKS, "grouped0")
+        words = words + gather_words(2, CHUNKS, "rounded0")
         for b in (0, 2, 3):
             open_window(b, "window%d" % b)
 
-        relu0, sums0 = first_product(0, words[0], "bank_a", relu_tile(1, "relu0")[0])
-        relu1, sums1 = first_product(1, words[1], "bank_b", relu_tile(1, "relu1")[0])
-        h0 = squared(relu0, square_on_vector, "h0")
-        h1 = laid.tile([P, CHUNK, PACK], BF16, name="h1", align_bytes=64, offset=0)
-        low, high = slice(0, CHUNK // 2), slice(CHUNK // 2, CHUNK)
-        nc.vector.tensor_tensor(h1[:, low, :], sums1[:, low, :], relu1[:, low, :], ALU.mult)
+        relu0, relu1 = relu_tile(0, keep), relu_tile(1, keep)
+        first_product(0, words[0], "bank_a", relu0)
+        sums1 = first_product(1, words[1], "bank_b", relu1)
+        h0, h1 = h_tile(0, keep), h_tile(1, laid, offset=AT_H1)
+
+        def square_chunk1(slots):
+            nc.vector.scalar_tensor_tensor(h1[:, slots, :], sums1[:, slots, :], 0.0, relu1[:, slots, :], ALU.max, ALU.mult)
+
+        nc.vector.tensor_tensor(h0[:], relu0[:], relu0[:], ALU.mult)
+        square_chunk1(slice(0, CHUNK // 2))
         quantize_hidden(0, h0)
         open_window(1, "h0")
-        nc.vector.tensor_tensor(h1[:, high, :], sums1[:, high, :], relu1[:, high, :], ALU.mult)
-        light_product(0, 0, "light0", nc.scalar.copy)
-        light_product(0, 1, "light1", nc.scalar.copy)
-        light_product(1, 0, "bank_d", nc.vector.tensor_copy)
-        quantize_hidden(1, h1[:].rearrange("p s t -> p (s t)"))
-        z00 = heavy_product((0,), 0, 1, "bank_c", nc.scalar.copy)
-        light_product(1, 1, "bank_a", nc.vector.tensor_copy, nc.scalar.copy)
+        square_chunk1(slice(CHUNK // 2, CHUNK))
+        light_on_scalar(0, 0, "bank_g")
+        light_on_scalar(0, 1, "bank_h")
+        sums, columns = light_product(1, 0, "bank_d")
+        nc.vector.tensor_copy(out=columns, in_=sums)
+        quantize_hidden(1, h1)
+        z00 = heavy_product((0,), 0, 1, "bank_c", keep)
+        sums, columns = light_product(1, 1, "bank_a")
+        nc.vector.tensor_copy(out=columns[:, :VECTOR_SHARE], in_=sums[:, :VECTOR_SHARE])
+        nc.scalar.copy(out=columns[:, VECTOR_SHARE:], in_=sums[:, VECTOR_SHARE:])
         scatter(0, 0, 1, z00[:, 0, :])
-        z10 = heavy_product((1,), 0, 1, "bank_f", nc.scalar.copy)
-        scatter(1, 0, 1, z10[:, 0, :])
+        scatter(1, 0, 1, heavy_product((1,), 0, 1, "bank_f", keep)[:, 0, :])
 
-        relu2 = laid.tile([P, CHUNK, PACK], F32, name="relu2", align_bytes=64, offset=0)
-        first_product(2, words[2], "bank_b", relu2[:])
-        z01 = heavy_product((0,), 1, 2, "bank_e", nc.scalar.copy)
-        h2 = squared(relu2[:], square_on_scalar, "h2")
+        relu2 = relu_tile(2, laid, offset=AT_RELU2)
+        first_product(2, words[2], "bank_b", relu2)
+        z01 = heavy_product((0,), 1, 2, "bank_e", keep)
+        h2 = square_on_scalar(2, relu2)
         scatter(0, 1, 2, z01[:, 0, :])
         quantize_hidden(2, h2)
-        z11 = heavy_product((1,), 1, 2, "light1", nc.scalar.copy, 0)
-        scatter(1, 1, 2, z11[:, 0, :])
+        scatter(1, 1, 2, heavy_product((1,), 1, 2, "bank_h", laid, offset=AT_Z11)[:, 0, :])
 
-        relu3 = laid.tile([P, CHUNK, PACK], F32, name="relu3", align_bytes=64, offset=1024)
-        first_product(3, words[3], "bank_c", relu3[:])
-        h3 = squared(relu3[:], square_on_scalar, "h3")
-        quantize_hidden(3, h3)
-        z02 = heavy_product((0,), 2, 3, "bank_e", nc.scalar.copy, 2048)
-        scatter(0, 2, 3, z02[:, 0, :])
-        quantize_light(2, 3, cast_light(raw2[:], P, "grouped2", laid, 2560))
-        z12 = heavy_product((1,), 2, 3, "bank_d", nc.scalar.copy, 4096)
-        scatter(1, 2, 3, z12[:, 0, :])
+        relu3 = relu_tile(3, laid, offset=AT_RELU3)
+        first_product(3, words[3], "bank_c", relu3)
+        quantize_hidden(3, square_on_scalar(3, relu3))
+        scatter(0, 2, 3, heavy_product((0,), 2, 3, "bank_e", laid, offset=AT_Z02)[:, 0, :])
+        quantize_light(2, laid, offset=AT_ROUNDED2)
+        scatter(1, 2, 3, heavy_product((1,), 2, 3, "bank_d", laid, offset=AT_Z12)[:, 0, :])
 
-        z = heavy_product(EARLY_BLOCKS, 3, CHUNKS, "bank_a", nc.scalar.copy, 5120)
-        scatter(0, 3, CHUNKS, z[:, 0, :])
+        z3 = heavy_product(EARLY_BLOCKS, 3, CHUNKS, "bank_a", laid, offset=AT_Z3)
+        scatter(0, 3, CHUNKS, z3[:, 0, :])
         store(0)
-        quantize_light(3, 4, cast_light(raw3[:], P, "h3"))
-        scatter(1, 3, CHUNKS, z[:, 1, :])
+        quantize_light(3, keep, tag="h3")
+        scatter(1, 3, CHUNKS, z3[:, 1, :])
         store(1)
 
         for b, bank in ((2, "bank_b"), (3, "bank_f")):
-            for half in range(T // BANK):
-                light_product(b, half, "light%d" % half, nc.scalar.copy)
-            scatter(b, 0, CHUNKS, heavy_product((b,), 0, CHUNKS, bank, nc.scalar.copy)[:, 0, :])
+            light_on_scalar(b, 0, "bank_g")
+            light_on_scalar(b, 1, "bank_h")
+            scatter(b, 0, CHUNKS, heavy_product((b,), 0, CHUNKS, bank, keep)[:, 0, :])
             store(b)

@@ -25,7 +25,7 @@ BLOCKS = N // P
 LIST_COLS = CHUNK // 16
 RUN = 4
 EARLY_BLOCKS = (0, 1)
-VECTOR_SHARE = 256
+VECTOR_SHARE = 384
 
 KIB = 1024
 AT_H1 = 0

@@ -39,9 +39,9 @@ AT_Z12 = 4 * KIB
 AT_Z3 = 5 * KIB
 
 
-def load_scale_rows(nc, plane, rows):
-    for q in range(4):
-        nc.sync.dma_start(out=plane[32 * q : 32 * q + 4, :].bitcast(I32), in_=rows[4 * q : 4 * q + 4, :].bitcast(I32))
+def load_scale_rows(queue, plane, rows, quadrants):
+    for q in quadrants:
+        queue.dma_start(out=plane[32 * q : 32 * q + 4, :].bitcast(I32), in_=rows[4 * q : 4 * q + 4, :].bitcast(I32))
 
 
 def tile_moe_cas_mlp_relu2_kernel(tc, x_words, x_scales, w, w1_words, w1_scales, w2_words, w2_scales, offs, out):
@@ -69,12 +69,12 @@ def tile_moe_cas_mlp_relu2_kernel(tc, x_words, x_scales, w, w1_words, w1_scales,
         light_codes = keep.tile([P, N], U32, name="light_codes", align_bytes=64)
         light_plane = keep.tile([P, N], U8, name="light_plane", align_bytes=64)
         windows = {}
-        slot_plane = keep.tile([P, S], U8, name="slot_plane", align_bytes=64)
+        slot_planes = {}
         h_codes = keep.tile([P, S], U32, name="h_codes", align_bytes=64)
         h_plane = keep.tile([P, S], U8, name="h_plane", align_bytes=64)
 
-        nc.vector.memset(w1_raw_plane[:].bitcast(I32), 0)
         nc.vector.memset(x_plane[:].bitcast(I32), 0)
+        nc.vector.memset(w1_raw_plane[:].bitcast(I32), 0)
         nc.vector.memset(w2_plane[:].bitcast(I32), 0)
 
         w_rows = w.rearrange("(p j) n -> p j n", j=PACK)
@@ -82,29 +82,35 @@ def tile_moe_cas_mlp_relu2_kernel(tc, x_words, x_scales, w, w1_words, w1_scales,
         def load_light(b):
             nc.sync.dma_start(out=light_raw[b][:], in_=w_rows[:, :, b * P : (b + 1) * P])
 
-        def load_words(tile, words):
-            nc.sync.dma_start(out=tile[:].bitcast(I32), in_=words.bitcast(I32))
+        def load_words(queue, tile, words):
+            queue.dma_start(out=tile[:].bitcast(I32), in_=words.bitcast(I32))
 
         nc.sync.dma_start(offsets[:], offs)
-        load_words(w1_raw, w1_words[0])
-        load_scale_rows(nc, w1_raw_plane, w1_scales[0])
-        load_words(x_codes, x_words[0].rearrange("p t d -> p (t d)"))
-        load_scale_rows(nc, x_plane, x_scales[0])
+        load_words(nc.scalar, w1_raw, w1_words[0])
+        load_scale_rows(nc.sync, x_plane, x_scales[0], (0,))
+        load_scale_rows(nc.scalar, x_plane, x_scales[0], (1,))
+        load_scale_rows(nc.sync, x_plane, x_scales[0], (2,))
+        load_scale_rows(nc.scalar, x_plane, x_scales[0], (3,))
+        load_scale_rows(nc.sync, w1_raw_plane, w1_scales[0], (0,))
+        load_words(nc.scalar, x_codes, x_words[0].rearrange("p t d -> p (t d)"))
+        load_scale_rows(nc.sync, w1_raw_plane, w1_scales[0], (1, 2, 3))
         for b in EARLY_BLOCKS:
             load_light(b)
-        load_words(w2_codes, w2_words[0])
-        load_scale_rows(nc, w2_plane, w2_scales[0])
+        load_words(nc.sync, w2_codes, w2_words[0])
+        load_scale_rows(nc.sync, w2_plane, w2_scales[0], range(4))
         for b in range(len(EARLY_BLOCKS), BLOCKS):
             load_light(b)
 
-        def permute_w1():
+        def permute_w1_words():
             nc.vector.tensor_copy(
                 out=w1_codes[:].bitcast(U16).rearrange("p (t m) -> p t m", t=PACK),
                 in_=w1_raw[:].bitcast(U16).rearrange("p (m t) -> p t m", t=PACK),
             )
+
+        def permute_w1_scales(ts):
             nc.vector.tensor_copy(
-                out=w1_plane[:].rearrange("p (t m) -> p t m", t=PACK),
-                in_=w1_raw_plane[:].rearrange("p (m t) -> p t m", t=PACK),
+                out=w1_plane[:].rearrange("p (t m) -> p t m", t=PACK)[:, ts, :],
+                in_=w1_raw_plane[:].rearrange("p (m t) -> p t m", t=PACK)[:, ts, :],
             )
 
         def entries(first, last):
@@ -115,8 +121,11 @@ def tile_moe_cas_mlp_relu2_kernel(tc, x_words, x_scales, w, w1_words, w1_scales,
             nc.vector.tensor_copy(words[:], x_codes[:].indirect(entries(first, last)))
             return [words[:, c * CHUNK : (c + 1) * CHUNK] for c in range(last - first)]
 
-        def gather_scales(first, last):
-            nc.vector.tensor_copy(slot_plane[:, first * CHUNK : last * CHUNK], x_plane[:].indirect(entries(first, last)))
+        def gather_scales(first, last, tag):
+            scales = keep.tile([P, (last - first) * CHUNK], U8, name="slot_scales", tag=tag, align_bytes=64)
+            nc.vector.tensor_copy(scales[:], x_plane[:].indirect(entries(first, last)))
+            for c in range(first, last):
+                slot_planes[c] = scales[:, (c - first) * CHUNK : (c - first + 1) * CHUNK]
 
         def quantize_light(b, pool, **place):
             rounded = pool.tile([P, P, PACK], BF16, name="rounded%d" % b, align_bytes=64, **place)
@@ -154,7 +163,6 @@ def tile_moe_cas_mlp_relu2_kernel(tc, x_words, x_scales, w, w1_words, w1_scales,
             nc.scalar.copy(out=columns, in_=sums)
 
         def first_product(c, words, bank, relu):
-            slots = slice(c * CHUNK, (c + 1) * CHUNK)
             acc = psum.tile([P, PACK, CHUNK], F32, name="h_acc", tag=bank)
             for t in range(PACK):
                 nc.tensor.matmul_mx(
@@ -162,7 +170,7 @@ def tile_moe_cas_mlp_relu2_kernel(tc, x_words, x_scales, w, w1_words, w1_scales,
                     lhsT=w1_codes[:, 2 * t * P : 2 * (t + 1) * P].bitcast(FP4X4),
                     lhsT_scale=w1_plane[:, t * P : (t + 1) * P],
                     rhs=words.bitcast(FP8X4),
-                    rhs_scale=slot_plane[:, slots],
+                    rhs_scale=slot_planes[c],
                     start=True,
                     stop=True,
                 )
@@ -213,13 +221,14 @@ def tile_moe_cas_mlp_relu2_kernel(tc, x_words, x_scales, w, w1_words, w1_scales,
         def store(b):
             nc.sync.dma_start(out=out[b * P : (b + 1) * P, :], in_=windows[b][:])
 
-        permute_w1()
+        permute_w1_words()
+        gather_scales(0, 2, "scales01")
         words = gather_words(0, 2, "words01")
-        gather_scales(0, 1)
-        gather_scales(1, 2)
+        permute_w1_scales(slice(0, 2))
+        permute_w1_scales(slice(2, PACK))
+        gather_scales(2, CHUNKS, "w1_raw_plane")
         for b in EARLY_BLOCKS:
             quantize_light(b, keep)
-        gather_scales(2, CHUNKS)
         words = words + gather_words(2, CHUNKS, "rounded0")
         for b in (0, 2, 3):
             open_window(b, "window%d" % b)

@@ -19,6 +19,7 @@ ALU = mybir.AluOpType
 P = 128
 PACK = 4
 BANK = 512
+WARM_ROWS = 32
 CHUNK = 128
 CHUNKS = S // CHUNK
 BLOCKS = N // P
@@ -28,15 +29,21 @@ EARLY_BLOCKS = (0, 1)
 VECTOR_SHARE = 384
 
 KIB = 1024
+AT_RAW0 = 10 * KIB
+AT_RELU0 = 9 * KIB
+AT_RELU1 = 11 * KIB
 AT_H1 = 0
 AT_RELU2 = 0
+AT_Z01 = KIB // 2
 AT_Z11 = 0
-AT_RELU3 = KIB
-AT_Z02 = 2 * KIB
-AT_ROUNDED2 = 2 * KIB + KIB // 2
+AT_RELU3 = 13 * KIB
+AT_Z02 = 14 * KIB
+AT_ROUNDED2 = 14 * KIB + KIB // 2
 AT_RAW2 = 4 * KIB
-AT_Z12 = 4 * KIB
-AT_Z3 = 5 * KIB
+AT_ROUNDED3 = 3 * KIB + 64
+AT_Z2 = 5824
+AT_Z12 = 5248
+AT_Z3 = 4224
 
 
 def load_scale_rows(queue, plane, rows, quadrants):
@@ -61,12 +68,12 @@ def tile_moe_cas_mlp_relu2_kernel(tc, x_words, x_scales, w, w1_words, w1_scales,
         w2_codes = keep.tile([P, 2 * N], U8, name="w2_codes", align_bytes=64)
         w2_plane = keep.tile([P, N], U8, name="w2_plane", align_bytes=64)
         light_raw = [
-            keep.tile([P, PACK, P], F32, name="raw0", align_bytes=64),
+            laid.tile([P, PACK, P], F32, name="raw0", align_bytes=64, offset=AT_RAW0),
             keep.tile([P, PACK, P], F32, name="raw1", align_bytes=64),
             laid.tile([P, PACK, P], F32, name="raw2", align_bytes=64, offset=AT_RAW2),
             keep.tile([P, PACK, P], F32, name="raw3", align_bytes=64),
         ]
-        light_codes = keep.tile([P, N], U32, name="light_codes", align_bytes=64)
+        light_codes = {}
         light_plane = keep.tile([P, N], U8, name="light_plane", align_bytes=64)
         windows = {}
         slot_planes = {}
@@ -86,13 +93,13 @@ def tile_moe_cas_mlp_relu2_kernel(tc, x_words, x_scales, w, w1_words, w1_scales,
             queue.dma_start(out=tile[:].bitcast(I32), in_=words.bitcast(I32))
 
         nc.sync.dma_start(offsets[:], offs)
-        load_words(nc.scalar, w1_raw, w1_words[0])
+        load_words(nc.sync, w1_raw, w1_words[0])
         load_scale_rows(nc.sync, x_plane, x_scales[0], (0,))
-        load_scale_rows(nc.scalar, x_plane, x_scales[0], (1,))
+        load_scale_rows(nc.sync, x_plane, x_scales[0], (1,))
         load_scale_rows(nc.sync, x_plane, x_scales[0], (2,))
-        load_scale_rows(nc.scalar, x_plane, x_scales[0], (3,))
+        load_scale_rows(nc.sync, x_plane, x_scales[0], (3,))
+        load_words(nc.sync, x_codes, x_words[0].rearrange("p t d -> p (t d)"))
         load_scale_rows(nc.sync, w1_raw_plane, w1_scales[0], (0,))
-        load_words(nc.scalar, x_codes, x_words[0].rearrange("p t d -> p (t d)"))
         load_scale_rows(nc.sync, w1_raw_plane, w1_scales[0], (1, 2, 3))
         for b in EARLY_BLOCKS:
             load_light(b)
@@ -127,16 +134,19 @@ def tile_moe_cas_mlp_relu2_kernel(tc, x_words, x_scales, w, w1_words, w1_scales,
             for c in range(first, last):
                 slot_planes[c] = scales[:, (c - first) * CHUNK : (c - first + 1) * CHUNK]
 
-        def quantize_light(b, pool, **place):
+        def round_light(b, copy, pool, **place):
             rounded = pool.tile([P, P, PACK], BF16, name="rounded%d" % b, align_bytes=64, **place)
-            nc.scalar.copy(
+            copy(
                 out=rounded[:].rearrange("p (c i) j -> p c j i", i=RUN),
                 in_=light_raw[b][:].rearrange("p j (c i) -> p c j i", i=RUN),
             )
-            cols = slice(b * P, (b + 1) * P)
+            return rounded
+
+        def quantize_light(b, rounded, **place):
+            light_codes[b] = keep.tile([P, P], U32, name="codes%d" % b, align_bytes=64, **place)
             nc.vector.quantize_mx(
-                out=light_codes[:, cols].bitcast(FP8X4),
-                scales=light_plane[:, cols],
+                out=light_codes[b][:].bitcast(FP8X4),
+                scales=light_plane[:, b * P : (b + 1) * P],
                 in_=rounded[:].rearrange("p n j -> p (n j)"),
             )
 
@@ -149,7 +159,7 @@ def tile_moe_cas_mlp_relu2_kernel(tc, x_words, x_scales, w, w1_words, w1_scales,
             acc = psum.tile([P, BANK], F32, name="light_acc", tag=bank)
             nc.tensor.matmul_mx(
                 out=acc[:],
-                lhsT=light_codes[:, cols].bitcast(FP8X4),
+                lhsT=light_codes[b][:].bitcast(FP8X4),
                 lhsT_scale=light_plane[:, cols],
                 rhs=x_codes[:, tokens].bitcast(FP8X4),
                 rhs_scale=x_plane[:, tokens],
@@ -162,11 +172,11 @@ def tile_moe_cas_mlp_relu2_kernel(tc, x_words, x_scales, w, w1_words, w1_scales,
             sums, columns = light_product(b, half, bank)
             nc.scalar.copy(out=columns, in_=sums)
 
-        def first_product(c, words, bank, relu):
-            acc = psum.tile([P, PACK, CHUNK], F32, name="h_acc", tag=bank)
-            for t in range(PACK):
+        def first_product(c, words, bank, relu, ts=range(PACK)):
+            acc = psum.tile([P, len(ts), CHUNK], F32, name="h_acc", tag=bank)
+            for column, t in enumerate(ts):
                 nc.tensor.matmul_mx(
-                    out=acc[:, t, :],
+                    out=acc[:, column, :],
                     lhsT=w1_codes[:, 2 * t * P : 2 * (t + 1) * P].bitcast(FP4X4),
                     lhsT_scale=w1_plane[:, t * P : (t + 1) * P],
                     rhs=words.bitcast(FP8X4),
@@ -175,7 +185,7 @@ def tile_moe_cas_mlp_relu2_kernel(tc, x_words, x_scales, w, w1_words, w1_scales,
                     stop=True,
                 )
             sums = acc[:].rearrange("p t s -> p s t")
-            nc.scalar.activation(out=relu[:], in_=sums, func=ACT.Relu)
+            nc.scalar.activation(out=relu, in_=sums, func=ACT.Relu)
             return sums
 
         def relu_tile(c, pool, **place):
@@ -222,66 +232,90 @@ def tile_moe_cas_mlp_relu2_kernel(tc, x_words, x_scales, w, w1_words, w1_scales,
             nc.sync.dma_start(out=out[b * P : (b + 1) * P, :], in_=windows[b][:])
 
         permute_w1_words()
-        gather_scales(0, 2, "scales01")
+
+        for bank in ("bank_g", "bank_h", "bank_f")[:2]:
+            idle = psum.tile([WARM_ROWS, BANK], F32, name="warm_up", tag=bank)
+            nc.tensor.matmul_mx(
+                out=idle[:],
+                lhsT=x_codes[:, :WARM_ROWS].bitcast(FP8X4),
+                lhsT_scale=x_plane[:, :WARM_ROWS],
+                rhs=x_codes[:, :BANK].bitcast(FP8X4),
+                rhs_scale=x_plane[:, :BANK],
+                start=True,
+                stop=True,
+            )
+        gather_scales(0, CHUNKS, "scales")
         words = gather_words(0, 2, "words01")
         permute_w1_scales(slice(0, 2))
         permute_w1_scales(slice(2, PACK))
-        gather_scales(2, CHUNKS, "w1_raw_plane")
-        for b in EARLY_BLOCKS:
-            quantize_light(b, keep)
-        words = words + gather_words(2, CHUNKS, "rounded0")
+        words = words + gather_words(2, CHUNKS, "w1_raw_plane")
+        rounded0 = round_light(0, nc.scalar.copy, keep)
+        rounded1 = round_light(1, nc.vector.tensor_copy, keep)
+        quantize_light(0, rounded0)
+        quantize_light(1, rounded1, tag="rounded0")
         for b in (0, 2, 3):
             open_window(b, "window%d" % b)
 
-        relu0, relu1 = relu_tile(0, keep), relu_tile(1, keep)
-        first_product(0, words[0], "bank_a", relu0)
-        sums1 = first_product(1, words[1], "bank_b", relu1)
+        relu0 = laid.tile([P, 2, CHUNK, 2], F32, name="relu0", offset=AT_RELU0, align_bytes=64)
+        relu1 = laid.tile([P, 2, CHUNK, 2], F32, name="relu1", offset=AT_RELU1, align_bytes=64)
         h0, h1 = h_tile(0, keep), h_tile(1, laid, offset=AT_H1)
 
-        def square_chunk1(slots):
-            nc.vector.scalar_tensor_tensor(h1[:, slots, :], sums1[:, slots, :], 0.0, relu1[:, slots, :], ALU.max, ALU.mult)
+        def square_pairs(h, relu, slots):
+            source = relu[:, :, slots, :].rearrange("p u s e -> p s u e")
+            nc.vector.tensor_tensor(h[:, slots, :].rearrange("p s (u e) -> p s u e", e=2), source, source, ALU.mult)
 
-        nc.vector.tensor_tensor(h0[:], relu0[:], relu0[:], ALU.mult)
-        square_chunk1(slice(0, CHUNK // 2))
+        first_product(0, words[0], "bank_a", relu0[:, 0], (0, 1))
+        first_product(0, words[0], "bank_b", relu0[:, 1], (2, 3))
+        first_product(1, words[1], "bank_c", relu1[:, 0], (0, 1))
+        first_product(1, words[1], "bank_d", relu1[:, 1], (2, 3))
+        square_pairs(h0, relu0, slice(0, CHUNK))
+        square_pairs(h1, relu1, slice(0, CHUNK // 2))
         quantize_hidden(0, h0)
         open_window(1, "h0")
-        square_chunk1(slice(CHUNK // 2, CHUNK))
+        square_pairs(h1, relu1, slice(CHUNK // 2, CHUNK))
         light_on_scalar(0, 0, "bank_g")
         light_on_scalar(0, 1, "bank_h")
-        sums, columns = light_product(1, 0, "bank_d")
-        nc.vector.tensor_copy(out=columns, in_=sums)
+        sums, columns = light_product(1, 0, "bank_e")
+        nc.vector.tensor_copy(out=columns[:, : BANK // 2], in_=sums[:, : BANK // 2])
         quantize_hidden(1, h1)
-        z00 = heavy_product((0,), 0, 1, "bank_c", keep)
-        sums, columns = light_product(1, 1, "bank_a")
-        nc.vector.tensor_copy(out=columns[:, :VECTOR_SHARE], in_=sums[:, :VECTOR_SHARE])
-        nc.scalar.copy(out=columns[:, VECTOR_SHARE:], in_=sums[:, VECTOR_SHARE:])
+        nc.vector.tensor_copy(out=columns[:, BANK // 2 :], in_=sums[:, BANK // 2 :])
+        z00 = heavy_product((0,), 0, 1, "bank_f", keep)
         scatter(0, 0, 1, z00[:, 0, :])
-        scatter(1, 0, 1, heavy_product((1,), 0, 1, "bank_f", keep)[:, 0, :])
-
-        relu2 = relu_tile(2, laid, offset=AT_RELU2)
-        first_product(2, words[2], "bank_b", relu2)
-        z01 = heavy_product((0,), 1, 2, "bank_e", keep)
-        h2 = square_on_scalar(2, relu2)
+        relu2 = relu_tile(2, laid, offset=AT_RELU1 + KIB)
+        first_product(2, words[2], "bank_c", relu2[:])
+        z01 = heavy_product((0,), 1, 2, "bank_b", keep)
         scatter(0, 1, 2, z01[:, 0, :])
+        h2 = square_on_scalar(2, relu2)
         quantize_hidden(2, h2)
-        scatter(1, 1, 2, heavy_product((1,), 1, 2, "bank_h", laid, offset=AT_Z11)[:, 0, :])
-
+        light_on_scalar(1, 1, "bank_c")
+        z10 = heavy_product((1,), 0, 1, "bank_a", laid, offset=AT_RELU1 + KIB)
+        scatter(1, 0, 1, z10[:, 0, :])
+        z11 = heavy_product((1,), 1, 2, "bank_d", laid, offset=AT_RELU1 + KIB + 512)
+        scatter(1, 1, 2, z11[:, 0, :])
         relu3 = relu_tile(3, laid, offset=AT_RELU3)
-        first_product(3, words[3], "bank_c", relu3)
-        quantize_hidden(3, square_on_scalar(3, relu3))
-        scatter(0, 2, 3, heavy_product((0,), 2, 3, "bank_e", laid, offset=AT_Z02)[:, 0, :])
-        quantize_light(2, laid, offset=AT_ROUNDED2)
-        scatter(1, 2, 3, heavy_product((1,), 2, 3, "bank_d", laid, offset=AT_Z12)[:, 0, :])
+        first_product(3, words[3], "bank_f", relu3[:])
+
+        h3 = square_on_scalar(3, relu3)
+        quantize_hidden(3, h3)
+        z02 = heavy_product((0,), 2, 3, "bank_e", laid, offset=AT_Z02)
+        scatter(0, 2, 3, z02[:, 0, :])
+        quantize_light(2, round_light(2, nc.scalar.copy, laid, offset=AT_ROUNDED2))
+        z12 = heavy_product((1,), 2, 3, "bank_d", laid, offset=AT_Z12)
+        scatter(1, 2, 3, z12[:, 0, :])
+        quantize_light(3, round_light(3, nc.scalar.copy, laid, offset=AT_ROUNDED3))
 
         z3 = heavy_product(EARLY_BLOCKS, 3, CHUNKS, "bank_a", laid, offset=AT_Z3)
         scatter(0, 3, CHUNKS, z3[:, 0, :])
         store(0)
-        quantize_light(3, keep, tag="h3")
         scatter(1, 3, CHUNKS, z3[:, 1, :])
         store(1)
 
-        for b, bank in ((2, "bank_b"), (3, "bank_f")):
-            light_on_scalar(b, 0, "bank_g")
-            light_on_scalar(b, 1, "bank_h")
-            scatter(b, 0, CHUNKS, heavy_product((b,), 0, CHUNKS, bank, keep)[:, 0, :])
-            store(b)
+        z2 = heavy_product((2,), 0, CHUNKS, "bank_b", laid, offset=AT_Z2)
+        light_on_scalar(2, 0, "bank_g")
+        light_on_scalar(2, 1, "bank_h")
+        scatter(2, 0, CHUNKS, z2[:, 0, :])
+        store(2)
+        light_on_scalar(3, 0, "bank_h")
+        light_on_scalar(3, 1, "bank_d")
+        scatter(3, 0, CHUNKS, heavy_product((3,), 0, CHUNKS, "bank_g", keep)[:, 0, :])
+        store(3)

@@ -19,7 +19,6 @@ ALU = mybir.AluOpType
 P = 128
 PACK = 4
 BANK = 512
-WARM_ROWS = 32
 CHUNK = 128
 CHUNKS = S // CHUNK
 BLOCKS = N // P
@@ -67,11 +66,12 @@ def tile_moe_cas_mlp_relu2_kernel(tc, x_words, x_scales, w, w1_words, w1_scales,
         w1_plane = keep.tile([P, H], U8, name="w1_plane", align_bytes=64)
         w2_codes = keep.tile([P, 2 * N], U8, name="w2_codes", align_bytes=64)
         w2_plane = keep.tile([P, N], U8, name="w2_plane", align_bytes=64)
+        raw_early = keep.tile([P, PACK, 2 * P], F32, name="raw_early", align_bytes=64)
         light_raw = [
-            laid.tile([P, PACK, P], F32, name="raw0", align_bytes=64, offset=AT_RAW0),
-            keep.tile([P, PACK, P], F32, name="raw1", align_bytes=64),
-            laid.tile([P, PACK, P], F32, name="raw2", align_bytes=64, offset=AT_RAW2),
-            keep.tile([P, PACK, P], F32, name="raw3", align_bytes=64),
+            raw_early[:, :, :P],
+            raw_early[:, :, P:],
+            laid.tile([P, PACK, P], F32, name="raw2", align_bytes=64, offset=AT_RAW2)[:],
+            keep.tile([P, PACK, P], F32, name="raw3", align_bytes=64)[:],
         ]
         light_codes = {}
         light_plane = keep.tile([P, N], U8, name="light_plane", align_bytes=64)
@@ -87,7 +87,7 @@ def tile_moe_cas_mlp_relu2_kernel(tc, x_words, x_scales, w, w1_words, w1_scales,
         w_rows = w.rearrange("(p j) n -> p j n", j=PACK)
 
         def load_light(b):
-            nc.sync.dma_start(out=light_raw[b][:], in_=w_rows[:, :, b * P : (b + 1) * P])
+            nc.sync.dma_start(out=light_raw[b], in_=w_rows[:, :, b * P : (b + 1) * P])
 
         def load_words(queue, tile, words):
             queue.dma_start(out=tile[:].bitcast(I32), in_=words.bitcast(I32))
@@ -101,8 +101,7 @@ def tile_moe_cas_mlp_relu2_kernel(tc, x_words, x_scales, w, w1_words, w1_scales,
         load_words(nc.sync, x_codes, x_words[0].rearrange("p t d -> p (t d)"))
         load_scale_rows(nc.sync, w1_raw_plane, w1_scales[0], (0,))
         load_scale_rows(nc.sync, w1_raw_plane, w1_scales[0], (1, 2, 3))
-        for b in EARLY_BLOCKS:
-            load_light(b)
+        nc.sync.dma_start(out=raw_early[:], in_=w_rows[:, :, : 2 * P])
         load_words(nc.sync, w2_codes, w2_words[0])
         load_scale_rows(nc.sync, w2_plane, w2_scales[0], range(4))
         for b in range(len(EARLY_BLOCKS), BLOCKS):
@@ -138,7 +137,7 @@ def tile_moe_cas_mlp_relu2_kernel(tc, x_words, x_scales, w, w1_words, w1_scales,
             rounded = pool.tile([P, P, PACK], BF16, name="rounded%d" % b, align_bytes=64, **place)
             copy(
                 out=rounded[:].rearrange("p (c i) j -> p c j i", i=RUN),
-                in_=light_raw[b][:].rearrange("p j (c i) -> p c j i", i=RUN),
+                in_=light_raw[b].rearrange("p j (c i) -> p c j i", i=RUN),
             )
             return rounded
 
@@ -233,31 +232,20 @@ def tile_moe_cas_mlp_relu2_kernel(tc, x_words, x_scales, w, w1_words, w1_scales,
 
         permute_w1_words()
 
-        for bank in ("bank_g", "bank_h", "bank_f")[:2]:
-            idle = psum.tile([WARM_ROWS, BANK], F32, name="warm_up", tag=bank)
-            nc.tensor.matmul_mx(
-                out=idle[:],
-                lhsT=x_codes[:, :WARM_ROWS].bitcast(FP8X4),
-                lhsT_scale=x_plane[:, :WARM_ROWS],
-                rhs=x_codes[:, :BANK].bitcast(FP8X4),
-                rhs_scale=x_plane[:, :BANK],
-                start=True,
-                stop=True,
-            )
         gather_scales(0, CHUNKS, "scales")
         words = gather_words(0, 2, "words01")
         permute_w1_scales(slice(0, 2))
         permute_w1_scales(slice(2, PACK))
         words = words + gather_words(2, CHUNKS, "w1_raw_plane")
-        rounded0 = round_light(0, nc.scalar.copy, keep)
+        rounded0 = round_light(0, nc.vector.tensor_copy, keep)
         rounded1 = round_light(1, nc.vector.tensor_copy, keep)
         quantize_light(0, rounded0)
-        quantize_light(1, rounded1, tag="rounded0")
+        quantize_light(1, rounded1)
         for b in (0, 2, 3):
             open_window(b, "window%d" % b)
 
-        relu0 = laid.tile([P, 2, CHUNK, 2], F32, name="relu0", offset=AT_RELU0, align_bytes=64)
-        relu1 = laid.tile([P, 2, CHUNK, 2], F32, name="relu1", offset=AT_RELU1, align_bytes=64)
+        relu0 = keep.tile([P, 2, CHUNK, 2], F32, name="relu0", align_bytes=64)
+        relu1 = keep.tile([P, 2, CHUNK, 2], F32, name="relu1", align_bytes=64)
         h0, h1 = h_tile(0, keep), h_tile(1, laid, offset=AT_H1)
 
         def square_pairs(h, relu, slots):
@@ -268,6 +256,8 @@ def tile_moe_cas_mlp_relu2_kernel(tc, x_words, x_scales, w, w1_words, w1_scales,
         first_product(0, words[0], "bank_b", relu0[:, 1], (2, 3))
         first_product(1, words[1], "bank_c", relu1[:, 0], (0, 1))
         first_product(1, words[1], "bank_d", relu1[:, 1], (2, 3))
+        relu2 = relu_tile(2, keep)
+        first_product(2, words[2], "bank_e", relu2[:])
         square_pairs(h0, relu0, slice(0, CHUNK))
         square_pairs(h1, relu1, slice(0, CHUNK // 2))
         quantize_hidden(0, h0)
@@ -275,32 +265,30 @@ def tile_moe_cas_mlp_relu2_kernel(tc, x_words, x_scales, w, w1_words, w1_scales,
         square_pairs(h1, relu1, slice(CHUNK // 2, CHUNK))
         light_on_scalar(0, 0, "bank_g")
         light_on_scalar(0, 1, "bank_h")
-        sums, columns = light_product(1, 0, "bank_e")
+        sums, columns = light_product(1, 0, "bank_f")
         nc.vector.tensor_copy(out=columns[:, : BANK // 2], in_=sums[:, : BANK // 2])
         quantize_hidden(1, h1)
         nc.vector.tensor_copy(out=columns[:, BANK // 2 :], in_=sums[:, BANK // 2 :])
-        z00 = heavy_product((0,), 0, 1, "bank_f", keep)
+        z00 = heavy_product((0,), 0, 1, "bank_a", keep)
         scatter(0, 0, 1, z00[:, 0, :])
-        relu2 = relu_tile(2, laid, offset=AT_RELU1 + KIB)
-        first_product(2, words[2], "bank_c", relu2[:])
-        z01 = heavy_product((0,), 1, 2, "bank_b", keep)
-        scatter(0, 1, 2, z01[:, 0, :])
+        light_on_scalar(1, 1, "bank_c")
+        z10 = heavy_product((1,), 0, 1, "bank_e", keep)
+        scatter(1, 0, 1, z10[:, 0, :])
         h2 = square_on_scalar(2, relu2)
         quantize_hidden(2, h2)
-        light_on_scalar(1, 1, "bank_c")
-        z10 = heavy_product((1,), 0, 1, "bank_a", laid, offset=AT_RELU1 + KIB)
-        scatter(1, 0, 1, z10[:, 0, :])
-        z11 = heavy_product((1,), 1, 2, "bank_d", laid, offset=AT_RELU1 + KIB + 512)
-        scatter(1, 1, 2, z11[:, 0, :])
+        z01 = heavy_product((0,), 1, 2, "bank_b", keep)
+        scatter(0, 1, 2, z01[:, 0, :])
         relu3 = relu_tile(3, laid, offset=AT_RELU3)
-        first_product(3, words[3], "bank_f", relu3[:])
+        first_product(3, words[3], "bank_g", relu3[:])
+        z11 = heavy_product((1,), 1, 2, "bank_d", keep)
+        scatter(1, 1, 2, z11[:, 0, :])
 
         h3 = square_on_scalar(3, relu3)
         quantize_hidden(3, h3)
-        z02 = heavy_product((0,), 2, 3, "bank_e", laid, offset=AT_Z02)
+        z02 = heavy_product((0,), 2, 3, "bank_f", laid, offset=AT_Z02)
         scatter(0, 2, 3, z02[:, 0, :])
         quantize_light(2, round_light(2, nc.scalar.copy, laid, offset=AT_ROUNDED2))
-        z12 = heavy_product((1,), 2, 3, "bank_d", laid, offset=AT_Z12)
+        z12 = heavy_product((1,), 2, 3, "bank_e", laid, offset=AT_Z12)
         scatter(1, 2, 3, z12[:, 0, :])
         quantize_light(3, round_light(3, nc.scalar.copy, laid, offset=AT_ROUNDED3))
 
@@ -311,11 +299,11 @@ def tile_moe_cas_mlp_relu2_kernel(tc, x_words, x_scales, w, w1_words, w1_scales,
         store(1)
 
         z2 = heavy_product((2,), 0, CHUNKS, "bank_b", laid, offset=AT_Z2)
-        light_on_scalar(2, 0, "bank_g")
+        light_on_scalar(2, 0, "bank_c")
         light_on_scalar(2, 1, "bank_h")
         scatter(2, 0, CHUNKS, z2[:, 0, :])
         store(2)
         light_on_scalar(3, 0, "bank_h")
-        light_on_scalar(3, 1, "bank_d")
-        scatter(3, 0, CHUNKS, heavy_product((3,), 0, CHUNKS, "bank_g", keep)[:, 0, :])
+        light_on_scalar(3, 1, "bank_b")
+        scatter(3, 0, CHUNKS, heavy_product((3,), 0, CHUNKS, "bank_c", keep)[:, 0, :])
         store(3)

@@ -19,6 +19,7 @@ ALU = mybir.AluOpType
 P = 128
 PACK = 4
 BANK = 512
+WARM_ROWS = 32
 CHUNK = 128
 CHUNKS = S // CHUNK
 BLOCKS = N // P
@@ -232,6 +233,17 @@ def tile_moe_cas_mlp_relu2_kernel(tc, x_words, x_scales, w, w1_words, w1_scales,
 
         permute_w1_words()
 
+        for bank in ("bank_g", "bank_h", "bank_f")[:2]:
+            idle = psum.tile([WARM_ROWS, BANK], F32, name="warm_up", tag=bank)
+            nc.tensor.matmul_mx(
+                out=idle[:],
+                lhsT=x_codes[:, :WARM_ROWS].bitcast(FP8X4),
+                lhsT_scale=x_plane[:, :WARM_ROWS],
+                rhs=x_codes[:, :BANK].bitcast(FP8X4),
+                rhs_scale=x_plane[:, :BANK],
+                start=True,
+                stop=True,
+            )
         gather_scales(0, CHUNKS, "scales")
         words = gather_words(0, 2, "words01")
         permute_w1_scales(slice(0, 2))

@@ -61,6 +61,7 @@ def tile_moe_cas_mlp_relu2_kernel(tc, x_words, x_scales, w, w1_words, w1_scales,
         offsets = keep.tile([P, S // 16], U16, name="offsets")
         x_codes = keep.tile([P, T], U32, name="x_codes", align_bytes=64)
         x_plane = keep.tile([P, T], U8, name="x_plane", align_bytes=64)
+        x_first_rows = keep.tile([P, T], U8, name="x_first_rows", align_bytes=64)
         w1_raw = keep.tile([P, 2 * H], U8, name="w1_raw", align_bytes=64)
         w1_raw_plane = keep.tile([P, H], U8, name="w1_raw_plane", align_bytes=64)
         w1_codes = keep.tile([P, 2 * H], U8, name="w1_codes", align_bytes=64)
@@ -94,8 +95,8 @@ def tile_moe_cas_mlp_relu2_kernel(tc, x_words, x_scales, w, w1_words, w1_scales,
             queue.dma_start(out=tile[:].bitcast(I32), in_=words.bitcast(I32))
 
         nc.sync.dma_start(offsets[:], offs)
+        load_scale_rows(nc.sync, x_first_rows, x_scales[0], (0,))
         load_words(nc.sync, w1_raw, w1_words[0])
-        load_scale_rows(nc.sync, x_plane, x_scales[0], (0,))
         load_scale_rows(nc.sync, x_plane, x_scales[0], (1,))
         load_scale_rows(nc.sync, x_plane, x_scales[0], (2,))
         load_scale_rows(nc.sync, x_plane, x_scales[0], (3,))
@@ -231,6 +232,7 @@ def tile_moe_cas_mlp_relu2_kernel(tc, x_words, x_scales, w, w1_words, w1_scales,
         def store(b):
             nc.sync.dma_start(out=out[b * P : (b + 1) * P, :], in_=windows[b][:])
 
+        nc.vector.tensor_copy(x_plane[0:4, :].bitcast(I32), x_first_rows[0:4, :].bitcast(I32))
         permute_w1_words()
 
         for bank in ("bank_g", "bank_h", "bank_f")[:2]:

@@ -94,9 +94,9 @@ def tile_moe_cas_mlp_relu2_kernel(tc, x_words, x_scales, w, w1_words, w1_scales,
         def load_words(queue, tile, words):
             queue.dma_start(out=tile[:].bitcast(I32), in_=words.bitcast(I32))
 
-        nc.sync.dma_start(offsets[:], offs)
         load_scale_rows(nc.sync, x_first_rows, x_scales[0], (0,))
         load_words(nc.sync, w1_raw, w1_words[0])
+        nc.sync.dma_start(offsets[:], offs)
         load_scale_rows(nc.sync, x_plane, x_scales[0], (1,))
         load_scale_rows(nc.sync, x_plane, x_scales[0], (2,))
         load_scale_rows(nc.sync, x_plane, x_scales[0], (3,))

@@ -19,31 +19,11 @@ ALU = mybir.AluOpType
 P = 128
 PACK = 4
 BANK = 512
-WARM_ROWS = 32
 CHUNK = 128
 CHUNKS = S // CHUNK
 BLOCKS = N // P
-LIST_COLS = CHUNK // 16
+PER_COLUMN = 16
 RUN = 4
-EARLY_BLOCKS = (0, 1)
-VECTOR_SHARE = 384
-
-KIB = 1024
-AT_RAW0 = 10 * KIB
-AT_RELU0 = 9 * KIB
-AT_RELU1 = 11 * KIB
-AT_H1 = 0
-AT_RELU2 = 0
-AT_Z01 = KIB // 2
-AT_Z11 = 0
-AT_RELU3 = 13 * KIB
-AT_Z02 = 14 * KIB
-AT_ROUNDED2 = 14 * KIB + KIB // 2
-AT_RAW2 = 4 * KIB
-AT_ROUNDED3 = 3 * KIB + 64
-AT_Z2 = 5824
-AT_Z12 = 5248
-AT_Z3 = 4224
 
 
 def load_scale_rows(queue, plane, rows, quadrants):
@@ -55,32 +35,28 @@ def tile_moe_cas_mlp_relu2_kernel(tc, x_words, x_scales, w, w1_words, w1_scales,
     nc = tc.nc
     with ExitStack() as ctx:
         keep = ctx.enter_context(tc.tile_pool(name="keep", bufs=1))
-        laid = ctx.enter_context(tc.tile_pool(name="laid", bufs=1))
         psum = ctx.enter_context(tc.psum_pool(name="psum", bufs=1))
 
-        offsets = keep.tile([P, S // 16], U16, name="offsets")
-        x_codes = keep.tile([P, T], U32, name="x_codes", align_bytes=64)
-        x_plane = keep.tile([P, T], U8, name="x_plane", align_bytes=64)
-        x_first_rows = keep.tile([P, T], U8, name="x_first_rows", align_bytes=64)
-        w1_raw = keep.tile([P, 2 * H], U8, name="w1_raw", align_bytes=64)
-        w1_raw_plane = keep.tile([P, H], U8, name="w1_raw_plane", align_bytes=64)
-        w1_codes = keep.tile([P, 2 * H], U8, name="w1_codes", align_bytes=64)
-        w1_plane = keep.tile([P, H], U8, name="w1_plane", align_bytes=64)
-        w2_codes = keep.tile([P, 2 * N], U8, name="w2_codes", align_bytes=64)
-        w2_plane = keep.tile([P, N], U8, name="w2_plane", align_bytes=64)
-        raw_early = keep.tile([P, PACK, 2 * P], F32, name="raw_early", align_bytes=64)
-        light_raw = [
-            raw_early[:, :, :P],
-            raw_early[:, :, P:],
-            laid.tile([P, PACK, P], F32, name="raw2", align_bytes=64, offset=AT_RAW2)[:],
-            keep.tile([P, PACK, P], F32, name="raw3", align_bytes=64)[:],
-        ]
-        light_codes = {}
-        light_plane = keep.tile([P, N], U8, name="light_plane", align_bytes=64)
-        windows = {}
-        slot_planes = {}
-        h_codes = keep.tile([P, S], U32, name="h_codes", align_bytes=64)
-        h_plane = keep.tile([P, S], U8, name="h_plane", align_bytes=64)
+        def tile(name, shape, dtype, **place):
+            return keep.tile(shape, dtype, name=name, align_bytes=64, **place)
+
+        offsets = keep.tile([P, S // PER_COLUMN], U16, name="offsets")
+        x_codes = tile("x_codes", [P, T], U32)
+        x_plane = tile("x_plane", [P, T], U8)
+        x_first_rows = tile("x_first_rows", [P, T], U8)
+        w1_raw = tile("w1_raw", [P, 2 * H], U8)
+        w1_raw_plane = tile("w1_raw_plane", [P, H], U8)
+        w1_codes = tile("w1_codes", [P, 2 * H], U8)
+        w1_plane = tile("w1_plane", [P, H], U8)
+        w2_codes = tile("w2_codes", [P, 2 * N], U8)
+        w2_plane = tile("w2_plane", [P, N], U8)
+        light_raw = [tile("raw%d" % u, [P, PACK, 2 * P], F32) for u in range(2)]
+        light_codes = tile("light_codes", [P, N], U32)
+        light_plane = tile("light_plane", [P, N], U8)
+        windows = [tile("window%d" % b, [P, T], F32) for b in range(BLOCKS)]
+        slot_plane = tile("slot_plane", [P, S], U8)
+        h_codes = tile("h_codes", [P, S], U32)
+        h_plane = tile("h_plane", [P, S], U8)
 
         nc.vector.memset(x_plane[:].bitcast(I32), 0)
         nc.vector.memset(w1_raw_plane[:].bitcast(I32), 0)
@@ -88,32 +64,27 @@ def tile_moe_cas_mlp_relu2_kernel(tc, x_words, x_scales, w, w1_words, w1_scales,
 
         w_rows = w.rearrange("(p j) n -> p j n", j=PACK)
 
-        def load_light(b):
-            nc.sync.dma_start(out=light_raw[b], in_=w_rows[:, :, b * P : (b + 1) * P])
-
-        def load_words(queue, tile, words):
-            queue.dma_start(out=tile[:].bitcast(I32), in_=words.bitcast(I32))
+        def load_words(tile_, words):
+            nc.sync.dma_start(out=tile_[:].bitcast(I32), in_=words.bitcast(I32))
 
         load_scale_rows(nc.sync, x_first_rows, x_scales[0], (0,))
-        load_words(nc.sync, w1_raw, w1_words[0])
+        load_words(w1_raw, w1_words[0])
         nc.sync.dma_start(offsets[:], offs)
-        load_scale_rows(nc.sync, x_plane, x_scales[0], (1,))
-        load_scale_rows(nc.sync, x_plane, x_scales[0], (2,))
-        load_scale_rows(nc.sync, x_plane, x_scales[0], (3,))
-        load_words(nc.sync, x_codes, x_words[0].rearrange("p t d -> p (t d)"))
-        load_scale_rows(nc.sync, w1_raw_plane, w1_scales[0], (0,))
-        load_scale_rows(nc.sync, w1_raw_plane, w1_scales[0], (1, 2, 3))
-        nc.sync.dma_start(out=raw_early[:], in_=w_rows[:, :, : 2 * P])
-        load_words(nc.sync, w2_codes, w2_words[0])
+        load_scale_rows(nc.sync, x_plane, x_scales[0], (1, 2, 3))
+        load_words(x_codes, x_words[0].rearrange("p t d -> p (t d)"))
+        load_scale_rows(nc.sync, w1_raw_plane, w1_scales[0], range(4))
+        nc.sync.dma_start(out=light_raw[0][:], in_=w_rows[:, :, : 2 * P])
+        load_words(w2_codes, w2_words[0])
         load_scale_rows(nc.sync, w2_plane, w2_scales[0], range(4))
-        for b in range(len(EARLY_BLOCKS), BLOCKS):
-            load_light(b)
+        nc.sync.dma_start(out=light_raw[1][:], in_=w_rows[:, :, 2 * P :])
 
-        def permute_w1_words():
-            nc.vector.tensor_copy(
-                out=w1_codes[:].bitcast(U16).rearrange("p (t m) -> p t m", t=PACK),
-                in_=w1_raw[:].bitcast(U16).rearrange("p (m t) -> p t m", t=PACK),
-            )
+        def entries(first, last):
+            return offsets[:, first // PER_COLUMN : last // PER_COLUMN]
+
+        def gather_words(u, **place):
+            words = tile("slot_codes%d" % u, [P, 2 * CHUNK], U32, **place)
+            nc.vector.tensor_copy(words[:], x_codes[:].indirect(entries(2 * u * CHUNK, 2 * (u + 1) * CHUNK)))
+            return [words[:, :CHUNK], words[:, CHUNK:]]
 
         def permute_w1_scales(ts):
             nc.vector.tensor_copy(
@@ -121,82 +92,60 @@ def tile_moe_cas_mlp_relu2_kernel(tc, x_words, x_scales, w, w1_words, w1_scales,
                 in_=w1_raw_plane[:].rearrange("p (m t) -> p t m", t=PACK)[:, ts, :],
             )
 
-        def entries(first, last):
-            return offsets[:, first * LIST_COLS : last * LIST_COLS]
-
-        def gather_words(first, last, tag):
-            words = keep.tile([P, (last - first) * CHUNK], U32, name="slot_codes", tag=tag, align_bytes=64)
-            nc.vector.tensor_copy(words[:], x_codes[:].indirect(entries(first, last)))
-            return [words[:, c * CHUNK : (c + 1) * CHUNK] for c in range(last - first)]
-
-        def gather_scales(first, last, tag):
-            scales = keep.tile([P, (last - first) * CHUNK], U8, name="slot_scales", tag=tag, align_bytes=64)
-            nc.vector.tensor_copy(scales[:], x_plane[:].indirect(entries(first, last)))
-            for c in range(first, last):
-                slot_planes[c] = scales[:, (c - first) * CHUNK : (c - first + 1) * CHUNK]
-
-        def round_light(b, copy, pool, **place):
-            rounded = pool.tile([P, P, PACK], BF16, name="rounded%d" % b, align_bytes=64, **place)
-            copy(
+        def round_light(u):
+            rounded = tile("rounded%d" % u, [P, 2 * P, PACK], BF16)
+            nc.vector.tensor_copy(
                 out=rounded[:].rearrange("p (c i) j -> p c j i", i=RUN),
-                in_=light_raw[b].rearrange("p j (c i) -> p c j i", i=RUN),
+                in_=light_raw[u][:].rearrange("p j (c i) -> p c j i", i=RUN),
             )
             return rounded
 
-        def quantize_light(b, rounded, **place):
-            light_codes[b] = keep.tile([P, P], U32, name="codes%d" % b, align_bytes=64, **place)
+        def quantize_light(u, rounded):
+            cols = slice(2 * u * P, 2 * (u + 1) * P)
             nc.vector.quantize_mx(
-                out=light_codes[b][:].bitcast(FP8X4),
-                scales=light_plane[:, b * P : (b + 1) * P],
+                out=light_codes[:, cols].bitcast(FP8X4),
+                scales=light_plane[:, cols],
                 in_=rounded[:].rearrange("p n j -> p (n j)"),
             )
 
-        def open_window(b, tag):
-            windows[b] = keep.tile([P, T], F32, name="window", tag=tag, align_bytes=64)
-
-        def light_product(b, half, bank):
+        def light(b, half, bank, copy):
             cols = slice(b * P, (b + 1) * P)
             tokens = slice(half * BANK, (half + 1) * BANK)
             acc = psum.tile([P, BANK], F32, name="light_acc", tag=bank)
             nc.tensor.matmul_mx(
                 out=acc[:],
-                lhsT=light_codes[b][:].bitcast(FP8X4),
+                lhsT=light_codes[:, cols].bitcast(FP8X4),
                 lhsT_scale=light_plane[:, cols],
                 rhs=x_codes[:, tokens].bitcast(FP8X4),
                 rhs_scale=x_plane[:, tokens],
                 start=True,
                 stop=True,
             )
-            return acc[:], windows[b][:, tokens]
+            copy(out=windows[b][:, tokens], in_=acc[:])
 
-        def light_on_scalar(b, half, bank):
-            sums, columns = light_product(b, half, bank)
-            nc.scalar.copy(out=columns, in_=sums)
-
-        def first_product(c, words, bank, relu, ts=range(PACK)):
-            acc = psum.tile([P, len(ts), CHUNK], F32, name="h_acc", tag=bank)
-            for column, t in enumerate(ts):
+        def first_product(c, words, bank):
+            acc = psum.tile([P, PACK, CHUNK], F32, name="h_acc", tag=bank)
+            for t in range(PACK):
                 nc.tensor.matmul_mx(
-                    out=acc[:, column, :],
+                    out=acc[:, t, :],
                     lhsT=w1_codes[:, 2 * t * P : 2 * (t + 1) * P].bitcast(FP4X4),
                     lhsT_scale=w1_plane[:, t * P : (t + 1) * P],
                     rhs=words.bitcast(FP8X4),
-                    rhs_scale=slot_planes[c],
+                    rhs_scale=slot_plane[:, c * CHUNK : (c + 1) * CHUNK],
                     start=True,
                     stop=True,
                 )
-            sums = acc[:].rearrange("p t s -> p s t")
-            nc.scalar.activation(out=relu, in_=sums, func=ACT.Relu)
-            return sums
+            relu = tile("relu%d" % c, [P, CHUNK, PACK], F32)
+            nc.scalar.activation(out=relu[:], in_=acc[:].rearrange("p t s -> p s t"), func=ACT.Relu)
+            return relu
 
-        def relu_tile(c, pool, **place):
-            return pool.tile([P, CHUNK, PACK], F32, name="relu%d" % c, align_bytes=64, **place)
-
-        def h_tile(c, pool, **place):
-            return pool.tile([P, CHUNK, PACK], BF16, name="h%d" % c, align_bytes=64, **place)
+        def square(c, relu):
+            h = tile("h%d" % c, [P, CHUNK, PACK], BF16)
+            nc.vector.tensor_tensor(h[:], relu[:], relu[:], ALU.mult)
+            return h
 
         def square_on_scalar(c, relu):
-            h = h_tile(c, keep)
+            h = tile("h%d" % c, [P, CHUNK, PACK], BF16)
             nc.scalar.activation(out=h[:], in_=relu[:], func=ACT.Square)
             return h
 
@@ -208,116 +157,75 @@ def tile_moe_cas_mlp_relu2_kernel(tc, x_words, x_scales, w, w1_words, w1_scales,
                 in_=h[:].rearrange("p s t -> p (s t)"),
             )
 
-        def heavy_product(blocks, first, last, bank, pool, **place):
-            slots = slice(first * CHUNK, last * CHUNK)
-            shape = [P, len(blocks), slots.stop - slots.start]
-            acc = psum.tile(shape, F32, name="z_acc", tag=bank)
-            for column, b in enumerate(blocks):
-                nc.tensor.matmul_mx(
-                    out=acc[:, column, :],
-                    lhsT=w2_codes[:, 2 * b * P : 2 * (b + 1) * P].bitcast(FP4X4),
-                    lhsT_scale=w2_plane[:, b * P : (b + 1) * P],
-                    rhs=h_codes[:, slots].bitcast(FP8X4),
-                    rhs_scale=h_plane[:, slots],
-                    start=True,
-                    stop=True,
-                )
-            z = pool.tile(shape, F32, name="z%d_%d" % (blocks[0], first), align_bytes=64, **place)
-            nc.scalar.copy(out=z[:], in_=acc[:])
-            return z
-
-        def scatter(b, first, last, z):
-            nc.vector.tensor_copy(windows[b][:].indirect(entries(first, last)), z)
-
-        def store(b):
-            nc.sync.dma_start(out=out[b * P : (b + 1) * P, :], in_=windows[b][:])
-
-        nc.vector.tensor_copy(x_plane[0:4, :].bitcast(I32), x_first_rows[0:4, :].bitcast(I32))
-        permute_w1_words()
-
-        for bank in ("bank_g", "bank_h", "bank_f")[:2]:
-            idle = psum.tile([WARM_ROWS, BANK], F32, name="warm_up", tag=bank)
+        def heavy(b, first, last, bank, copy):
+            acc = psum.tile([P, last - first], F32, name="z_acc", tag=bank)
             nc.tensor.matmul_mx(
-                out=idle[:],
-                lhsT=x_codes[:, :WARM_ROWS].bitcast(FP8X4),
-                lhsT_scale=x_plane[:, :WARM_ROWS],
-                rhs=x_codes[:, :BANK].bitcast(FP8X4),
-                rhs_scale=x_plane[:, :BANK],
+                out=acc[:],
+                lhsT=w2_codes[:, 2 * b * P : 2 * (b + 1) * P].bitcast(FP4X4),
+                lhsT_scale=w2_plane[:, b * P : (b + 1) * P],
+                rhs=h_codes[:, first:last].bitcast(FP8X4),
+                rhs_scale=h_plane[:, first:last],
                 start=True,
                 stop=True,
             )
-        gather_scales(0, CHUNKS, "scales")
-        words = gather_words(0, 2, "words01")
+            z = tile("z%d_%d" % (b, first), [P, last - first], F32)
+            copy(out=z[:], in_=acc[:])
+            return z
+
+        def scatter_on_vector(b, z, first, last):
+            nc.vector.tensor_copy(windows[b][:].indirect(entries(first, last)), z)
+
+        def scatter_on_scalar(b, z, first, last):
+            nc.scalar.activation(windows[b][:].indirect(entries(first, last)), z, ACT.Copy)
+
+        def store(b, queue):
+            queue.dma_start(out=out[b * P : (b + 1) * P, :], in_=windows[b][:])
+
+        nc.vector.tensor_copy(x_plane[0:4, :].bitcast(I32), x_first_rows[0:4, :].bitcast(I32))
+        nc.vector.tensor_copy(
+            out=w1_codes[:].bitcast(U16).rearrange("p (t m) -> p t m", t=PACK),
+            in_=w1_raw[:].bitcast(U16).rearrange("p (m t) -> p t m", t=PACK),
+        )
+        nc.vector.tensor_copy(slot_plane[:], x_plane[:].indirect(offsets[:]))
+        words = gather_words(0)
         permute_w1_scales(slice(0, 2))
         permute_w1_scales(slice(2, PACK))
-        words = words + gather_words(2, CHUNKS, "w1_raw_plane")
-        rounded0 = round_light(0, nc.vector.tensor_copy, keep)
-        rounded1 = round_light(1, nc.vector.tensor_copy, keep)
-        quantize_light(0, rounded0)
-        quantize_light(1, rounded1)
-        for b in (0, 2, 3):
-            open_window(b, "window%d" % b)
-
-        relu0 = keep.tile([P, 2, CHUNK, 2], F32, name="relu0", align_bytes=64)
-        relu1 = keep.tile([P, 2, CHUNK, 2], F32, name="relu1", align_bytes=64)
-        h0, h1 = h_tile(0, keep), h_tile(1, laid, offset=AT_H1)
-
-        def square_pairs(h, relu, slots):
-            source = relu[:, :, slots, :].rearrange("p u s e -> p s u e")
-            nc.vector.tensor_tensor(h[:, slots, :].rearrange("p s (u e) -> p s u e", e=2), source, source, ALU.mult)
-
-        first_product(0, words[0], "bank_a", relu0[:, 0], (0, 1))
-        first_product(0, words[0], "bank_b", relu0[:, 1], (2, 3))
-        first_product(1, words[1], "bank_c", relu1[:, 0], (0, 1))
-        first_product(1, words[1], "bank_d", relu1[:, 1], (2, 3))
-        relu2 = relu_tile(2, keep)
-        first_product(2, words[2], "bank_e", relu2[:])
-        square_pairs(h0, relu0, slice(0, CHUNK))
-        square_pairs(h1, relu1, slice(0, CHUNK // 2))
+        words = words + gather_words(1, tag="w1_raw_plane")
+        rounded = round_light(0)
+        relus = [first_product(c, words[c], "bank%d" % c) for c in range(CHUNKS)]
+        h0 = square(0, relus[0])
+        quantize_light(0, rounded)
+        h1 = square(1, relus[1])
         quantize_hidden(0, h0)
-        open_window(1, "h0")
-        square_pairs(h1, relu1, slice(CHUNK // 2, CHUNK))
-        light_on_scalar(0, 0, "bank_g")
-        light_on_scalar(0, 1, "bank_h")
-        sums, columns = light_product(1, 0, "bank_f")
-        nc.vector.tensor_copy(out=columns[:, : BANK // 2], in_=sums[:, : BANK // 2])
+        h2 = square(2, relus[2])
         quantize_hidden(1, h1)
-        nc.vector.tensor_copy(out=columns[:, BANK // 2 :], in_=sums[:, BANK // 2 :])
-        z00 = heavy_product((0,), 0, 1, "bank_a", keep)
-        scatter(0, 0, 1, z00[:, 0, :])
-        light_on_scalar(1, 1, "bank_c")
-        z10 = heavy_product((1,), 0, 1, "bank_e", keep)
-        scatter(1, 0, 1, z10[:, 0, :])
-        h2 = square_on_scalar(2, relu2)
+        light(0, 0, "bank4", nc.scalar.copy)
+        h3 = square_on_scalar(3, relus[3])
         quantize_hidden(2, h2)
-        z01 = heavy_product((0,), 1, 2, "bank_b", keep)
-        scatter(0, 1, 2, z01[:, 0, :])
-        relu3 = relu_tile(3, laid, offset=AT_RELU3)
-        first_product(3, words[3], "bank_g", relu3[:])
-        z11 = heavy_product((1,), 1, 2, "bank_d", keep)
-        scatter(1, 1, 2, z11[:, 0, :])
-
-        h3 = square_on_scalar(3, relu3)
+        light(0, 1, "bank5", nc.scalar.copy)
         quantize_hidden(3, h3)
-        z02 = heavy_product((0,), 2, 3, "bank_f", laid, offset=AT_Z02)
-        scatter(0, 2, 3, z02[:, 0, :])
-        quantize_light(2, round_light(2, nc.scalar.copy, laid, offset=AT_ROUNDED2))
-        z12 = heavy_product((1,), 2, 3, "bank_e", laid, offset=AT_Z12)
-        scatter(1, 2, 3, z12[:, 0, :])
-        quantize_light(3, round_light(3, nc.scalar.copy, laid, offset=AT_ROUNDED3))
-
-        z3 = heavy_product(EARLY_BLOCKS, 3, CHUNKS, "bank_a", laid, offset=AT_Z3)
-        scatter(0, 3, CHUNKS, z3[:, 0, :])
-        store(0)
-        scatter(1, 3, CHUNKS, z3[:, 1, :])
-        store(1)
-
-        z2 = heavy_product((2,), 0, CHUNKS, "bank_b", laid, offset=AT_Z2)
-        light_on_scalar(2, 0, "bank_c")
-        light_on_scalar(2, 1, "bank_h")
-        scatter(2, 0, CHUNKS, z2[:, 0, :])
-        store(2)
-        light_on_scalar(3, 0, "bank_h")
-        light_on_scalar(3, 1, "bank_b")
-        scatter(3, 0, CHUNKS, heavy_product((3,), 0, CHUNKS, "bank_c", keep)[:, 0, :])
-        store(3)
+        half = S // 2
+        z0a = heavy(0, 0, half, "bank0", nc.scalar.copy)
+        rounded = round_light(1)
+        light(1, 0, "bank6", nc.scalar.copy)
+        scatter_on_vector(0, z0a[:], 0, half)
+        quantize_light(1, rounded)
+        z0b = heavy(0, half, S, "bank1", nc.scalar.copy)
+        light(1, 1, "bank7", nc.scalar.copy)
+        z1 = heavy(1, 0, S, "bank2", nc.scalar.copy)
+        scatter_on_vector(0, z0b[:], half, S)
+        store(0, nc.sync)
+        scatter_on_scalar(1, z1[:, :half], 0, half)
+        z3 = heavy(3, 0, S, "bank3", nc.scalar.copy)
+        scatter_on_scalar(1, z1[:, half:], half, S)
+        store(1, nc.scalar)
+        z2 = heavy(2, 0, S, "bank0", nc.vector.tensor_copy)
+        light(2, 0, "bank4", nc.vector.tensor_copy)
+        light(2, 1, "bank5", nc.vector.tensor_copy)
+        light(3, 0, "bank6", nc.vector.tensor_copy)
+        light(3, 1, "bank7", nc.scalar.copy)
+        scatter_on_scalar(3, z3[:, :half], 0, half)
+        scatter_on_scalar(3, z3[:, half:], half, S)
+        store(3, nc.scalar)
+        scatter_on_vector(2, z2[:], 0, S)
+        store(2, nc.sync)

@@ -43,14 +43,15 @@ def tile_moe_cas_mlp_relu2_kernel(tc, x_words, x_scales, w, w1_words, w1_scales,
         offsets = keep.tile([P, S // PER_COLUMN], U16, name="offsets")
         x_codes = tile("x_codes", [P, T], U32)
         x_plane = tile("x_plane", [P, T], U8)
-        x_first_rows = tile("x_first_rows", [P, T], U8)
         w1_raw = tile("w1_raw", [P, 2 * H], U8)
         w1_raw_plane = tile("w1_raw_plane", [P, H], U8)
         w1_codes = tile("w1_codes", [P, 2 * H], U8)
         w1_plane = tile("w1_plane", [P, H], U8)
         w2_codes = tile("w2_codes", [P, 2 * N], U8)
         w2_plane = tile("w2_plane", [P, N], U8)
-        light_raw = [tile("raw%d" % u, [P, PACK, 2 * P], F32) for u in range(2)]
+        raw_first = tile("raw_first", [P, PACK, P], F32)
+        raw_second = tile("raw_second", [P, PACK, P], F32)
+        raw_rest = tile("raw_rest", [P, PACK, 2 * P], F32)
         light_codes = tile("light_codes", [P, N], U32)
         light_plane = tile("light_plane", [P, N], U8)
         windows = [tile("window%d" % b, [P, T], F32) for b in range(BLOCKS)]
@@ -67,16 +68,16 @@ def tile_moe_cas_mlp_relu2_kernel(tc, x_words, x_scales, w, w1_words, w1_scales,
         def load_words(tile_, words):
             nc.sync.dma_start(out=tile_[:].bitcast(I32), in_=words.bitcast(I32))
 
-        load_scale_rows(nc.sync, x_first_rows, x_scales[0], (0,))
-        load_words(w1_raw, w1_words[0])
+        nc.sync.dma_start(out=raw_first[:], in_=w_rows[:, :, :P])
         nc.sync.dma_start(offsets[:], offs)
-        load_scale_rows(nc.sync, x_plane, x_scales[0], (1, 2, 3))
+        load_words(w1_raw, w1_words[0])
+        load_scale_rows(nc.sync, x_plane, x_scales[0], range(4))
         load_words(x_codes, x_words[0].rearrange("p t d -> p (t d)"))
         load_scale_rows(nc.sync, w1_raw_plane, w1_scales[0], range(4))
-        nc.sync.dma_start(out=light_raw[0][:], in_=w_rows[:, :, : 2 * P])
+        nc.sync.dma_start(out=raw_second[:], in_=w_rows[:, :, P : 2 * P])
+        nc.sync.dma_start(out=raw_rest[:], in_=w_rows[:, :, 2 * P :])
         load_words(w2_codes, w2_words[0])
         load_scale_rows(nc.sync, w2_plane, w2_scales[0], range(4))
-        nc.sync.dma_start(out=light_raw[1][:], in_=w_rows[:, :, 2 * P :])
 
         def entries(first, last):
             return offsets[:, first // PER_COLUMN : last // PER_COLUMN]
@@ -92,16 +93,16 @@ def tile_moe_cas_mlp_relu2_kernel(tc, x_words, x_scales, w, w1_words, w1_scales,
                 in_=w1_raw_plane[:].rearrange("p (m t) -> p t m", t=PACK)[:, ts, :],
             )
 
-        def round_light(u):
-            rounded = tile("rounded%d" % u, [P, 2 * P, PACK], BF16)
-            nc.vector.tensor_copy(
+        def round_light(first, last, raw, copy):
+            rounded = tile("rounded%d" % first, [P, (last - first) * P, PACK], BF16)
+            copy(
                 out=rounded[:].rearrange("p (c i) j -> p c j i", i=RUN),
-                in_=light_raw[u][:].rearrange("p j (c i) -> p c j i", i=RUN),
+                in_=raw.rearrange("p j (c i) -> p c j i", i=RUN),
             )
             return rounded
 
-        def quantize_light(u, rounded):
-            cols = slice(2 * u * P, 2 * (u + 1) * P)
+        def quantize_light(first, last, rounded):
+            cols = slice(first * P, last * P)
             nc.vector.quantize_mx(
                 out=light_codes[:, cols].bitcast(FP8X4),
                 scales=light_plane[:, cols],
@@ -157,18 +158,20 @@ def tile_moe_cas_mlp_relu2_kernel(tc, x_words, x_scales, w, w1_words, w1_scales,
                 in_=h[:].rearrange("p s t -> p (s t)"),
             )
 
-        def heavy(b, first, last, bank, copy):
-            acc = psum.tile([P, last - first], F32, name="z_acc", tag=bank)
-            nc.tensor.matmul_mx(
-                out=acc[:],
-                lhsT=w2_codes[:, 2 * b * P : 2 * (b + 1) * P].bitcast(FP4X4),
-                lhsT_scale=w2_plane[:, b * P : (b + 1) * P],
-                rhs=h_codes[:, first:last].bitcast(FP8X4),
-                rhs_scale=h_plane[:, first:last],
-                start=True,
-                stop=True,
-            )
-            z = tile("z%d_%d" % (b, first), [P, last - first], F32)
+        def heavy(blocks, first, last, bank, copy):
+            shape = [P, len(blocks), last - first]
+            acc = psum.tile(shape, F32, name="z_acc", tag=bank)
+            for column, b in enumerate(blocks):
+                nc.tensor.matmul_mx(
+                    out=acc[:, column, :],
+                    lhsT=w2_codes[:, 2 * b * P : 2 * (b + 1) * P].bitcast(FP4X4),
+                    lhsT_scale=w2_plane[:, b * P : (b + 1) * P],
+                    rhs=h_codes[:, first:last].bitcast(FP8X4),
+                    rhs_scale=h_plane[:, first:last],
+                    start=True,
+                    stop=True,
+                )
+            z = tile("z%d_%d" % (blocks[0], first), shape, F32)
             copy(out=z[:], in_=acc[:])
             return z
 
@@ -181,51 +184,48 @@ def tile_moe_cas_mlp_relu2_kernel(tc, x_words, x_scales, w, w1_words, w1_scales,
         def store(b, queue):
             queue.dma_start(out=out[b * P : (b + 1) * P, :], in_=windows[b][:])
 
-        nc.vector.tensor_copy(x_plane[0:4, :].bitcast(I32), x_first_rows[0:4, :].bitcast(I32))
-        nc.vector.tensor_copy(
+        rounded = round_light(0, 1, raw_first[:], nc.scalar.copy)
+        nc.scalar.copy(
             out=w1_codes[:].bitcast(U16).rearrange("p (t m) -> p t m", t=PACK),
             in_=w1_raw[:].bitcast(U16).rearrange("p (m t) -> p t m", t=PACK),
         )
-        nc.vector.tensor_copy(slot_plane[:], x_plane[:].indirect(offsets[:]))
+        half = S // 2
+        nc.vector.tensor_copy(slot_plane[:, :half], x_plane[:].indirect(entries(0, half)))
+        quantize_light(0, 1, rounded)
+        nc.vector.tensor_copy(slot_plane[:, half:], x_plane[:].indirect(entries(half, S)))
+        light(0, 0, "bank4", nc.scalar.copy)
+        light(0, 1, "bank5", nc.scalar.copy)
         words = gather_words(0)
         permute_w1_scales(slice(0, 2))
         permute_w1_scales(slice(2, PACK))
         words = words + gather_words(1, tag="w1_raw_plane")
-        rounded = round_light(0)
+        rounded = round_light(1, 2, raw_second[:], nc.vector.tensor_copy)
         relus = [first_product(c, words[c], "bank%d" % c) for c in range(CHUNKS)]
+        quantize_light(1, 2, rounded)
         h0 = square(0, relus[0])
-        quantize_light(0, rounded)
+        rounded = round_light(2, 4, raw_rest[:], nc.vector.tensor_copy)
         h1 = square(1, relus[1])
+        quantize_light(2, 4, rounded)
         quantize_hidden(0, h0)
-        h2 = square(2, relus[2])
         quantize_hidden(1, h1)
-        light(0, 0, "bank4", nc.scalar.copy)
-        h3 = square_on_scalar(3, relus[3])
-        quantize_hidden(2, h2)
-        light(0, 1, "bank5", nc.scalar.copy)
-        quantize_hidden(3, h3)
-        half = S // 2
-        z0a = heavy(0, 0, half, "bank0", nc.scalar.copy)
-        rounded = round_light(1)
         light(1, 0, "bank6", nc.scalar.copy)
-        scatter_on_vector(0, z0a[:], 0, half)
-        quantize_light(1, rounded)
-        z0b = heavy(0, half, S, "bank1", nc.scalar.copy)
+        h2 = square_on_scalar(2, relus[2])
         light(1, 1, "bank7", nc.scalar.copy)
-        z1 = heavy(1, 0, S, "bank2", nc.scalar.copy)
-        scatter_on_vector(0, z0b[:], half, S)
-        store(0, nc.sync)
-        scatter_on_scalar(1, z1[:, :half], 0, half)
-        z3 = heavy(3, 0, S, "bank3", nc.scalar.copy)
-        scatter_on_scalar(1, z1[:, half:], half, S)
-        store(1, nc.scalar)
-        z2 = heavy(2, 0, S, "bank0", nc.vector.tensor_copy)
-        light(2, 0, "bank4", nc.vector.tensor_copy)
-        light(2, 1, "bank5", nc.vector.tensor_copy)
-        light(3, 0, "bank6", nc.vector.tensor_copy)
-        light(3, 1, "bank7", nc.scalar.copy)
-        scatter_on_scalar(3, z3[:, :half], 0, half)
-        scatter_on_scalar(3, z3[:, half:], half, S)
-        store(3, nc.scalar)
-        scatter_on_vector(2, z2[:], 0, S)
-        store(2, nc.sync)
+        h3 = square_on_scalar(3, relus[3])
+        light(2, 0, "bank0", nc.vector.tensor_copy)
+        quantize_hidden(2, h2)
+        z_early = [heavy((0, 1), 0, half, "bank4", nc.scalar.copy)]
+        light(2, 1, "bank1", nc.vector.tensor_copy)
+        quantize_hidden(3, h3)
+        light(3, 0, "bank2", nc.vector.tensor_copy)
+        light(3, 1, "bank3", nc.vector.tensor_copy)
+        z_late = [heavy((b,), 0, S, "bank%d" % (b + 3), nc.vector.tensor_copy) for b in (2, 3)]
+        z_early.append(heavy((0, 1), half, S, "bank7", nc.scalar.copy))
+        for u in range(2):
+            for b in (0, 1):
+                scatter_on_scalar(b, z_early[u][:, b, :], u * half, (u + 1) * half)
+        for b in (0, 1):
+            store(b, nc.scalar)
+        for b in (2, 3):
+            scatter_on_vector(b, z_late[b - 2][:, 0, :], 0, S)
+            store(b, nc.sync)

@@ -158,7 +158,7 @@ def tile_moe_cas_mlp_relu2_kernel(tc, x_words, x_scales, w, w1_words, w1_scales,
                 in_=h[:].rearrange("p s t -> p (s t)"),
             )
 
-        def heavy(blocks, first, last, bank, copy):
+        def heavy(blocks, first, last, bank, copy, z=None):
             shape = [P, len(blocks), last - first]
             acc = psum.tile(shape, F32, name="z_acc", tag=bank)
             for column, b in enumerate(blocks):
@@ -171,8 +171,9 @@ def tile_moe_cas_mlp_relu2_kernel(tc, x_words, x_scales, w, w1_words, w1_scales,
                     start=True,
                     stop=True,
                 )
-            z = tile("z%d_%d" % (blocks[0], first), shape, F32)
-            copy(out=z[:], in_=acc[:])
+            if z is None:
+                z = tile("z%d_%d" % (blocks[0], first), shape, F32)[:]
+            copy(out=z, in_=acc[:])
             return z
 
         def scatter_on_vector(b, z, first, last):
@@ -214,18 +215,20 @@ def tile_moe_cas_mlp_relu2_kernel(tc, x_words, x_scales, w, w1_words, w1_scales,
         h3 = square_on_scalar(3, relus[3])
         light(2, 0, "bank0", nc.vector.tensor_copy)
         quantize_hidden(2, h2)
-        z_early = [heavy((0, 1), 0, half, "bank4", nc.scalar.copy)]
+        z_early = tile("z_early", [P, 2, S], F32)
+        heavy((0, 1), 0, half, "bank4", nc.scalar.copy, z_early[:, :, :half])
         light(2, 1, "bank1", nc.vector.tensor_copy)
         quantize_hidden(3, h3)
         light(3, 0, "bank2", nc.vector.tensor_copy)
         light(3, 1, "bank3", nc.vector.tensor_copy)
         z_late = [heavy((b,), 0, S, "bank%d" % (b + 3), nc.vector.tensor_copy) for b in (2, 3)]
-        z_early.append(heavy((0, 1), half, S, "bank7", nc.scalar.copy))
-        for u in range(2):
-            for b in (0, 1):
-                scatter_on_scalar(b, z_early[u][:, b, :], u * half, (u + 1) * half)
-        for b in (0, 1):
-            store(b, nc.scalar)
+        scatter_on_scalar(0, z_early[:, 0, :half], 0, half)
+        scatter_on_scalar(1, z_early[:, 1, :CHUNK], 0, CHUNK)
+        heavy((0, 1), half, S, "bank7", nc.scalar.copy, z_early[:, :, half:])
+        scatter_on_scalar(0, z_early[:, 0, half:], half, S)
+        store(0, nc.sync)
+        scatter_on_scalar(1, z_early[:, 1, CHUNK:], CHUNK, S)
         for b in (2, 3):
             scatter_on_vector(b, z_late[b - 2][:, 0, :], 0, S)
             store(b, nc.sync)
+        store(1, nc.scalar)

@@ -23,6 +23,7 @@ CHUNK = 128
 CHUNKS = S // CHUNK
 BLOCKS = N // P
 PER_COLUMN = 16
+WARM_ROWS = 32
 RUN = 4
 
 
@@ -43,19 +44,21 @@ def tile_moe_cas_mlp_relu2_kernel(tc, x_words, x_scales, w, w1_words, w1_scales,
         offsets = keep.tile([P, S // PER_COLUMN], U16, name="offsets")
         x_codes = tile("x_codes", [P, T], U32)
         x_plane = tile("x_plane", [P, T], U8)
+        x_first_rows = tile("x_first_rows", [P, T], U8)
         w1_raw = tile("w1_raw", [P, 2 * H], U8)
         w1_raw_plane = tile("w1_raw_plane", [P, H], U8)
         w1_codes = tile("w1_codes", [P, 2 * H], U8)
         w1_plane = tile("w1_plane", [P, H], U8)
         w2_codes = tile("w2_codes", [P, 2 * N], U8)
         w2_plane = tile("w2_plane", [P, N], U8)
-        raw_first = tile("raw_first", [P, PACK, P], F32)
-        raw_second = tile("raw_second", [P, PACK, P], F32)
-        raw_rest = tile("raw_rest", [P, PACK, 2 * P], F32)
+        raw_early = tile("raw_early", [P, PACK, 2 * P], F32)
+        raw_late = tile("raw_late", [P, PACK, 2 * P], F32)
         light_codes = tile("light_codes", [P, N], U32)
         light_plane = tile("light_plane", [P, N], U8)
         windows = [tile("window%d" % b, [P, T], F32) for b in range(BLOCKS)]
         slot_plane = tile("slot_plane", [P, S], U8)
+        relu = tile("relu", [P, S, PACK], F32)
+        h = [tile("h%d" % u, [P, S // 2, PACK], BF16) for u in range(2)]
         h_codes = tile("h_codes", [P, S], U32)
         h_plane = tile("h_plane", [P, S], U8)
 
@@ -68,22 +71,22 @@ def tile_moe_cas_mlp_relu2_kernel(tc, x_words, x_scales, w, w1_words, w1_scales,
         def load_words(tile_, words):
             nc.sync.dma_start(out=tile_[:].bitcast(I32), in_=words.bitcast(I32))
 
-        nc.sync.dma_start(out=raw_first[:], in_=w_rows[:, :, :P])
-        nc.sync.dma_start(offsets[:], offs)
+        load_scale_rows(nc.sync, x_first_rows, x_scales[0], (0,))
         load_words(w1_raw, w1_words[0])
-        load_scale_rows(nc.sync, x_plane, x_scales[0], range(4))
+        nc.sync.dma_start(offsets[:], offs)
+        load_scale_rows(nc.sync, x_plane, x_scales[0], (1, 2, 3))
         load_words(x_codes, x_words[0].rearrange("p t d -> p (t d)"))
         load_scale_rows(nc.sync, w1_raw_plane, w1_scales[0], range(4))
-        nc.sync.dma_start(out=raw_second[:], in_=w_rows[:, :, P : 2 * P])
-        nc.sync.dma_start(out=raw_rest[:], in_=w_rows[:, :, 2 * P :])
+        nc.sync.dma_start(out=raw_early[:], in_=w_rows[:, :, : 2 * P])
+        nc.sync.dma_start(out=raw_late[:], in_=w_rows[:, :, 2 * P :])
         load_words(w2_codes, w2_words[0])
         load_scale_rows(nc.sync, w2_plane, w2_scales[0], range(4))
 
         def entries(first, last):
             return offsets[:, first // PER_COLUMN : last // PER_COLUMN]
 
-        def gather_words(u, **place):
-            words = tile("slot_codes%d" % u, [P, 2 * CHUNK], U32, **place)
+        def gather_words(u, pool, **place):
+            words = pool.tile([P, 2 * CHUNK], U32, name="slot_codes%d" % u, align_bytes=64, **place)
             nc.vector.tensor_copy(words[:], x_codes[:].indirect(entries(2 * u * CHUNK, 2 * (u + 1) * CHUNK)))
             return [words[:, :CHUNK], words[:, CHUNK:]]
 
@@ -93,23 +96,21 @@ def tile_moe_cas_mlp_relu2_kernel(tc, x_words, x_scales, w, w1_words, w1_scales,
                 in_=w1_raw_plane[:].rearrange("p (m t) -> p t m", t=PACK)[:, ts, :],
             )
 
-        def round_light(first, last, raw, copy):
-            rounded = tile("rounded%d" % first, [P, (last - first) * P, PACK], BF16)
+        def round_light(rounded, raw, copy):
             copy(
-                out=rounded[:].rearrange("p (c i) j -> p c j i", i=RUN),
+                out=rounded.rearrange("p (c i) j -> p c j i", i=RUN),
                 in_=raw.rearrange("p j (c i) -> p c j i", i=RUN),
             )
-            return rounded
 
         def quantize_light(first, last, rounded):
             cols = slice(first * P, last * P)
             nc.vector.quantize_mx(
                 out=light_codes[:, cols].bitcast(FP8X4),
                 scales=light_plane[:, cols],
-                in_=rounded[:].rearrange("p n j -> p (n j)"),
+                in_=rounded.rearrange("p n j -> p (n j)"),
             )
 
-        def light(b, half, bank, copy):
+        def light(b, half, bank, copy, rest=None, share=BANK):
             cols = slice(b * P, (b + 1) * P)
             tokens = slice(half * BANK, (half + 1) * BANK)
             acc = psum.tile([P, BANK], F32, name="light_acc", tag=bank)
@@ -122,13 +123,16 @@ def tile_moe_cas_mlp_relu2_kernel(tc, x_words, x_scales, w, w1_words, w1_scales,
                 start=True,
                 stop=True,
             )
-            copy(out=windows[b][:, tokens], in_=acc[:])
+            columns = windows[b][:, tokens]
+            copy(out=columns[:, :share], in_=acc[:, :share])
+            if rest is not None:
+                rest(out=columns[:, share:], in_=acc[:, share:])
 
-        def first_product(c, words, bank):
-            acc = psum.tile([P, PACK, CHUNK], F32, name="h_acc", tag=bank)
-            for t in range(PACK):
+        def first_product(c, words, bank, relu, ts=range(PACK)):
+            acc = psum.tile([P, len(ts), CHUNK], F32, name="h_acc", tag=bank)
+            for column, t in enumerate(ts):
                 nc.tensor.matmul_mx(
-                    out=acc[:, t, :],
+                    out=acc[:, column, :],
                     lhsT=w1_codes[:, 2 * t * P : 2 * (t + 1) * P].bitcast(FP4X4),
                     lhsT_scale=w1_plane[:, t * P : (t + 1) * P],
                     rhs=words.bitcast(FP8X4),
@@ -136,26 +140,15 @@ def tile_moe_cas_mlp_relu2_kernel(tc, x_words, x_scales, w, w1_words, w1_scales,
                     start=True,
                     stop=True,
                 )
-            relu = tile("relu%d" % c, [P, CHUNK, PACK], F32)
-            nc.scalar.activation(out=relu[:], in_=acc[:].rearrange("p t s -> p s t"), func=ACT.Relu)
-            return relu
+            sums = acc[:].rearrange("p t s -> p s t")
+            nc.scalar.activation(out=relu, in_=sums, func=ACT.Relu)
+            return sums
 
-        def square(c, relu):
-            h = tile("h%d" % c, [P, CHUNK, PACK], BF16)
-            nc.vector.tensor_tensor(h[:], relu[:], relu[:], ALU.mult)
-            return h
-
-        def square_on_scalar(c, relu):
-            h = tile("h%d" % c, [P, CHUNK, PACK], BF16)
-            nc.scalar.activation(out=h[:], in_=relu[:], func=ACT.Square)
-            return h
-
-        def quantize_hidden(c, h):
-            slots = slice(c * CHUNK, (c + 1) * CHUNK)
+        def quantize_hidden(first, last, h):
             nc.vector.quantize_mx(
-                out=h_codes[:, slots].bitcast(FP8X4),
-                scales=h_plane[:, slots],
-                in_=h[:].rearrange("p s t -> p (s t)"),
+                out=h_codes[:, first:last].bitcast(FP8X4),
+                scales=h_plane[:, first:last],
+                in_=h.rearrange("p s t -> p (s t)"),
             )
 
         def heavy(blocks, first, last, bank, copy, z=None):
@@ -185,50 +178,66 @@ def tile_moe_cas_mlp_relu2_kernel(tc, x_words, x_scales, w, w1_words, w1_scales,
         def store(b, queue):
             queue.dma_start(out=out[b * P : (b + 1) * P, :], in_=windows[b][:])
 
-        rounded = round_light(0, 1, raw_first[:], nc.scalar.copy)
+        nc.vector.tensor_copy(x_plane[0:4, :].bitcast(I32), x_first_rows[0:4, :].bitcast(I32))
         nc.scalar.copy(
             out=w1_codes[:].bitcast(U16).rearrange("p (t m) -> p t m", t=PACK),
             in_=w1_raw[:].bitcast(U16).rearrange("p (m t) -> p t m", t=PACK),
         )
+        for bank in ("bank6", "bank7"):
+            idle = psum.tile([WARM_ROWS, BANK], F32, name="warm_up", tag=bank)
+            nc.tensor.matmul_mx(
+                out=idle[:],
+                lhsT=x_codes[:, :WARM_ROWS].bitcast(FP8X4),
+                lhsT_scale=x_plane[:, :WARM_ROWS],
+                rhs=x_codes[:, :BANK].bitcast(FP8X4),
+                rhs_scale=x_plane[:, :BANK],
+                start=True,
+                stop=True,
+            )
         half = S // 2
-        nc.vector.tensor_copy(slot_plane[:, :half], x_plane[:].indirect(entries(0, half)))
-        quantize_light(0, 1, rounded)
-        nc.vector.tensor_copy(slot_plane[:, half:], x_plane[:].indirect(entries(half, S)))
-        light(0, 0, "bank4", nc.scalar.copy)
-        light(0, 1, "bank5", nc.scalar.copy)
-        words = gather_words(0)
+        nc.vector.tensor_copy(slot_plane[:], x_plane[:].indirect(offsets[:]))
+        words = gather_words(0, keep)
         permute_w1_scales(slice(0, 2))
         permute_w1_scales(slice(2, PACK))
-        words = words + gather_words(1, tag="w1_raw_plane")
-        rounded = round_light(1, 2, raw_second[:], nc.vector.tensor_copy)
-        relus = [first_product(c, words[c], "bank%d" % c) for c in range(CHUNKS)]
-        quantize_light(1, 2, rounded)
-        h0 = square(0, relus[0])
-        rounded = round_light(2, 4, raw_rest[:], nc.vector.tensor_copy)
-        h1 = square(1, relus[1])
-        quantize_light(2, 4, rounded)
-        quantize_hidden(0, h0)
-        quantize_hidden(1, h1)
+        words = words + gather_words(1, keep, tag="w1_raw_plane")
+        early = tile("rounded_early", [P, 2 * P, PACK], BF16)
+        round_light(early[:], raw_early[:], nc.vector.tensor_copy)
+        chunks = [slice(c * CHUNK, (c + 1) * CHUNK) for c in range(CHUNKS)]
+        pairs = tile("relu_pairs", [P, 2, CHUNK, 2], F32)
+        first_product(0, words[0], "bank0", pairs[:, 0], (0, 1))
+        first_product(0, words[0], "bank4", pairs[:, 1], (2, 3))
+        for c in range(1, CHUNKS):
+            first_product(c, words[c], "bank%d" % c, relu[:, chunks[c], :])
+        source = pairs[:].rearrange("p u s e -> p s u e")
+        nc.vector.tensor_tensor(h[0][:, chunks[0], :].rearrange("p s (u e) -> p s u e", e=2), source, source, ALU.mult)
+        quantize_light(0, 2, early[:])
+        late = tile("rounded_late", [P, 2 * P, PACK], BF16)
+        round_light(late[:], raw_late[:], nc.vector.tensor_copy)
+        nc.vector.tensor_tensor(h[0][:, chunks[1], :], relu[:, chunks[1], :], relu[:, chunks[1], :], ALU.mult)
+        quantize_light(2, 4, late[:])
+        quantize_hidden(0, half, h[0][:])
+        nc.scalar.activation(out=h[1][:, chunks[0], :], in_=relu[:, chunks[2], :], func=ACT.Square)
+        light(0, 0, "bank4", nc.scalar.copy)
+        nc.scalar.activation(out=h[1][:, chunks[1], :], in_=relu[:, chunks[3], :], func=ACT.Square)
+        light(1, 1, "bank7", nc.vector.tensor_copy)
+        light(0, 1, "bank5", nc.scalar.copy)
         light(1, 0, "bank6", nc.scalar.copy)
-        h2 = square_on_scalar(2, relus[2])
-        light(1, 1, "bank7", nc.scalar.copy)
-        h3 = square_on_scalar(3, relus[3])
-        light(2, 0, "bank0", nc.vector.tensor_copy)
-        quantize_hidden(2, h2)
         z_early = tile("z_early", [P, 2, S], F32)
         heavy((0, 1), 0, half, "bank4", nc.scalar.copy, z_early[:, :, :half])
+        quantize_hidden(half, S, h[1][:])
+        light(2, 0, "bank0", nc.vector.tensor_copy)
         light(2, 1, "bank1", nc.vector.tensor_copy)
-        quantize_hidden(3, h3)
         light(3, 0, "bank2", nc.vector.tensor_copy)
-        light(3, 1, "bank3", nc.vector.tensor_copy)
-        z_late = [heavy((b,), 0, S, "bank%d" % (b + 3), nc.vector.tensor_copy) for b in (2, 3)]
+        z2 = heavy((2,), 0, S, "bank7", nc.vector.tensor_copy)
+        z3 = heavy((3,), 0, S, "bank5", nc.vector.tensor_copy)
+        light(3, 1, "bank0", nc.vector.tensor_copy)
         scatter_on_scalar(0, z_early[:, 0, :half], 0, half)
+        heavy((0, 1), half, S, "bank3", nc.scalar.copy, z_early[:, :, half:])
         scatter_on_scalar(1, z_early[:, 1, :CHUNK], 0, CHUNK)
-        heavy((0, 1), half, S, "bank7", nc.scalar.copy, z_early[:, :, half:])
         scatter_on_scalar(0, z_early[:, 0, half:], half, S)
-        store(0, nc.sync)
+        store(0, nc.scalar)
         scatter_on_scalar(1, z_early[:, 1, CHUNK:], CHUNK, S)
-        for b in (2, 3):
-            scatter_on_vector(b, z_late[b - 2][:, 0, :], 0, S)
+        for b, z in ((2, z2), (3, z3)):
+            scatter_on_vector(b, z[:, 0, :], 0, S)
             store(b, nc.sync)
         store(1, nc.scalar)

@@ -23,7 +23,6 @@ CHUNK = 128
 CHUNKS = S // CHUNK
 BLOCKS = N // P
 PER_COLUMN = 16
-WARM_ROWS = 32
 RUN = 4
 
 
@@ -85,10 +84,8 @@ def tile_moe_cas_mlp_relu2_kernel(tc, x_words, x_scales, w, w1_words, w1_scales,
         def entries(first, last):
             return offsets[:, first // PER_COLUMN : last // PER_COLUMN]
 
-        def gather_words(u, pool, **place):
-            words = pool.tile([P, 2 * CHUNK], U32, name="slot_codes%d" % u, align_bytes=64, **place)
-            nc.vector.tensor_copy(words[:], x_codes[:].indirect(entries(2 * u * CHUNK, 2 * (u + 1) * CHUNK)))
-            return [words[:, :CHUNK], words[:, CHUNK:]]
+        def gather_words(words, first, last):
+            nc.vector.tensor_copy(words, x_codes[:].indirect(entries(first, last)))
 
         def permute_w1_scales(ts):
             nc.vector.tensor_copy(
@@ -183,23 +180,16 @@ def tile_moe_cas_mlp_relu2_kernel(tc, x_words, x_scales, w, w1_words, w1_scales,
             out=w1_codes[:].bitcast(U16).rearrange("p (t m) -> p t m", t=PACK),
             in_=w1_raw[:].bitcast(U16).rearrange("p (m t) -> p t m", t=PACK),
         )
-        for bank in ("bank6", "bank7"):
-            idle = psum.tile([WARM_ROWS, BANK], F32, name="warm_up", tag=bank)
-            nc.tensor.matmul_mx(
-                out=idle[:],
-                lhsT=x_codes[:, :WARM_ROWS].bitcast(FP8X4),
-                lhsT_scale=x_plane[:, :WARM_ROWS],
-                rhs=x_codes[:, :BANK].bitcast(FP8X4),
-                rhs_scale=x_plane[:, :BANK],
-                start=True,
-                stop=True,
-            )
         half = S // 2
         nc.vector.tensor_copy(slot_plane[:], x_plane[:].indirect(offsets[:]))
-        words = gather_words(0, keep)
+        first_words = tile("first_words", [P, CHUNK], U32)
+        gather_words(first_words[:], 0, CHUNK)
         permute_w1_scales(slice(0, 2))
         permute_w1_scales(slice(2, PACK))
-        words = words + gather_words(1, keep, tag="w1_raw_plane")
+        later_words = tile("later_words", [P, S - CHUNK], U32, tag="w1_raw_plane")
+        gather_words(later_words[:, :CHUNK], CHUNK, half)
+        gather_words(later_words[:, CHUNK:], half, S)
+        words = [first_words[:]] + [later_words[:, c * CHUNK : (c + 1) * CHUNK] for c in range(CHUNKS - 1)]
         early = tile("rounded_early", [P, 2 * P, PACK], BF16)
         round_light(early[:], raw_early[:], nc.vector.tensor_copy)
         chunks = [slice(c * CHUNK, (c + 1) * CHUNK) for c in range(CHUNKS)]

@@ -212,17 +212,17 @@ def tile_moe_cas_mlp_relu2_kernel(tc, x_words, x_scales, w, w1_words, w1_scales,
         light(1, 1, "bank7", nc.vector.tensor_copy)
         light(0, 1, "bank5", nc.scalar.copy)
         light(1, 0, "bank6", nc.scalar.copy)
+        light(2, 0, "bank0", nc.vector.tensor_copy)
+        light(3, 0, "bank2", nc.scalar.copy)
+        quantize_hidden(half, S, h[1][:])
         z_early = tile("z_early", [P, 2, S], F32)
         heavy((0, 1), 0, half, "bank4", nc.scalar.copy, z_early[:, :, :half])
-        quantize_hidden(half, S, h[1][:])
-        light(2, 0, "bank0", nc.vector.tensor_copy)
         light(2, 1, "bank1", nc.vector.tensor_copy)
-        light(3, 0, "bank2", nc.vector.tensor_copy)
+        heavy((0, 1), half, S, "bank3", nc.vector.tensor_copy, z_early[:, :, half:])
         z2 = heavy((2,), 0, S, "bank7", nc.vector.tensor_copy)
         z3 = heavy((3,), 0, S, "bank5", nc.vector.tensor_copy)
         light(3, 1, "bank0", nc.vector.tensor_copy)
         scatter_on_scalar(0, z_early[:, 0, :half], 0, half)
-        heavy((0, 1), half, S, "bank3", nc.scalar.copy, z_early[:, :, half:])
         scatter_on_scalar(1, z_early[:, 1, :CHUNK], 0, CHUNK)
         scatter_on_scalar(0, z_early[:, 0, half:], half, S)
         store(0, nc.scalar)

@@ -70,10 +70,10 @@ def tile_moe_cas_mlp_relu2_kernel(tc, x_words, x_scales, w, w1_words, w1_scales,
         def load_words(tile_, words):
             nc.sync.dma_start(out=tile_[:].bitcast(I32), in_=words.bitcast(I32))
 
-        load_scale_rows(nc.sync, x_first_rows, x_scales[0], (0,))
+        load_scale_rows(nc.sync, x_first_rows, x_scales[0], (0, 1))
         load_words(w1_raw, w1_words[0])
         nc.sync.dma_start(offsets[:], offs)
-        load_scale_rows(nc.sync, x_plane, x_scales[0], (1, 2, 3))
+        load_scale_rows(nc.sync, x_plane, x_scales[0], (2, 3))
         load_words(x_codes, x_words[0].rearrange("p t d -> p (t d)"))
         load_scale_rows(nc.sync, w1_raw_plane, w1_scales[0], range(4))
         nc.sync.dma_start(out=raw_early[:], in_=w_rows[:, :, : 2 * P])
@@ -175,7 +175,9 @@ def tile_moe_cas_mlp_relu2_kernel(tc, x_words, x_scales, w, w1_words, w1_scales,
         def store(b, queue):
             queue.dma_start(out=out[b * P : (b + 1) * P, :], in_=windows[b][:])
 
-        nc.vector.tensor_copy(x_plane[0:4, :].bitcast(I32), x_first_rows[0:4, :].bitcast(I32))
+        for q in (0, 1):
+            rows = slice(32 * q, 32 * q + 4)
+            nc.vector.tensor_copy(x_plane[rows, :].bitcast(I32), x_first_rows[rows, :].bitcast(I32))
         nc.scalar.copy(
             out=w1_codes[:].bitcast(U16).rearrange("p (t m) -> p t m", t=PACK),
             in_=w1_raw[:].bitcast(U16).rearrange("p (m t) -> p t m", t=PACK),

@@ -46,7 +46,7 @@ def tile_moe_cas_mlp_relu2_kernel(tc, x_words, x_scales, w, w1_words, w1_scales,
         x_first_rows = tile("x_first_rows", [P, T], U8)
         w1_raw = tile("w1_raw", [P, 2 * H], U8)
         w1_raw_plane = tile("w1_raw_plane", [P, H], U8)
-        w1_codes = tile("w1_codes", [P, 2 * H], U8)
+        w1_codes = [tile("w1_codes%d" % u, [P, H], U8) for u in range(2)]
         w1_plane = tile("w1_plane", [P, H], U8)
         w2_codes = tile("w2_codes", [P, 2 * N], U8)
         w2_plane = tile("w2_plane", [P, N], U8)
@@ -71,10 +71,10 @@ def tile_moe_cas_mlp_relu2_kernel(tc, x_words, x_scales, w, w1_words, w1_scales,
             nc.sync.dma_start(out=tile_[:].bitcast(I32), in_=words.bitcast(I32))
 
         load_scale_rows(nc.sync, x_first_rows, x_scales[0], (0, 1))
-        load_words(w1_raw, w1_words[0])
         nc.sync.dma_start(offsets[:], offs)
         load_scale_rows(nc.sync, x_plane, x_scales[0], (2, 3))
         load_words(x_codes, x_words[0].rearrange("p t d -> p (t d)"))
+        load_words(w1_raw, w1_words[0])
         load_scale_rows(nc.sync, w1_raw_plane, w1_scales[0], range(4))
         nc.sync.dma_start(out=raw_early[:], in_=w_rows[:, :, : 2 * P])
         nc.sync.dma_start(out=raw_late[:], in_=w_rows[:, :, 2 * P :])
@@ -130,7 +130,7 @@ def tile_moe_cas_mlp_relu2_kernel(tc, x_words, x_scales, w, w1_words, w1_scales,
             for column, t in enumerate(ts):
                 nc.tensor.matmul_mx(
                     out=acc[:, column, :],
-                    lhsT=w1_codes[:, 2 * t * P : 2 * (t + 1) * P].bitcast(FP4X4),
+                    lhsT=w1_codes[t // 2][:, 2 * (t % 2) * P : 2 * (t % 2 + 1) * P].bitcast(FP4X4),
                     lhsT_scale=w1_plane[:, t * P : (t + 1) * P],
                     rhs=words.bitcast(FP8X4),
                     rhs_scale=slot_plane[:, c * CHUNK : (c + 1) * CHUNK],
@@ -178,20 +178,20 @@ def tile_moe_cas_mlp_relu2_kernel(tc, x_words, x_scales, w, w1_words, w1_scales,
         for q in (0, 1):
             rows = slice(32 * q, 32 * q + 4)
             nc.vector.tensor_copy(x_plane[rows, :].bitcast(I32), x_first_rows[rows, :].bitcast(I32))
-        nc.scalar.copy(
-            out=w1_codes[:].bitcast(U16).rearrange("p (t m) -> p t m", t=PACK),
-            in_=w1_raw[:].bitcast(U16).rearrange("p (m t) -> p t m", t=PACK),
-        )
+        for u in range(2):
+            nc.scalar.copy(
+                out=w1_codes[u][:].bitcast(U16).rearrange("p (t m) -> p t m", t=2),
+                in_=w1_raw[:].bitcast(U16).rearrange("p (m t) -> p t m", t=PACK)[:, 2 * u : 2 * u + 2, :],
+            )
         half = S // 2
         nc.vector.tensor_copy(slot_plane[:], x_plane[:].indirect(offsets[:]))
-        first_words = tile("first_words", [P, CHUNK], U32)
-        gather_words(first_words[:], 0, CHUNK)
+        first_words = tile("first_words", [P, half], U32)
+        gather_words(first_words[:], 0, half)
         permute_w1_scales(slice(0, 2))
         permute_w1_scales(slice(2, PACK))
-        later_words = tile("later_words", [P, S - CHUNK], U32, tag="w1_raw_plane")
-        gather_words(later_words[:, :CHUNK], CHUNK, half)
-        gather_words(later_words[:, CHUNK:], half, S)
-        words = [first_words[:]] + [later_words[:, c * CHUNK : (c + 1) * CHUNK] for c in range(CHUNKS - 1)]
+        later_words = tile("later_words", [P, half], U32, tag="w1_raw_plane")
+        gather_words(later_words[:], half, S)
+        words = [part[:, c * CHUNK : (c + 1) * CHUNK] for part in (first_words, later_words) for c in range(2)]
         early = tile("rounded_early", [P, 2 * P, PACK], BF16)
         round_light(early[:], raw_early[:], nc.vector.tensor_copy)
         chunks = [slice(c * CHUNK, (c + 1) * CHUNK) for c in range(CHUNKS)]

@@ -21,18 +21,15 @@ PACK = 4
 BANK = 512
 CHUNK = 128
 CHUNKS = S // CHUNK
-BLOCKS = N // P
+HALF = S // 2
+BANDS = N // P
 PER_COLUMN = 16
 RUN = 4
 
 
-def load_scale_rows(queue, plane, rows, quadrants):
-    for q in quadrants:
-        queue.dma_start(out=plane[32 * q : 32 * q + 4, :].bitcast(I32), in_=rows[4 * q : 4 * q + 4, :].bitcast(I32))
-
-
 def tile_moe_cas_mlp_relu2_kernel(tc, x_words, x_scales, w, w1_words, w1_scales, w2_words, w2_scales, offs, out):
     nc = tc.nc
+    on_vector, on_scalar = nc.vector.tensor_copy, nc.scalar.copy
     with ExitStack() as ctx:
         keep = ctx.enter_context(tc.tile_pool(name="keep", bufs=1))
         psum = ctx.enter_context(tc.psum_pool(name="psum", bufs=1))
@@ -50,127 +47,116 @@ def tile_moe_cas_mlp_relu2_kernel(tc, x_words, x_scales, w, w1_words, w1_scales,
         w1_plane = tile("w1_plane", [P, H], U8)
         w2_codes = tile("w2_codes", [P, 2 * N], U8)
         w2_plane = tile("w2_plane", [P, N], U8)
-        raw_early = tile("raw_early", [P, PACK, 2 * P], F32)
-        raw_late = tile("raw_late", [P, PACK, 2 * P], F32)
-        light_codes = tile("light_codes", [P, N], U32)
-        light_plane = tile("light_plane", [P, N], U8)
-        windows = [tile("window%d" % b, [P, T], F32) for b in range(BLOCKS)]
+        w_early = tile("w_early", [P, PACK, 2 * P], F32)
+        w_late = tile("w_late", [P, PACK, 2 * P], F32)
+        w_codes = tile("w_codes", [P, N], U32)
+        w_plane = tile("w_plane", [P, N], U8)
+        windows = [tile("window%d" % b, [P, T], F32) for b in range(BANDS)]
         slot_plane = tile("slot_plane", [P, S], U8)
         relu = tile("relu", [P, S, PACK], F32)
-        h = [tile("h%d" % u, [P, S // 2, PACK], BF16) for u in range(2)]
+        h = [tile("h%d" % u, [P, HALF, PACK], BF16) for u in range(2)]
         h_codes = tile("h_codes", [P, S], U32)
         h_plane = tile("h_plane", [P, S], U8)
 
-        nc.vector.memset(x_plane[:].bitcast(I32), 0)
-        nc.vector.memset(w1_raw_plane[:].bitcast(I32), 0)
-        nc.vector.memset(w2_plane[:].bitcast(I32), 0)
+        for plane in (x_plane, w1_raw_plane, w2_plane):
+            nc.vector.memset(plane[:].bitcast(I32), 0)
+
+        def load_bytes(target, source):
+            nc.sync.dma_start(out=target.bitcast(I32), in_=source.bitcast(I32))
+
+        def load_scale_rows(plane, rows, quadrants):
+            for q in quadrants:
+                load_bytes(plane[32 * q : 32 * q + 4, :], rows[4 * q : 4 * q + 4, :])
 
         w_rows = w.rearrange("(p j) n -> p j n", j=PACK)
-
-        def load_words(tile_, words):
-            nc.sync.dma_start(out=tile_[:].bitcast(I32), in_=words.bitcast(I32))
-
-        load_scale_rows(nc.sync, x_first_rows, x_scales[0], (0, 1))
+        load_scale_rows(x_first_rows, x_scales[0], (0, 1))
         nc.sync.dma_start(offsets[:], offs)
-        load_scale_rows(nc.sync, x_plane, x_scales[0], (2, 3))
-        load_words(x_codes, x_words[0].rearrange("p t d -> p (t d)"))
-        load_words(w1_raw, w1_words[0])
-        load_scale_rows(nc.sync, w1_raw_plane, w1_scales[0], range(4))
-        nc.sync.dma_start(out=raw_early[:], in_=w_rows[:, :, : 2 * P])
-        nc.sync.dma_start(out=raw_late[:], in_=w_rows[:, :, 2 * P :])
-        load_words(w2_codes, w2_words[0])
-        load_scale_rows(nc.sync, w2_plane, w2_scales[0], range(4))
+        load_scale_rows(x_plane, x_scales[0], (2, 3))
+        load_bytes(x_codes[:], x_words[0].rearrange("p t d -> p (t d)"))
+        load_bytes(w1_raw[:], w1_words[0])
+        load_scale_rows(w1_raw_plane, w1_scales[0], range(4))
+        nc.sync.dma_start(out=w_early[:], in_=w_rows[:, :, : 2 * P])
+        nc.sync.dma_start(out=w_late[:], in_=w_rows[:, :, 2 * P :])
+        load_bytes(w2_codes[:], w2_words[0])
+        load_scale_rows(w2_plane, w2_scales[0], range(4))
 
         def entries(first, last):
             return offsets[:, first // PER_COLUMN : last // PER_COLUMN]
 
-        def gather_words(words, first, last):
-            nc.vector.tensor_copy(words, x_codes[:].indirect(entries(first, last)))
+        def gather_words(name, first, **place):
+            gathered = tile(name, [P, HALF], U32, **place)
+            nc.vector.tensor_copy(gathered[:], x_codes[:].indirect(entries(first, first + HALF)))
+            return [gathered[:, :CHUNK], gathered[:, CHUNK:]]
 
-        def permute_w1_scales(ts):
+        def round_w(name, raw):
+            rounded = tile(name, [P, 2 * P, PACK], BF16)
             nc.vector.tensor_copy(
-                out=w1_plane[:].rearrange("p (t m) -> p t m", t=PACK)[:, ts, :],
-                in_=w1_raw_plane[:].rearrange("p (m t) -> p t m", t=PACK)[:, ts, :],
+                out=rounded[:].rearrange("p (c i) j -> p c j i", i=RUN),
+                in_=raw[:].rearrange("p j (c i) -> p c j i", i=RUN),
             )
+            return rounded
 
-        def round_light(rounded, raw, copy):
-            copy(
-                out=rounded.rearrange("p (c i) j -> p c j i", i=RUN),
-                in_=raw.rearrange("p j (c i) -> p c j i", i=RUN),
-            )
-
-        def quantize_light(first, last, rounded):
-            cols = slice(first * P, last * P)
+        def quantize(codes, plane, first, values):
+            columns = slice(first, first + values.shape[1])
             nc.vector.quantize_mx(
-                out=light_codes[:, cols].bitcast(FP8X4),
-                scales=light_plane[:, cols],
-                in_=rounded.rearrange("p n j -> p (n j)"),
+                out=codes[:, columns].bitcast(FP8X4),
+                scales=plane[:, columns],
+                in_=values[:].rearrange("p c j -> p (c j)"),
             )
 
-        def light(b, half, bank, copy, rest=None, share=BANK):
-            cols = slice(b * P, (b + 1) * P)
-            tokens = slice(half * BANK, (half + 1) * BANK)
-            acc = psum.tile([P, BANK], F32, name="light_acc", tag=bank)
+        def product(acc, lhsT, lhsT_scale, rhs, rhs_scale):
             nc.tensor.matmul_mx(
-                out=acc[:],
-                lhsT=light_codes[:, cols].bitcast(FP8X4),
-                lhsT_scale=light_plane[:, cols],
-                rhs=x_codes[:, tokens].bitcast(FP8X4),
-                rhs_scale=x_plane[:, tokens],
-                start=True,
-                stop=True,
+                out=acc, lhsT=lhsT, lhsT_scale=lhsT_scale, rhs=rhs, rhs_scale=rhs_scale, start=True, stop=True
             )
-            columns = windows[b][:, tokens]
-            copy(out=columns[:, :share], in_=acc[:, :share])
-            if rest is not None:
-                rest(out=columns[:, share:], in_=acc[:, share:])
 
-        def first_product(c, words, bank, relu, ts=range(PACK)):
-            acc = psum.tile([P, len(ts), CHUNK], F32, name="h_acc", tag=bank)
+        def light(b, u, bank, copy):
+            rows = slice(b * P, (b + 1) * P)
+            tokens = slice(u * BANK, (u + 1) * BANK)
+            acc = psum.tile([P, BANK], F32, name="light_acc", tag=bank)
+            product(
+                acc[:],
+                w_codes[:, rows].bitcast(FP8X4),
+                w_plane[:, rows],
+                x_codes[:, tokens].bitcast(FP8X4),
+                x_plane[:, tokens],
+            )
+            copy(out=windows[b][:, tokens], in_=acc[:])
+
+        def hidden(c, words, bank, target, ts=range(PACK)):
+            acc = psum.tile([P, len(ts), CHUNK], F32, name="hidden_acc", tag=bank)
             for column, t in enumerate(ts):
-                nc.tensor.matmul_mx(
-                    out=acc[:, column, :],
-                    lhsT=w1_codes[t // 2][:, 2 * (t % 2) * P : 2 * (t % 2 + 1) * P].bitcast(FP4X4),
-                    lhsT_scale=w1_plane[:, t * P : (t + 1) * P],
-                    rhs=words.bitcast(FP8X4),
-                    rhs_scale=slot_plane[:, c * CHUNK : (c + 1) * CHUNK],
-                    start=True,
-                    stop=True,
+                product(
+                    acc[:, column, :],
+                    w1_codes[t // 2][:, 2 * (t % 2) * P : 2 * (t % 2 + 1) * P].bitcast(FP4X4),
+                    w1_plane[:, t * P : (t + 1) * P],
+                    words.bitcast(FP8X4),
+                    slot_plane[:, c * CHUNK : (c + 1) * CHUNK],
                 )
-            sums = acc[:].rearrange("p t s -> p s t")
-            nc.scalar.activation(out=relu, in_=sums, func=ACT.Relu)
-            return sums
+            nc.scalar.activation(out=target, in_=acc[:].rearrange("p t s -> p s t"), func=ACT.Relu)
 
-        def quantize_hidden(first, last, h):
-            nc.vector.quantize_mx(
-                out=h_codes[:, first:last].bitcast(FP8X4),
-                scales=h_plane[:, first:last],
-                in_=h.rearrange("p s t -> p (s t)"),
-            )
+        def relu_of(c):
+            return relu[:, c * CHUNK : (c + 1) * CHUNK, :]
 
-        def heavy(blocks, first, last, bank, copy, z=None):
-            shape = [P, len(blocks), last - first]
-            acc = psum.tile(shape, F32, name="z_acc", tag=bank)
-            for column, b in enumerate(blocks):
-                nc.tensor.matmul_mx(
-                    out=acc[:, column, :],
-                    lhsT=w2_codes[:, 2 * b * P : 2 * (b + 1) * P].bitcast(FP4X4),
-                    lhsT_scale=w2_plane[:, b * P : (b + 1) * P],
-                    rhs=h_codes[:, first:last].bitcast(FP8X4),
-                    rhs_scale=h_plane[:, first:last],
-                    start=True,
-                    stop=True,
+        def h_of(c):
+            return h[c // 2][:, (c % 2) * CHUNK : (c % 2 + 1) * CHUNK, :]
+
+        def heavy(bands, first, last, bank):
+            acc = psum.tile([P, len(bands), last - first], F32, name="z_acc", tag=bank)
+            for column, b in enumerate(bands):
+                product(
+                    acc[:, column, :],
+                    w2_codes[:, 2 * b * P : 2 * (b + 1) * P].bitcast(FP4X4),
+                    w2_plane[:, b * P : (b + 1) * P],
+                    h_codes[:, first:last].bitcast(FP8X4),
+                    h_plane[:, first:last],
                 )
-            if z is None:
-                z = tile("z%d_%d" % (blocks[0], first), shape, F32)[:]
-            copy(out=z, in_=acc[:])
-            return z
+            return acc
 
-        def scatter_on_vector(b, z, first, last):
-            nc.vector.tensor_copy(windows[b][:].indirect(entries(first, last)), z)
-
-        def scatter_on_scalar(b, z, first, last):
-            nc.scalar.activation(windows[b][:].indirect(entries(first, last)), z, ACT.Copy)
+        def heavy_on_vector(b, bank):
+            acc = heavy((b,), 0, S, bank)
+            z = tile("z%d" % b, [P, 1, S], F32)
+            nc.vector.tensor_copy(out=z[:], in_=acc[:])
+            return z[:, 0, :]
 
         def store(b, queue):
             queue.dma_start(out=out[b * P : (b + 1) * P, :], in_=windows[b][:])
@@ -178,58 +164,61 @@ def tile_moe_cas_mlp_relu2_kernel(tc, x_words, x_scales, w, w1_words, w1_scales,
         for q in (0, 1):
             rows = slice(32 * q, 32 * q + 4)
             nc.vector.tensor_copy(x_plane[rows, :].bitcast(I32), x_first_rows[rows, :].bitcast(I32))
+
         for u in range(2):
             nc.scalar.copy(
                 out=w1_codes[u][:].bitcast(U16).rearrange("p (t m) -> p t m", t=2),
                 in_=w1_raw[:].bitcast(U16).rearrange("p (m t) -> p t m", t=PACK)[:, 2 * u : 2 * u + 2, :],
             )
-        half = S // 2
         nc.vector.tensor_copy(slot_plane[:], x_plane[:].indirect(offsets[:]))
-        first_words = tile("first_words", [P, half], U32)
-        gather_words(first_words[:], 0, half)
-        permute_w1_scales(slice(0, 2))
-        permute_w1_scales(slice(2, PACK))
-        later_words = tile("later_words", [P, half], U32, tag="w1_raw_plane")
-        gather_words(later_words[:], half, S)
-        words = [part[:, c * CHUNK : (c + 1) * CHUNK] for part in (first_words, later_words) for c in range(2)]
-        early = tile("rounded_early", [P, 2 * P, PACK], BF16)
-        round_light(early[:], raw_early[:], nc.vector.tensor_copy)
-        chunks = [slice(c * CHUNK, (c + 1) * CHUNK) for c in range(CHUNKS)]
+        words = gather_words("first_words", 0)
+        for u in range(2):
+            nc.vector.tensor_copy(
+                out=w1_plane[:].rearrange("p (t m) -> p t m", t=PACK)[:, 2 * u : 2 * u + 2, :],
+                in_=w1_raw_plane[:].rearrange("p (m t) -> p t m", t=PACK)[:, 2 * u : 2 * u + 2, :],
+            )
+        words = words + gather_words("later_words", HALF, tag="w1_raw_plane")
+        rounded_early = round_w("rounded_early", w_early)
+
         pairs = tile("relu_pairs", [P, 2, CHUNK, 2], F32)
-        first_product(0, words[0], "bank0", pairs[:, 0], (0, 1))
-        first_product(0, words[0], "bank4", pairs[:, 1], (2, 3))
+        hidden(0, words[0], "bank0", pairs[:, 0], (0, 1))
+        hidden(0, words[0], "bank4", pairs[:, 1], (2, 3))
         for c in range(1, CHUNKS):
-            first_product(c, words[c], "bank%d" % c, relu[:, chunks[c], :])
-        source = pairs[:].rearrange("p u s e -> p s u e")
-        nc.vector.tensor_tensor(h[0][:, chunks[0], :].rearrange("p s (u e) -> p s u e", e=2), source, source, ALU.mult)
-        quantize_light(0, 2, early[:])
-        late = tile("rounded_late", [P, 2 * P, PACK], BF16)
-        round_light(late[:], raw_late[:], nc.vector.tensor_copy)
-        nc.vector.tensor_tensor(h[0][:, chunks[1], :], relu[:, chunks[1], :], relu[:, chunks[1], :], ALU.mult)
-        quantize_light(2, 4, late[:])
-        quantize_hidden(0, half, h[0][:])
-        nc.scalar.activation(out=h[1][:, chunks[0], :], in_=relu[:, chunks[2], :], func=ACT.Square)
-        light(0, 0, "bank4", nc.scalar.copy)
-        nc.scalar.activation(out=h[1][:, chunks[1], :], in_=relu[:, chunks[3], :], func=ACT.Square)
-        light(1, 1, "bank7", nc.vector.tensor_copy)
-        light(0, 1, "bank5", nc.scalar.copy)
-        light(1, 0, "bank6", nc.scalar.copy)
-        light(2, 0, "bank0", nc.vector.tensor_copy)
-        light(3, 0, "bank2", nc.scalar.copy)
-        quantize_hidden(half, S, h[1][:])
-        z_early = tile("z_early", [P, 2, S], F32)
-        heavy((0, 1), 0, half, "bank4", nc.scalar.copy, z_early[:, :, :half])
-        light(2, 1, "bank1", nc.vector.tensor_copy)
-        heavy((0, 1), half, S, "bank3", nc.vector.tensor_copy, z_early[:, :, half:])
-        z2 = heavy((2,), 0, S, "bank7", nc.vector.tensor_copy)
-        z3 = heavy((3,), 0, S, "bank5", nc.vector.tensor_copy)
-        light(3, 1, "bank0", nc.vector.tensor_copy)
-        scatter_on_scalar(0, z_early[:, 0, :half], 0, half)
-        scatter_on_scalar(1, z_early[:, 1, :CHUNK], 0, CHUNK)
-        scatter_on_scalar(0, z_early[:, 0, half:], half, S)
-        store(0, nc.scalar)
-        scatter_on_scalar(1, z_early[:, 1, CHUNK:], CHUNK, S)
+            hidden(c, words[c], "bank%d" % c, relu_of(c))
+
+        by_slot = pairs[:].rearrange("p u s e -> p s u e")
+        nc.vector.tensor_tensor(h_of(0).rearrange("p s (u e) -> p s u e", e=2), by_slot, by_slot, ALU.mult)
+        quantize(w_codes, w_plane, 0, rounded_early)
+        rounded_late = round_w("rounded_late", w_late)
+        nc.vector.tensor_tensor(h_of(1), relu_of(1), relu_of(1), ALU.mult)
+        quantize(w_codes, w_plane, 2 * P, rounded_late)
+        quantize(h_codes, h_plane, 0, h[0])
+
+        nc.scalar.activation(out=h_of(2), in_=relu_of(2), func=ACT.Square)
+        light(0, 0, "bank4", on_scalar)
+        nc.scalar.activation(out=h_of(3), in_=relu_of(3), func=ACT.Square)
+        light(1, 1, "bank7", on_vector)
+        light(0, 1, "bank5", on_scalar)
+        light(1, 0, "bank6", on_scalar)
+        light(2, 0, "bank0", on_vector)
+        light(3, 0, "bank2", on_scalar)
+        quantize(h_codes, h_plane, HALF, h[1])
+
+        z01 = tile("z01", [P, 2, S], F32)
+        acc = heavy((0, 1), 0, HALF, "bank4")
+        for b in (0, 1):
+            nc.scalar.copy(out=z01[:, b : b + 1, :HALF], in_=acc[:, b : b + 1, :])
+        light(2, 1, "bank1", on_vector)
+        nc.vector.tensor_copy(out=z01[:, :, HALF:], in_=heavy((0, 1), HALF, S, "bank3")[:])
+        z2 = heavy_on_vector(2, "bank7")
+        z3 = heavy_on_vector(3, "bank5")
+        light(3, 1, "bank0", on_vector)
+
+        for b, first, last in ((0, 0, HALF), (1, 0, CHUNK), (0, HALF, S), (1, CHUNK, S)):
+            nc.scalar.activation(windows[b][:].indirect(entries(first, last)), z01[:, b, first:last], ACT.Copy)
+            if (b, last) == (0, S):
+                store(0, nc.scalar)
         for b, z in ((2, z2), (3, z3)):
-            scatter_on_vector(b, z[:, 0, :], 0, S)
+            nc.vector.tensor_copy(windows[b][:].indirect(offsets[:]), z)
             store(b, nc.sync)
         store(1, nc.scalar)

@@ -89,10 +89,10 @@ def tile_moe_cas_mlp_relu2_kernel(tc, x_words, x_scales, w, w1_words, w1_scales,
             return [gathered[:, :CHUNK], gathered[:, CHUNK:]]
 
         def round_w(name, raw):
-            rounded = tile(name, [P, 2 * P, PACK], BF16)
+            rounded = tile(name, [P, raw.shape[2], PACK], BF16)
             nc.vector.tensor_copy(
                 out=rounded[:].rearrange("p (c i) j -> p c j i", i=RUN),
-                in_=raw[:].rearrange("p j (c i) -> p c j i", i=RUN),
+                in_=raw.rearrange("p j (c i) -> p c j i", i=RUN),
             )
             return rounded
 
@@ -177,8 +177,11 @@ def tile_moe_cas_mlp_relu2_kernel(tc, x_words, x_scales, w, w1_words, w1_scales,
                 out=w1_plane[:].rearrange("p (t m) -> p t m", t=PACK)[:, 2 * u : 2 * u + 2, :],
                 in_=w1_raw_plane[:].rearrange("p (m t) -> p t m", t=PACK)[:, 2 * u : 2 * u + 2, :],
             )
-        words = words + gather_words("later_words", HALF, tag="w1_raw_plane")
-        rounded_early = round_w("rounded_early", w_early)
+        words = words + gather_words("later_words", HALF, tag="w1_raw")
+
+        rounded_early = [round_w("rounded%d" % b, w_early[:, :, b * P : (b + 1) * P]) for b in (0, 1)]
+        for b in (0, 1):
+            quantize(w_codes, w_plane, b * P, rounded_early[b])
 
         pairs = tile("relu_pairs", [P, 2, CHUNK, 2], F32)
         hidden(0, words[0], "bank0", pairs[:, 0], (0, 1))
@@ -188,8 +191,7 @@ def tile_moe_cas_mlp_relu2_kernel(tc, x_words, x_scales, w, w1_words, w1_scales,
 
         by_slot = pairs[:].rearrange("p u s e -> p s u e")
         nc.vector.tensor_tensor(h_of(0).rearrange("p s (u e) -> p s u e", e=2), by_slot, by_slot, ALU.mult)
-        quantize(w_codes, w_plane, 0, rounded_early)
-        rounded_late = round_w("rounded_late", w_late)
+        rounded_late = round_w("rounded_late", w_late[:])
         nc.vector.tensor_tensor(h_of(1), relu_of(1), relu_of(1), ALU.mult)
         quantize(w_codes, w_plane, 2 * P, rounded_late)
         quantize(h_codes, h_plane, 0, h[0])

@@ -54,7 +54,7 @@ def tile_moe_cas_mlp_relu2_kernel(tc, x_words, x_scales, w, w1_words, w1_scales,
         windows = [tile("window%d" % b, [P, T], F32) for b in range(BANDS)]
         slot_plane = tile("slot_plane", [P, S], U8)
         relu = tile("relu", [P, S, PACK], F32)
-        h = [tile("h%d" % u, [P, HALF, PACK], BF16) for u in range(2)]
+        h = tile("h", [P, 3 * CHUNK, PACK], BF16)
         h_codes = tile("h_codes", [P, S], U32)
         h_plane = tile("h_plane", [P, S], U8)
 
@@ -96,13 +96,12 @@ def tile_moe_cas_mlp_relu2_kernel(tc, x_words, x_scales, w, w1_words, w1_scales,
             )
             return rounded
 
-        def quantize(codes, plane, first, values):
-            columns = slice(first, first + values.shape[1])
-            nc.vector.quantize_mx(
-                out=codes[:, columns].bitcast(FP8X4),
-                scales=plane[:, columns],
-                in_=values[:].rearrange("p c j -> p (c j)"),
-            )
+        def quantize(codes, plane, values):
+            nc.vector.quantize_mx(out=codes.bitcast(FP8X4), scales=plane, in_=values.rearrange("p c j -> p (c j)"))
+
+        def quantize_w(first, rounded):
+            columns = slice(first, first + rounded.shape[1])
+            quantize(w_codes[:, columns], w_plane[:, columns], rounded[:])
 
         def product(acc, lhsT, lhsT_scale, rhs, rhs_scale):
             nc.tensor.matmul_mx(
@@ -138,25 +137,23 @@ def tile_moe_cas_mlp_relu2_kernel(tc, x_words, x_scales, w, w1_words, w1_scales,
             return relu[:, c * CHUNK : (c + 1) * CHUNK, :]
 
         def h_of(c):
-            return h[c // 2][:, (c % 2) * CHUNK : (c % 2 + 1) * CHUNK, :]
+            place = (1, 2, 0, 1)[c]
+            return h[:, place * CHUNK : (place + 1) * CHUNK, :]
 
-        def heavy(bands, first, last, bank):
-            acc = psum.tile([P, len(bands), last - first], F32, name="z_acc", tag=bank)
+        def heavy(bands, u, bank, z, copy, pieces=2):
+            slots = slice(u * HALF, (u + 1) * HALF)
+            acc = psum.tile([P, len(bands), HALF], F32, name="z_acc", tag=bank)
             for column, b in enumerate(bands):
                 product(
                     acc[:, column, :],
                     w2_codes[:, 2 * b * P : 2 * (b + 1) * P].bitcast(FP4X4),
                     w2_plane[:, b * P : (b + 1) * P],
-                    h_codes[:, first:last].bitcast(FP8X4),
-                    h_plane[:, first:last],
+                    h_codes[:, slots].bitcast(FP8X4),
+                    h_plane[:, slots],
                 )
-            return acc
-
-        def heavy_on_vector(b, bank):
-            acc = heavy((b,), 0, S, bank)
-            z = tile("z%d" % b, [P, 1, S], F32)
-            nc.vector.tensor_copy(out=z[:], in_=acc[:])
-            return z[:, 0, :]
+            for first in range(0, 2, 2 // pieces):
+                columns = slice(first, first + 2 // pieces)
+                copy(out=z[:, columns, slots], in_=acc[:, columns, :])
 
         def store(b, queue):
             queue.dma_start(out=out[b * P : (b + 1) * P, :], in_=windows[b][:])
@@ -181,7 +178,7 @@ def tile_moe_cas_mlp_relu2_kernel(tc, x_words, x_scales, w, w1_words, w1_scales,
 
         rounded_early = [round_w("rounded%d" % b, w_early[:, :, b * P : (b + 1) * P]) for b in (0, 1)]
         for b in (0, 1):
-            quantize(w_codes, w_plane, b * P, rounded_early[b])
+            quantize_w(b * P, rounded_early[b])
 
         pairs = tile("relu_pairs", [P, 2, CHUNK, 2], F32)
         hidden(0, words[0], "bank0", pairs[:, 0], (0, 1))
@@ -193,34 +190,37 @@ def tile_moe_cas_mlp_relu2_kernel(tc, x_words, x_scales, w, w1_words, w1_scales,
         nc.vector.tensor_tensor(h_of(0).rearrange("p s (u e) -> p s u e", e=2), by_slot, by_slot, ALU.mult)
         rounded_late = round_w("rounded_late", w_late[:])
         nc.vector.tensor_tensor(h_of(1), relu_of(1), relu_of(1), ALU.mult)
-        quantize(w_codes, w_plane, 2 * P, rounded_late)
-        quantize(h_codes, h_plane, 0, h[0])
+        quantize_w(2 * P, rounded_late)
+        quantize(h_codes[:, :HALF], h_plane[:, :HALF], h[:, CHUNK:, :])
 
+        nc.gpsimd.tensor_tensor(h_of(3), relu_of(3), relu_of(3), ALU.mult)
         nc.scalar.activation(out=h_of(2), in_=relu_of(2), func=ACT.Square)
-        light(0, 0, "bank4", on_scalar)
-        nc.scalar.activation(out=h_of(3), in_=relu_of(3), func=ACT.Square)
-        light(1, 1, "bank7", on_vector)
-        light(0, 1, "bank5", on_scalar)
-        light(1, 0, "bank6", on_scalar)
-        light(2, 0, "bank0", on_vector)
-        light(3, 0, "bank2", on_scalar)
-        quantize(h_codes, h_plane, HALF, h[1])
-
         z01 = tile("z01", [P, 2, S], F32)
-        acc = heavy((0, 1), 0, HALF, "bank4")
-        for b in (0, 1):
-            nc.scalar.copy(out=z01[:, b : b + 1, :HALF], in_=acc[:, b : b + 1, :])
-        light(2, 1, "bank1", on_vector)
-        nc.vector.tensor_copy(out=z01[:, :, HALF:], in_=heavy((0, 1), HALF, S, "bank3")[:])
-        z2 = heavy_on_vector(2, "bank7")
-        z3 = heavy_on_vector(3, "bank5")
-        light(3, 1, "bank0", on_vector)
+        z23 = tile("z23", [P, 2, S], F32)
+        light(0, 0, "bank4", on_scalar)
+        light(2, 0, "bank7", on_vector)
+        light(0, 1, "bank5", on_scalar)
+        light(2, 1, "bank0", on_vector)
+        light(1, 0, "bank6", on_scalar)
+        heavy((2, 3), 0, "bank1", z23, on_vector, pieces=1)
+        light(1, 1, "bank2", on_scalar)
+        light(3, 0, "bank4", on_scalar)
+        heavy((0, 1), 0, "bank3", z01, on_scalar)
 
-        for b, first, last in ((0, 0, HALF), (1, 0, CHUNK), (0, HALF, S), (1, CHUNK, S)):
+        quantize(h_codes[:, HALF:], h_plane[:, HALF:], h[:, :HALF, :])
+        light(3, 1, "bank7", on_vector)
+        heavy((2, 3), 1, "bank5", z23, on_vector, pieces=1)
+        heavy((0, 1), 1, "bank0", z01, on_vector, pieces=1)
+
+        def scatter_on_scalar(b, first, last):
             nc.scalar.activation(windows[b][:].indirect(entries(first, last)), z01[:, b, first:last], ACT.Copy)
-            if (b, last) == (0, S):
-                store(0, nc.scalar)
-        for b, z in ((2, z2), (3, z3)):
-            nc.vector.tensor_copy(windows[b][:].indirect(offsets[:]), z)
+
+        scatter_on_scalar(0, 0, HALF)
+        scatter_on_scalar(1, 0, CHUNK)
+        scatter_on_scalar(0, HALF, S)
+        store(0, nc.scalar)
+        scatter_on_scalar(1, CHUNK, S)
+        for b in (2, 3):
+            nc.vector.tensor_copy(windows[b][:].indirect(offsets[:]), z23[:, b - 2, :])
             store(b, nc.sync)
         store(1, nc.scalar)

@@ -19,6 +19,7 @@ ALU = mybir.AluOpType
 P = 128
 PACK = 4
 BANK = 512
+QUARTER = T // 4
 CHUNK = 128
 CHUNKS = S // CHUNK
 HALF = S // 2
@@ -40,7 +41,6 @@ def tile_moe_cas_mlp_relu2_kernel(tc, x_words, x_scales, w, w1_words, w1_scales,
         offsets = keep.tile([P, S // PER_COLUMN], U16, name="offsets")
         x_codes = tile("x_codes", [P, T], U32)
         x_plane = tile("x_plane", [P, T], U8)
-        x_first_rows = tile("x_first_rows", [P, T], U8)
         w1_raw = tile("w1_raw", [P, 2 * H], U8)
         w1_raw_plane = tile("w1_raw_plane", [P, H], U8)
         w1_codes = [tile("w1_codes%d" % u, [P, H], U8) for u in range(2)]
@@ -58,7 +58,7 @@ def tile_moe_cas_mlp_relu2_kernel(tc, x_words, x_scales, w, w1_words, w1_scales,
         h_codes = tile("h_codes", [P, S], U32)
         h_plane = tile("h_plane", [P, S], U8)
 
-        for plane in (x_plane, w1_raw_plane, w2_plane):
+        for plane in (w1_raw_plane, w2_plane):
             nc.vector.memset(plane[:].bitcast(I32), 0)
 
         def load_bytes(target, source):
@@ -69,9 +69,12 @@ def tile_moe_cas_mlp_relu2_kernel(tc, x_words, x_scales, w, w1_words, w1_scales,
                 load_bytes(plane[32 * q : 32 * q + 4, :], rows[4 * q : 4 * q + 4, :])
 
         w_rows = w.rearrange("(p j) n -> p j n", j=PACK)
-        load_scale_rows(x_first_rows, x_scales[0], (0, 1))
+        for q in range(4):
+            rows = x_scales[0][4 * q : 4 * q + 4, :].bitcast(I32)
+            nc.sync.dma_start(
+                out=x_plane[32 * q : 32 * q + 32, :].bitcast(I32), in_=rows.unsqueeze(0).to_broadcast([8, 4, T // 4])
+            )
         nc.sync.dma_start(offsets[:], offs)
-        load_scale_rows(x_plane, x_scales[0], (2, 3))
         load_bytes(x_codes[:], x_words[0].rearrange("p t d -> p (t d)"))
         load_bytes(w1_raw[:], w1_words[0])
         load_scale_rows(w1_raw_plane, w1_scales[0], range(4))
@@ -108,10 +111,10 @@ def tile_moe_cas_mlp_relu2_kernel(tc, x_words, x_scales, w, w1_words, w1_scales,
                 out=acc, lhsT=lhsT, lhsT_scale=lhsT_scale, rhs=rhs, rhs_scale=rhs_scale, start=True, stop=True
             )
 
-        def light(b, u, bank, copy):
+        def light(b, first, count, bank, copy):
             rows = slice(b * P, (b + 1) * P)
-            tokens = slice(u * BANK, (u + 1) * BANK)
-            acc = psum.tile([P, BANK], F32, name="light_acc", tag=bank)
+            tokens = slice(first, first + count)
+            acc = psum.tile([P, count], F32, name="light_acc", tag=bank)
             product(
                 acc[:],
                 w_codes[:, rows].bitcast(FP8X4),
@@ -158,10 +161,6 @@ def tile_moe_cas_mlp_relu2_kernel(tc, x_words, x_scales, w, w1_words, w1_scales,
         def store(b, queue):
             queue.dma_start(out=out[b * P : (b + 1) * P, :], in_=windows[b][:])
 
-        for q in (0, 1):
-            rows = slice(32 * q, 32 * q + 4)
-            nc.vector.tensor_copy(x_plane[rows, :].bitcast(I32), x_first_rows[rows, :].bitcast(I32))
-
         for u in range(2):
             nc.scalar.copy(
                 out=w1_codes[u][:].bitcast(U16).rearrange("p (t m) -> p t m", t=2),
@@ -197,18 +196,19 @@ def tile_moe_cas_mlp_relu2_kernel(tc, x_words, x_scales, w, w1_words, w1_scales,
         nc.scalar.activation(out=h_of(2), in_=relu_of(2), func=ACT.Square)
         z01 = tile("z01", [P, 2, S], F32)
         z23 = tile("z23", [P, 2, S], F32)
-        light(0, 0, "bank4", on_scalar)
-        light(2, 0, "bank7", on_vector)
-        light(0, 1, "bank5", on_scalar)
-        light(2, 1, "bank0", on_vector)
-        light(1, 0, "bank6", on_scalar)
-        heavy((2, 3), 0, "bank1", z23, on_vector, pieces=1)
-        light(1, 1, "bank2", on_scalar)
-        light(3, 0, "bank4", on_scalar)
+        light(0, 0, BANK, "bank4", on_scalar)
+        light(1, BANK, BANK, "bank2", on_vector)
+        light(2, 0, BANK, "bank7", on_vector)
+        light(0, BANK, BANK, "bank5", on_scalar)
+        light(2, BANK, BANK, "bank0", on_vector)
+        light(1, 0, BANK, "bank6", on_scalar)
+        light(3, 0, BANK, "bank4", on_scalar)
+        light(3, BANK, QUARTER, "bank7", on_scalar)
         heavy((0, 1), 0, "bank3", z01, on_scalar)
+        heavy((2, 3), 0, "bank1", z23, on_vector, pieces=1)
 
         quantize(h_codes[:, HALF:], h_plane[:, HALF:], h[:, :HALF, :])
-        light(3, 1, "bank7", on_vector)
+        light(3, BANK + QUARTER, QUARTER, "bank2", on_vector)
         heavy((2, 3), 1, "bank5", z23, on_vector, pieces=1)
         heavy((0, 1), 1, "bank0", z01, on_vector, pieces=1)
 

@@ -143,20 +143,18 @@ def tile_moe_cas_mlp_relu2_kernel(tc, x_words, x_scales, w, w1_words, w1_scales,
             place = (1, 2, 0, 1)[c]
             return h[:, place * CHUNK : (place + 1) * CHUNK, :]
 
-        def heavy(bands, u, bank, z, copy, pieces=2):
+        def heavy(bands, u, bank):
             slots = slice(u * HALF, (u + 1) * HALF)
-            acc = psum.tile([P, len(bands), HALF], F32, name="z_acc", tag=bank)
-            for column, b in enumerate(bands):
+            acc = psum.tile([P, BANK], F32, name="z_acc", tag=bank)
+            for place, b in enumerate(bands):
                 product(
-                    acc[:, column, :],
+                    acc[:, place * HALF : (place + 1) * HALF],
                     w2_codes[:, 2 * b * P : 2 * (b + 1) * P].bitcast(FP4X4),
                     w2_plane[:, b * P : (b + 1) * P],
                     h_codes[:, slots].bitcast(FP8X4),
                     h_plane[:, slots],
                 )
-            for first in range(0, 2, 2 // pieces):
-                columns = slice(first, first + 2 // pieces)
-                copy(out=z[:, columns, slots], in_=acc[:, columns, :])
+            return acc
 
         def store(b, queue):
             queue.dma_start(out=out[b * P : (b + 1) * P, :], in_=windows[b][:])
@@ -194,7 +192,7 @@ def tile_moe_cas_mlp_relu2_kernel(tc, x_words, x_scales, w, w1_words, w1_scales,
 
         nc.gpsimd.tensor_tensor(h_of(3), relu_of(3), relu_of(3), ALU.mult)
         nc.scalar.activation(out=h_of(2), in_=relu_of(2), func=ACT.Square)
-        z01 = tile("z01", [P, 2, S], F32)
+        z01 = tile("z01", [P, 2 * S], F32)
         z23 = tile("z23", [P, 2, S], F32)
         light(0, 0, BANK, "bank4", on_scalar)
         light(1, BANK, BANK, "bank2", on_vector)
@@ -204,22 +202,26 @@ def tile_moe_cas_mlp_relu2_kernel(tc, x_words, x_scales, w, w1_words, w1_scales,
         light(1, 0, BANK, "bank6", on_scalar)
         light(3, 0, BANK, "bank4", on_scalar)
         light(3, BANK, QUARTER, "bank7", on_scalar)
-        heavy((0, 1), 0, "bank3", z01, on_scalar)
-        heavy((2, 3), 0, "bank1", z23, on_vector, pieces=1)
+        acc = heavy((0, 1), 0, "bank3")
+        for first in (0, HALF):
+            on_scalar(out=z01[:, first : first + HALF], in_=acc[:, first : first + HALF])
+        on_vector(out=z23[:, :, :HALF], in_=heavy((2, 3), 0, "bank1")[:].rearrange("p (b s) -> p b s", b=2))
 
         quantize(h_codes[:, HALF:], h_plane[:, HALF:], h[:, :HALF, :])
         light(3, BANK + QUARTER, QUARTER, "bank2", on_vector)
-        heavy((2, 3), 1, "bank5", z23, on_vector, pieces=1)
-        heavy((0, 1), 1, "bank0", z01, on_vector, pieces=1)
+        on_vector(out=z23[:, :, HALF:], in_=heavy((2, 3), 1, "bank5")[:].rearrange("p (b s) -> p b s", b=2))
+        acc = heavy((1, 0), 1, "bank0")
+        on_vector(out=z01[:, S + CHUNK :], in_=acc[:, CHUNK:])
 
-        def scatter_on_scalar(b, first, last):
-            nc.scalar.activation(windows[b][:].indirect(entries(first, last)), z01[:, b, first:last], ACT.Copy)
+        def scatter_on_scalar(b, first, last, place):
+            nc.scalar.activation(windows[b][:].indirect(entries(first, last)), z01[:, place : place + last - first], ACT.Copy)
 
-        scatter_on_scalar(0, 0, HALF)
-        scatter_on_scalar(1, 0, CHUNK)
-        scatter_on_scalar(0, HALF, S)
+        scatter_on_scalar(0, 0, HALF, 0)
+        scatter_on_scalar(1, 0, CHUNK, HALF)
+        on_scalar(out=z01[:, S : S + CHUNK], in_=acc[:, :CHUNK])
+        scatter_on_scalar(0, HALF, S, S + HALF)
         store(0, nc.scalar)
-        scatter_on_scalar(1, CHUNK, S)
+        scatter_on_scalar(1, CHUNK, S, HALF + CHUNK)
         for b in (2, 3):
             nc.vector.tensor_copy(windows[b][:].indirect(offsets[:]), z23[:, b - 2, :])
             store(b, nc.sync)

@@ -25,6 +25,7 @@ CHUNKS = S // CHUNK
 HALF = S // 2
 BANDS = N // P
 PER_COLUMN = 16
+SHARE = 64
 RUN = 4
 
 
@@ -54,19 +55,19 @@ def tile_moe_cas_mlp_relu2_kernel(tc, x_words, x_scales, w, w1_words, w1_scales,
         windows = [tile("window%d" % b, [P, T], F32) for b in range(BANDS)]
         slot_plane = tile("slot_plane", [P, S], U8)
         relu = tile("relu", [P, S, PACK], F32)
-        h = tile("h", [P, 3 * CHUNK, PACK], BF16)
-        h_codes = tile("h_codes", [P, S], U32)
-        h_plane = tile("h_plane", [P, S], U8)
+        h = tile("h", [P, SHARE + HALF, PACK], BF16)
+        h_codes = tile("h_codes", [P, HALF], U32)
+        h_plane = tile("h_plane", [P, HALF], U8)
 
         for plane in (w1_raw_plane, w2_plane):
             nc.vector.memset(plane[:].bitcast(I32), 0)
 
-        def load_bytes(target, source):
-            nc.sync.dma_start(out=target.bitcast(I32), in_=source.bitcast(I32))
+        def load_bytes(target, source, queue=nc.sync):
+            queue.dma_start(out=target.bitcast(I32), in_=source.bitcast(I32))
 
-        def load_scale_rows(plane, rows, quadrants):
-            for q in quadrants:
-                load_bytes(plane[32 * q : 32 * q + 4, :], rows[4 * q : 4 * q + 4, :])
+        def load_scale_rows(plane, rows, queue):
+            for q in range(4):
+                load_bytes(plane[32 * q : 32 * q + 4, :], rows[4 * q : 4 * q + 4, :], queue)
 
         w_rows = w.rearrange("(p j) n -> p j n", j=PACK)
         for q in range(4):
@@ -77,11 +78,11 @@ def tile_moe_cas_mlp_relu2_kernel(tc, x_words, x_scales, w, w1_words, w1_scales,
         nc.sync.dma_start(offsets[:], offs)
         load_bytes(x_codes[:], x_words[0].rearrange("p t d -> p (t d)"))
         load_bytes(w1_raw[:], w1_words[0])
-        load_scale_rows(w1_raw_plane, w1_scales[0], range(4))
+        load_scale_rows(w1_raw_plane, w1_scales[0], nc.sync)
         nc.sync.dma_start(out=w_early[:], in_=w_rows[:, :, : 2 * P])
         nc.sync.dma_start(out=w_late[:], in_=w_rows[:, :, 2 * P :])
         load_bytes(w2_codes[:], w2_words[0])
-        load_scale_rows(w2_plane, w2_scales[0], range(4))
+        load_scale_rows(w2_plane, w2_scales[0], nc.gpsimd)
 
         def entries(first, last):
             return offsets[:, first // PER_COLUMN : last // PER_COLUMN]
@@ -139,20 +140,16 @@ def tile_moe_cas_mlp_relu2_kernel(tc, x_words, x_scales, w, w1_words, w1_scales,
         def relu_of(c):
             return relu[:, c * CHUNK : (c + 1) * CHUNK, :]
 
-        def h_of(c):
-            place = (1, 2, 0, 1)[c]
-            return h[:, place * CHUNK : (place + 1) * CHUNK, :]
 
-        def heavy(bands, u, bank):
-            slots = slice(u * HALF, (u + 1) * HALF)
+        def heavy(bands, bank):
             acc = psum.tile([P, BANK], F32, name="z_acc", tag=bank)
             for place, b in enumerate(bands):
                 product(
                     acc[:, place * HALF : (place + 1) * HALF],
                     w2_codes[:, 2 * b * P : 2 * (b + 1) * P].bitcast(FP4X4),
                     w2_plane[:, b * P : (b + 1) * P],
-                    h_codes[:, slots].bitcast(FP8X4),
-                    h_plane[:, slots],
+                    h_codes[:].bitcast(FP8X4),
+                    h_plane[:],
                 )
             return acc
 
@@ -184,45 +181,54 @@ def tile_moe_cas_mlp_relu2_kernel(tc, x_words, x_scales, w, w1_words, w1_scales,
             hidden(c, words[c], "bank%d" % c, relu_of(c))
 
         by_slot = pairs[:].rearrange("p u s e -> p s u e")
-        nc.vector.tensor_tensor(h_of(0).rearrange("p s (u e) -> p s u e", e=2), by_slot, by_slot, ALU.mult)
+        nc.vector.tensor_tensor(h[:, SHARE : SHARE + CHUNK, :].rearrange("p s (u e) -> p s u e", e=2), by_slot, by_slot, ALU.mult)
         rounded_late = round_w("rounded_late", w_late[:])
-        nc.vector.tensor_tensor(h_of(1), relu_of(1), relu_of(1), ALU.mult)
+        nc.vector.tensor_tensor(h[:, SHARE + CHUNK :, :], relu_of(1), relu_of(1), ALU.mult)
         quantize_w(2 * P, rounded_late)
-        quantize(h_codes[:, :HALF], h_plane[:, :HALF], h[:, CHUNK:, :])
+        quantize(h_codes[:], h_plane[:], h[:, SHARE:, :])
+        late = relu[:, HALF + SHARE :, :]
+        nc.gpsimd.tensor_tensor(h[:, SHARE:HALF, :], late, late, ALU.mult)
+        nc.scalar.activation(out=h[:, :SHARE, :], in_=relu[:, HALF : HALF + SHARE, :], func=ACT.Square)
 
-        nc.gpsimd.tensor_tensor(h_of(3), relu_of(3), relu_of(3), ALU.mult)
-        nc.scalar.activation(out=h_of(2), in_=relu_of(2), func=ACT.Square)
-        z01 = tile("z01", [P, 2 * S], F32)
-        z23 = tile("z23", [P, 2, S], F32)
-        light(0, 0, BANK, "bank4", on_scalar)
-        light(1, BANK, BANK, "bank2", on_vector)
-        light(2, 0, BANK, "bank7", on_vector)
-        light(0, BANK, BANK, "bank5", on_scalar)
-        light(2, BANK, BANK, "bank0", on_vector)
-        light(1, 0, BANK, "bank6", on_scalar)
-        light(3, 0, BANK, "bank4", on_scalar)
-        light(3, BANK, QUARTER, "bank7", on_scalar)
-        acc = heavy((0, 1), 0, "bank3")
-        for first in (0, HALF):
-            on_scalar(out=z01[:, first : first + HALF], in_=acc[:, first : first + HALF])
-        on_vector(out=z23[:, :, :HALF], in_=heavy((2, 3), 0, "bank1")[:].rearrange("p (b s) -> p b s", b=2))
+        z = [tile("z%d" % b, [P, S], F32) for b in range(BANDS)]
 
-        quantize(h_codes[:, HALF:], h_plane[:, HALF:], h[:, :HALF, :])
-        light(3, BANK + QUARTER, QUARTER, "bank2", on_vector)
-        on_vector(out=z23[:, :, HALF:], in_=heavy((2, 3), 1, "bank5")[:].rearrange("p (b s) -> p b s", b=2))
-        acc = heavy((1, 0), 1, "bank0")
-        on_vector(out=z01[:, S + CHUNK :], in_=acc[:, CHUNK:])
+        def take_z(acc, place, b, u, copy):
+            copy(out=z[b][:, u * HALF : (u + 1) * HALF], in_=acc[:, place * HALF : (place + 1) * HALF])
 
-        def scatter_on_scalar(b, first, last, place):
-            nc.scalar.activation(windows[b][:].indirect(entries(first, last)), z01[:, place : place + last - first], ACT.Copy)
+        def scatter_on_scalar(b, first, last):
+            nc.scalar.activation(windows[b][:].indirect(entries(first, last)), z[b][:, first:last], ACT.Copy)
 
-        scatter_on_scalar(0, 0, HALF, 0)
-        scatter_on_scalar(1, 0, CHUNK, HALF)
-        on_scalar(out=z01[:, S : S + CHUNK], in_=acc[:, :CHUNK])
-        scatter_on_scalar(0, HALF, S, S + HALF)
+        def scatter_on_vector(b, first, last):
+            nc.vector.tensor_copy(windows[b][:].indirect(entries(first, last)), z[b][:, first:last])
+
+        light(0, 0, BANK, "bank5", on_scalar)
+        light(1, 0, BANK, "bank6", on_vector)
+        light(0, BANK, BANK, "bank7", on_scalar)
+        light(2, 0, BANK, "bank0", on_vector)
+        acc = heavy((0, 1), "bank4")
+        take_z(acc, 0, 0, 0, on_scalar)
+        take_z(acc, 1, 1, 0, on_scalar)
+        acc = heavy((2, 3), "bank1")
+        take_z(acc, 0, 2, 0, on_vector)
+        take_z(acc, 1, 3, 0, on_vector)
+        light(2, BANK, BANK, "bank6", on_vector)
+        scatter_on_scalar(0, 0, HALF)
+        quantize(h_codes[:], h_plane[:], h[:, :HALF, :])
+        light(1, BANK, BANK, "bank0", on_scalar)
+        light(3, 0, QUARTER, "bank4", on_scalar)
+        light(3, BANK, BANK, "bank1", on_vector)
+        light(3, QUARTER, QUARTER, "bank6", on_vector)
+        scatter_on_scalar(1, 0, CHUNK)
+        acc = heavy((2, 3), "bank5")
+        take_z(acc, 0, 2, 1, on_vector)
+        take_z(acc, 1, 3, 1, on_vector)
+        acc = heavy((0, 1), "bank2")
+        take_z(acc, 0, 0, 1, on_scalar)
+        take_z(acc, 1, 1, 1, on_scalar)
+        scatter_on_scalar(0, HALF, S)
         store(0, nc.scalar)
-        scatter_on_scalar(1, CHUNK, S, HALF + CHUNK)
+        scatter_on_scalar(1, CHUNK, S)
         for b in (2, 3):
-            nc.vector.tensor_copy(windows[b][:].indirect(offsets[:]), z23[:, b - 2, :])
+            scatter_on_vector(b, 0, S)
             store(b, nc.sync)
         store(1, nc.scalar)

@@ -47,7 +47,6 @@ def tile_moe_cas_mlp_relu2_kernel(tc, x_words, x_scales, w, w1_words, w1_scales,
         w1_codes = [tile("w1_codes%d" % u, [P, H], U8) for u in range(2)]
         w1_plane = tile("w1_plane", [P, H], U8)
         w2_codes = tile("w2_codes", [P, 2 * N], U8)
-        w2_plane = tile("w2_plane", [P, N], U8)
         w_early = tile("w_early", [P, PACK, 2 * P], F32)
         w_late = tile("w_late", [P, PACK, 2 * P], F32)
         w_codes = tile("w_codes", [P, N], U32)
@@ -59,14 +58,13 @@ def tile_moe_cas_mlp_relu2_kernel(tc, x_words, x_scales, w, w1_words, w1_scales,
         h_codes = tile("h_codes", [P, HALF], U32)
         h_plane = tile("h_plane", [P, HALF], U8)
 
-        for plane in (w1_raw_plane, w2_plane):
-            nc.vector.memset(plane[:].bitcast(I32), 0)
+        nc.vector.memset(w1_raw_plane[:].bitcast(I32), 0)
 
         def load_bytes(target, source, queue=nc.sync):
             queue.dma_start(out=target.bitcast(I32), in_=source.bitcast(I32))
 
-        def load_scale_rows(plane, rows, queue):
-            for q in range(4):
+        def load_scale_rows(plane, rows, queues):
+            for q, queue in enumerate(queues):
                 load_bytes(plane[32 * q : 32 * q + 4, :], rows[4 * q : 4 * q + 4, :], queue)
 
         w_rows = w.rearrange("(p j) n -> p j n", j=PACK)
@@ -78,11 +76,10 @@ def tile_moe_cas_mlp_relu2_kernel(tc, x_words, x_scales, w, w1_words, w1_scales,
         nc.sync.dma_start(offsets[:], offs)
         load_bytes(x_codes[:], x_words[0].rearrange("p t d -> p (t d)"))
         load_bytes(w1_raw[:], w1_words[0])
-        load_scale_rows(w1_raw_plane, w1_scales[0], nc.sync)
+        load_scale_rows(w1_raw_plane, w1_scales[0], [nc.sync] * 4)
         nc.sync.dma_start(out=w_early[:], in_=w_rows[:, :, : 2 * P])
         nc.sync.dma_start(out=w_late[:], in_=w_rows[:, :, 2 * P :])
         load_bytes(w2_codes[:], w2_words[0])
-        load_scale_rows(w2_plane, w2_scales[0], nc.gpsimd)
 
         def entries(first, last):
             return offsets[:, first // PER_COLUMN : last // PER_COLUMN]
@@ -168,6 +165,8 @@ def tile_moe_cas_mlp_relu2_kernel(tc, x_words, x_scales, w, w1_words, w1_scales,
                 out=w1_plane[:].rearrange("p (t m) -> p t m", t=PACK)[:, 2 * u : 2 * u + 2, :],
                 in_=w1_raw_plane[:].rearrange("p (m t) -> p t m", t=PACK)[:, 2 * u : 2 * u + 2, :],
             )
+        w2_plane = w1_raw_plane
+        load_scale_rows(w2_plane, w2_scales[0], [nc.scalar, nc.scalar, nc.sync, nc.sync])
         words = words + gather_words("later_words", HALF, tag="w1_raw")
 
         rounded_early = [round_w("rounded%d" % b, w_early[:, :, b * P : (b + 1) * P]) for b in (0, 1)]

@@ -165,9 +165,9 @@ def tile_moe_cas_mlp_relu2_kernel(tc, x_words, x_scales, w, w1_words, w1_scales,
                 out=w1_plane[:].rearrange("p (t m) -> p t m", t=PACK)[:, 2 * u : 2 * u + 2, :],
                 in_=w1_raw_plane[:].rearrange("p (m t) -> p t m", t=PACK)[:, 2 * u : 2 * u + 2, :],
             )
-        w2_plane = w1_raw_plane
+        w2_plane = w1_raw[:, :N]
         load_scale_rows(w2_plane, w2_scales[0], [nc.scalar, nc.scalar, nc.sync, nc.sync])
-        words = words + gather_words("later_words", HALF, tag="w1_raw")
+        words = words + gather_words("later_words", HALF, tag="w1_raw_plane")
 
         rounded_early = [round_w("rounded%d" % b, w_early[:, :, b * P : (b + 1) * P]) for b in (0, 1)]
         for b in (0, 1):
@@ -203,19 +203,19 @@ def tile_moe_cas_mlp_relu2_kernel(tc, x_words, x_scales, w, w1_words, w1_scales,
         light(0, 0, BANK, "bank5", on_scalar)
         light(1, 0, BANK, "bank6", on_vector)
         light(0, BANK, BANK, "bank7", on_scalar)
-        light(2, 0, BANK, "bank0", on_vector)
-        acc = heavy((0, 1), "bank4")
-        take_z(acc, 0, 0, 0, on_scalar)
-        take_z(acc, 1, 1, 0, on_scalar)
+        light(1, BANK, BANK, "bank0", on_vector)
+        light(2, 0, BANK, "bank3", on_scalar)
         acc = heavy((2, 3), "bank1")
         take_z(acc, 0, 2, 0, on_vector)
         take_z(acc, 1, 3, 0, on_vector)
+        acc = heavy((0, 1), "bank4")
+        take_z(acc, 0, 0, 0, on_scalar)
+        take_z(acc, 1, 1, 0, on_scalar)
         light(2, BANK, BANK, "bank6", on_vector)
         scatter_on_scalar(0, 0, HALF)
         quantize(h_codes[:], h_plane[:], h[:, :HALF, :])
-        light(1, BANK, BANK, "bank0", on_scalar)
         light(3, 0, QUARTER, "bank4", on_scalar)
-        light(3, BANK, BANK, "bank1", on_vector)
+        light(3, BANK, BANK, "bank3", on_vector)
         light(3, QUARTER, QUARTER, "bank6", on_vector)
         scatter_on_scalar(1, 0, CHUNK)
         acc = heavy((2, 3), "bank5")

@@ -26,6 +26,7 @@ HALF = S // 2
 BANDS = N // P
 PER_COLUMN = 16
 SHARE = 64
+HELP = 64
 RUN = 4
 
 
@@ -176,13 +177,16 @@ def tile_moe_cas_mlp_relu2_kernel(tc, x_words, x_scales, w, w1_words, w1_scales,
         pairs = tile("relu_pairs", [P, 2, CHUNK, 2], F32)
         hidden(0, words[0], "bank0", pairs[:, 0], (0, 1))
         hidden(0, words[0], "bank4", pairs[:, 1], (2, 3))
-        for c in range(1, CHUNKS):
+        hidden(1, words[1], "bank1", relu_of(1))
+        nc.scalar.activation(out=h[:, SHARE + HALF - HELP :, :], in_=relu[:, HALF - HELP : HALF, :], func=ACT.Square)
+        for c in range(2, CHUNKS):
             hidden(c, words[c], "bank%d" % c, relu_of(c))
 
         by_slot = pairs[:].rearrange("p u s e -> p s u e")
         nc.vector.tensor_tensor(h[:, SHARE : SHARE + CHUNK, :].rearrange("p s (u e) -> p s u e", e=2), by_slot, by_slot, ALU.mult)
         rounded_late = round_w("rounded_late", w_late[:])
-        nc.vector.tensor_tensor(h[:, SHARE + CHUNK :, :], relu_of(1), relu_of(1), ALU.mult)
+        rest = relu[:, CHUNK : HALF - HELP, :]
+        nc.vector.tensor_tensor(h[:, SHARE + CHUNK : SHARE + HALF - HELP, :], rest, rest, ALU.mult)
         quantize_w(2 * P, rounded_late)
         quantize(h_codes[:], h_plane[:], h[:, SHARE:, :])
         late = relu[:, HALF + SHARE :, :]

@@ -25,7 +25,7 @@ CHUNKS = S // CHUNK
 HALF = S // 2
 BANDS = N // P
 PER_COLUMN = 16
-SHARE = 64
+SHARE = 0
 HELP = 64
 RUN = 4
 
@@ -114,13 +114,18 @@ def tile_moe_cas_mlp_relu2_kernel(tc, x_words, x_scales, w, w1_words, w1_scales,
             rows = slice(b * P, (b + 1) * P)
             tokens = slice(first, first + count)
             acc = psum.tile([P, count], F32, name="light_acc", tag=bank)
-            product(
-                acc[:],
-                w_codes[:, rows].bitcast(FP8X4),
-                w_plane[:, rows],
-                x_codes[:, tokens].bitcast(FP8X4),
-                x_plane[:, tokens],
-            )
+            done = 0
+            for width in (BANK, QUARTER, CHUNK):
+                if count & width:
+                    part = slice(first + done, first + done + width)
+                    product(
+                        acc[:, done : done + width],
+                        w_codes[:, rows].bitcast(FP8X4),
+                        w_plane[:, rows],
+                        x_codes[:, part].bitcast(FP8X4),
+                        x_plane[:, part],
+                    )
+                    done = done + width
             copy(out=windows[b][:, tokens], in_=acc[:])
 
         def hidden(c, words, bank, target, ts=range(PACK)):
@@ -191,7 +196,6 @@ def tile_moe_cas_mlp_relu2_kernel(tc, x_words, x_scales, w, w1_words, w1_scales,
         quantize(h_codes[:], h_plane[:], h[:, SHARE:, :])
         late = relu[:, HALF + SHARE :, :]
         nc.gpsimd.tensor_tensor(h[:, SHARE:HALF, :], late, late, ALU.mult)
-        nc.scalar.activation(out=h[:, :SHARE, :], in_=relu[:, HALF : HALF + SHARE, :], func=ACT.Square)
 
         z = [tile("z%d" % b, [P, S], F32) for b in range(BANDS)]
 
@@ -216,11 +220,12 @@ def tile_moe_cas_mlp_relu2_kernel(tc, x_words, x_scales, w, w1_words, w1_scales,
         take_z(acc, 0, 0, 0, on_scalar)
         take_z(acc, 1, 1, 0, on_scalar)
         light(2, BANK, BANK, "bank6", on_vector)
+        light(3, BANK, BANK, "bank0", on_vector)
+        light(3, BANK - CHUNK, CHUNK, "bank1", on_vector)
         scatter_on_scalar(0, 0, HALF)
         quantize(h_codes[:], h_plane[:], h[:, :HALF, :])
-        light(3, 0, QUARTER, "bank4", on_scalar)
-        light(3, BANK, BANK, "bank3", on_vector)
-        light(3, QUARTER, QUARTER, "bank6", on_vector)
+        light(3, 0, BANK - CHUNK, "bank4", on_scalar)
+        scatter_on_vector(2, 0, CHUNK)
         scatter_on_scalar(1, 0, CHUNK)
         acc = heavy((2, 3), "bank5")
         take_z(acc, 0, 2, 1, on_vector)
@@ -231,7 +236,7 @@ def tile_moe_cas_mlp_relu2_kernel(tc, x_words, x_scales, w, w1_words, w1_scales,
         scatter_on_scalar(0, HALF, S)
         store(0, nc.scalar)
         scatter_on_scalar(1, CHUNK, S)
-        for b in (2, 3):
-            scatter_on_vector(b, 0, S)
+        for b, first in ((2, CHUNK), (3, 0)):
+            scatter_on_vector(b, first, S)
             store(b, nc.sync)
         store(1, nc.scalar)

@@ -213,24 +213,24 @@ def tile_moe_cas_mlp_relu2_kernel(tc, x_words, x_scales, w, w1_words, w1_scales,
         light(0, BANK, BANK, "bank7", on_scalar)
         light(1, BANK, BANK, "bank0", on_vector)
         light(2, 0, BANK, "bank3", on_scalar)
-        acc = heavy((2, 3), "bank1")
-        take_z(acc, 0, 2, 0, on_vector)
-        take_z(acc, 1, 3, 0, on_vector)
+        light(2, BANK, BANK, "bank2", on_vector)
         acc = heavy((0, 1), "bank4")
         take_z(acc, 0, 0, 0, on_scalar)
         take_z(acc, 1, 1, 0, on_scalar)
-        light(2, BANK, BANK, "bank6", on_vector)
-        light(3, BANK, BANK, "bank0", on_vector)
-        light(3, BANK - CHUNK, CHUNK, "bank1", on_vector)
+        acc = heavy((2, 3), "bank1")
+        take_z(acc, 0, 2, 0, on_vector)
+        take_z(acc, 1, 3, 0, on_vector)
         scatter_on_scalar(0, 0, HALF)
+        scatter_on_vector(2, 0, CHUNK)
         quantize(h_codes[:], h_plane[:], h[:, :HALF, :])
         light(3, 0, BANK - CHUNK, "bank4", on_scalar)
-        scatter_on_vector(2, 0, CHUNK)
+        light(3, BANK, BANK, "bank1", on_vector)
+        light(3, BANK - CHUNK, CHUNK, "bank2", on_vector)
         scatter_on_scalar(1, 0, CHUNK)
         acc = heavy((2, 3), "bank5")
         take_z(acc, 0, 2, 1, on_vector)
         take_z(acc, 1, 3, 1, on_vector)
-        acc = heavy((0, 1), "bank2")
+        acc = heavy((0, 1), "bank7")
         take_z(acc, 0, 0, 1, on_scalar)
         take_z(acc, 1, 1, 1, on_scalar)
         scatter_on_scalar(0, HALF, S)

@@ -19,14 +19,13 @@ ALU = mybir.AluOpType
 P = 128
 PACK = 4
 BANK = 512
-QUARTER = T // 4
 CHUNK = 128
-CHUNKS = S // CHUNK
 HALF = S // 2
 BANDS = N // P
 PER_COLUMN = 16
-SHARE = 0
-HELP = 64
+HELP = CHUNK // 2
+SPLIT = BANK - CHUNK
+WIDTHS = (512, 256, 128)
 RUN = 4
 
 
@@ -54,8 +53,8 @@ def tile_moe_cas_mlp_relu2_kernel(tc, x_words, x_scales, w, w1_words, w1_scales,
         w_plane = tile("w_plane", [P, N], U8)
         windows = [tile("window%d" % b, [P, T], F32) for b in range(BANDS)]
         slot_plane = tile("slot_plane", [P, S], U8)
-        relu = tile("relu", [P, S, PACK], F32)
-        h = tile("h", [P, SHARE + HALF, PACK], BF16)
+        relu = tile("relu", [P, CHUNK, PACK], F32)
+        h = tile("h", [P, HALF, PACK], BF16)
         h_codes = tile("h_codes", [P, HALF], U32)
         h_plane = tile("h_plane", [P, HALF], U8)
 
@@ -88,7 +87,7 @@ def tile_moe_cas_mlp_relu2_kernel(tc, x_words, x_scales, w, w1_words, w1_scales,
         def gather_words(name, first, **place):
             gathered = tile(name, [P, HALF], U32, **place)
             nc.vector.tensor_copy(gathered[:], x_codes[:].indirect(entries(first, first + HALF)))
-            return [gathered[:, :CHUNK], gathered[:, CHUNK:]]
+            return gathered
 
         def round_w(name, raw):
             rounded = tile(name, [P, raw.shape[2], PACK], BF16)
@@ -115,8 +114,8 @@ def tile_moe_cas_mlp_relu2_kernel(tc, x_words, x_scales, w, w1_words, w1_scales,
             tokens = slice(first, first + count)
             acc = psum.tile([P, count], F32, name="light_acc", tag=bank)
             done = 0
-            for width in (BANK, QUARTER, CHUNK):
-                if count & width:
+            for width in WIDTHS:
+                if count - done >= width:
                     part = slice(first + done, first + done + width)
                     product(
                         acc[:, done : done + width],
@@ -128,21 +127,18 @@ def tile_moe_cas_mlp_relu2_kernel(tc, x_words, x_scales, w, w1_words, w1_scales,
                     done = done + width
             copy(out=windows[b][:, tokens], in_=acc[:])
 
-        def hidden(c, words, bank, target, ts=range(PACK)):
-            acc = psum.tile([P, len(ts), CHUNK], F32, name="hidden_acc", tag=bank)
+        def hidden(first, words, bank, target, ts=range(PACK)):
+            count = words.shape[1]
+            acc = psum.tile([P, len(ts), count], F32, name="hidden_acc", tag=bank)
             for column, t in enumerate(ts):
                 product(
                     acc[:, column, :],
                     w1_codes[t // 2][:, 2 * (t % 2) * P : 2 * (t % 2 + 1) * P].bitcast(FP4X4),
                     w1_plane[:, t * P : (t + 1) * P],
                     words.bitcast(FP8X4),
-                    slot_plane[:, c * CHUNK : (c + 1) * CHUNK],
+                    slot_plane[:, first : first + count],
                 )
             nc.scalar.activation(out=target, in_=acc[:].rearrange("p t s -> p s t"), func=ACT.Relu)
-
-        def relu_of(c):
-            return relu[:, c * CHUNK : (c + 1) * CHUNK, :]
-
 
         def heavy(bands, bank):
             acc = psum.tile([P, BANK], F32, name="z_acc", tag=bank)
@@ -166,41 +162,44 @@ def tile_moe_cas_mlp_relu2_kernel(tc, x_words, x_scales, w, w1_words, w1_scales,
             )
         nc.vector.tensor_copy(slot_plane[:], x_plane[:].indirect(offsets[:]))
         words = gather_words("first_words", 0)
-        for u in range(2):
+        for first, last in ((0, 1), (1, 2), (2, PACK)):
             nc.vector.tensor_copy(
-                out=w1_plane[:].rearrange("p (t m) -> p t m", t=PACK)[:, 2 * u : 2 * u + 2, :],
-                in_=w1_raw_plane[:].rearrange("p (m t) -> p t m", t=PACK)[:, 2 * u : 2 * u + 2, :],
+                out=w1_plane[:].rearrange("p (t m) -> p t m", t=PACK)[:, first:last, :],
+                in_=w1_raw_plane[:].rearrange("p (m t) -> p t m", t=PACK)[:, first:last, :],
             )
         w2_plane = w1_raw[:, :N]
         load_scale_rows(w2_plane, w2_scales[0], [nc.scalar, nc.scalar, nc.sync, nc.sync])
-        words = words + gather_words("later_words", HALF, tag="w1_raw_plane")
+        later_words = gather_words("later_words", HALF, tag="w1_raw_plane")
 
         rounded_early = [round_w("rounded%d" % b, w_early[:, :, b * P : (b + 1) * P]) for b in (0, 1)]
         for b in (0, 1):
             quantize_w(b * P, rounded_early[b])
 
         pairs = tile("relu_pairs", [P, 2, CHUNK, 2], F32)
-        hidden(0, words[0], "bank0", pairs[:, 0], (0, 1))
-        hidden(0, words[0], "bank4", pairs[:, 1], (2, 3))
-        hidden(1, words[1], "bank1", relu_of(1))
-        nc.scalar.activation(out=h[:, SHARE + HALF - HELP :, :], in_=relu[:, HALF - HELP : HALF, :], func=ACT.Square)
-        for c in range(2, CHUNKS):
-            hidden(c, words[c], "bank%d" % c, relu_of(c))
+        hidden(0, words[:, :CHUNK], "bank0", pairs[:, 0], (0, 1))
+        hidden(0, words[:, :CHUNK], "bank4", pairs[:, 1], (2, 3))
+        hidden(CHUNK, words[:, CHUNK:], "bank1", relu[:])
+        nc.scalar.activation(out=h[:, HALF - HELP :, :], in_=relu[:, CHUNK - HELP :, :], func=ACT.Square)
+        later_pairs = tile("later_pairs", [P, 2, HALF, 2], F32)
+        hidden(HALF, later_words[:], "bank2", later_pairs[:, 0], (0, 1))
+        hidden(HALF, later_words[:], "bank3", later_pairs[:, 1], (2, 3))
 
         by_slot = pairs[:].rearrange("p u s e -> p s u e")
-        nc.vector.tensor_tensor(h[:, SHARE : SHARE + CHUNK, :].rearrange("p s (u e) -> p s u e", e=2), by_slot, by_slot, ALU.mult)
+        nc.vector.tensor_tensor(h[:, :CHUNK, :].rearrange("p s (u e) -> p s u e", e=2), by_slot, by_slot, ALU.mult)
         rounded_late = round_w("rounded_late", w_late[:])
-        rest = relu[:, CHUNK : HALF - HELP, :]
-        nc.vector.tensor_tensor(h[:, SHARE + CHUNK : SHARE + HALF - HELP, :], rest, rest, ALU.mult)
+        rest = relu[:, : CHUNK - HELP, :]
+        nc.vector.tensor_tensor(h[:, CHUNK : HALF - HELP, :], rest, rest, ALU.mult)
         quantize_w(2 * P, rounded_late)
-        quantize(h_codes[:], h_plane[:], h[:, SHARE:, :])
-        late = relu[:, HALF + SHARE :, :]
-        nc.gpsimd.tensor_tensor(h[:, SHARE:HALF, :], late, late, ALU.mult)
+        quantize(h_codes[:], h_plane[:], h[:])
+        late = later_pairs[:].rearrange("p u s e -> p s u e")
+        nc.gpsimd.tensor_tensor(h[:].rearrange("p s (u e) -> p s u e", e=2), late, late, ALU.mult)
 
         z = [tile("z%d" % b, [P, S], F32) for b in range(BANDS)]
 
-        def take_z(acc, place, b, u, copy):
-            copy(out=z[b][:, u * HALF : (u + 1) * HALF], in_=acc[:, place * HALF : (place + 1) * HALF])
+        def take_z(bands, u, bank, copy):
+            acc = heavy(bands, bank)
+            for place, b in enumerate(bands):
+                copy(out=z[b][:, u * HALF : (u + 1) * HALF], in_=acc[:, place * HALF : (place + 1) * HALF])
 
         def scatter_on_scalar(b, first, last):
             nc.scalar.activation(windows[b][:].indirect(entries(first, last)), z[b][:, first:last], ACT.Copy)
@@ -214,25 +213,19 @@ def tile_moe_cas_mlp_relu2_kernel(tc, x_words, x_scales, w, w1_words, w1_scales,
         light(1, BANK, BANK, "bank0", on_vector)
         light(2, 0, BANK, "bank3", on_scalar)
         light(2, BANK, BANK, "bank2", on_vector)
-        acc = heavy((0, 1), "bank4")
-        take_z(acc, 0, 0, 0, on_scalar)
-        take_z(acc, 1, 1, 0, on_scalar)
-        acc = heavy((2, 3), "bank1")
-        take_z(acc, 0, 2, 0, on_vector)
-        take_z(acc, 1, 3, 0, on_vector)
+        take_z((0, 1), 0, "bank4", on_scalar)
+        take_z((2, 3), 0, "bank1", on_vector)
         scatter_on_scalar(0, 0, HALF)
         scatter_on_vector(2, 0, CHUNK)
-        quantize(h_codes[:], h_plane[:], h[:, :HALF, :])
-        light(3, 0, BANK - CHUNK, "bank4", on_scalar)
+
+        quantize(h_codes[:], h_plane[:], h[:])
+        light(3, 0, SPLIT, "bank4", on_scalar)
         light(3, BANK, BANK, "bank1", on_vector)
-        light(3, BANK - CHUNK, CHUNK, "bank2", on_vector)
+        light(3, SPLIT, BANK - SPLIT, "bank2", on_vector)
         scatter_on_scalar(1, 0, CHUNK)
-        acc = heavy((2, 3), "bank5")
-        take_z(acc, 0, 2, 1, on_vector)
-        take_z(acc, 1, 3, 1, on_vector)
-        acc = heavy((0, 1), "bank7")
-        take_z(acc, 0, 0, 1, on_scalar)
-        take_z(acc, 1, 1, 1, on_scalar)
+        take_z((2, 3), 1, "bank5", on_vector)
+        take_z((0, 1), 1, "bank7", on_scalar)
+
         scatter_on_scalar(0, HALF, S)
         store(0, nc.scalar)
         scatter_on_scalar(1, CHUNK, S)

@@ -70,7 +70,7 @@ def tile_moe_cas_mlp_relu2_kernel(tc, x_words, x_scales, w, w1_words, w1_scales,
         w_rows = w.rearrange("(p j) n -> p j n", j=PACK)
         for q in range(4):
             rows = x_scales[0][4 * q : 4 * q + 4, :].bitcast(I32)
-            nc.sync.dma_start(
+            (nc.sync, nc.scalar)[q % 2].dma_start(
                 out=x_plane[32 * q : 32 * q + 32, :].bitcast(I32), in_=rows.unsqueeze(0).to_broadcast([8, 4, T // 4])
             )
         nc.sync.dma_start(offsets[:], offs)

@@ -37,7 +37,7 @@ def tile_moe_cas_mlp_relu2_kernel(tc, x_words, x_scales, w, w1_words, w1_scales,
         psum = ctx.enter_context(tc.psum_pool(name="psum", bufs=1))
 
         def tile(name, shape, dtype, **place):
-            return keep.tile(shape, dtype, name=name, align_bytes=64, **place)
+            return keep.tile(shape, dtype, name=name, align_bytes=256, **place)
 
         offsets = keep.tile([P, S // PER_COLUMN], U16, name="offsets")
         x_codes = tile("x_codes", [P, T], U32)

from contextlib import ExitStack

import concourse.mybir as mybir

K, T, S, H, N = 512, 1024, 512, 512, 512
FLOPS = 2 * K * N * T + 2 * K * H * S + 2 * H * N * S

F32 = mybir.dt.float32
BF16 = mybir.dt.bfloat16
I32 = mybir.dt.int32
U32 = mybir.dt.uint32
U16 = mybir.dt.uint16
U8 = mybir.dt.uint8
FP8X4 = mybir.dt.float8_e4m3fn_x4
FP4X4 = mybir.dt.float4_e2m1fn_x4
ACT = mybir.ActivationFunctionType
ALU = mybir.AluOpType

P = 128
PACK = 4
BANK = 512
CHUNK = 128
HALF = S // 2
BANDS = N // P
PER_COLUMN = 16
HELP = CHUNK // 2
SPLIT = BANK - CHUNK
WIDTHS = (512, 256, 128)
RUN = 4


def tile_moe_cas_mlp_relu2_kernel(tc, x_words, x_scales, w, w1_words, w1_scales, w2_words, w2_scales, offs, out):
    nc = tc.nc
    on_vector, on_scalar = nc.vector.tensor_copy, nc.scalar.copy
    with ExitStack() as ctx:
        keep = ctx.enter_context(tc.tile_pool(name="keep", bufs=1))
        psum = ctx.enter_context(tc.psum_pool(name="psum", bufs=1))

        def tile(name, shape, dtype, **place):
            return keep.tile(shape, dtype, name=name, align_bytes=256, **place)

        offsets = keep.tile([P, S // PER_COLUMN], U16, name="offsets")
        x_codes = tile("x_codes", [P, T], U32)
        x_plane = tile("x_plane", [P, T], U8)
        w1_raw = tile("w1_raw", [P, 2 * H], U8)
        w1_raw_plane = tile("w1_raw_plane", [P, H], U8)
        w1_codes = [tile("w1_codes%d" % u, [P, H], U8) for u in range(2)]
        w1_plane = tile("w1_plane", [P, H], U8)
        w2_codes = tile("w2_codes", [P, 2 * N], U8)
        w_early = tile("w_early", [P, PACK, 2 * P], F32)
        w_late = tile("w_late", [P, PACK, 2 * P], F32)
        w_codes = tile("w_codes", [P, N], U32)
        w_plane = tile("w_plane", [P, N], U8)
        windows = [tile("window%d" % b, [P, T], F32) for b in range(BANDS)]
        slot_plane = tile("slot_plane", [P, S], U8)
        relu = tile("relu", [P, CHUNK, PACK], F32)
        h = tile("h", [P, HALF, PACK], BF16)
        h_codes = tile("h_codes", [P, HALF], U32)
        h_plane = tile("h_plane", [P, HALF], U8)

        nc.vector.memset(w1_raw_plane[:].bitcast(I32), 0)

        def load_bytes(target, source, queue=nc.sync):
            queue.dma_start(out=target.bitcast(I32), in_=source.bitcast(I32))

        def load_scale_rows(plane, rows, queues):
            for q, queue in enumerate(queues):
                load_bytes(plane[32 * q : 32 * q + 4, :], rows[4 * q : 4 * q + 4, :], queue)

        w_rows = w.rearrange("(p j) n -> p j n", j=PACK)
        for q in range(4):
            rows = x_scales[0][4 * q : 4 * q + 4, :].bitcast(I32)
            (nc.sync, nc.scalar)[q % 2].dma_start(
                out=x_plane[32 * q : 32 * q + 32, :].bitcast(I32), in_=rows.unsqueeze(0).to_broadcast([8, 4, T // 4])
            )
        nc.sync.dma_start(offsets[:], offs)
        load_bytes(x_codes[:], x_words[0].rearrange("p t d -> p (t d)"))
        load_bytes(w1_raw[:], w1_words[0])
        load_scale_rows(w1_raw_plane, w1_scales[0], [nc.sync] * 4)
        nc.sync.dma_start(out=w_early[:], in_=w_rows[:, :, : 2 * P])
        nc.sync.dma_start(out=w_late[:], in_=w_rows[:, :, 2 * P :])
        load_bytes(w2_codes[:], w2_words[0])

        def entries(first, last):
            return offsets[:, first // PER_COLUMN : last // PER_COLUMN]

        def gather_words(name, first, **place):
            gathered = tile(name, [P, HALF], U32, **place)
            nc.vector.tensor_copy(gathered[:], x_codes[:].indirect(entries(first, first + HALF)))
            return gathered

        def round_w(name, raw):
            rounded = tile(name, [P, raw.shape[2], PACK], BF16)
            nc.vector.tensor_copy(
                out=rounded[:].rearrange("p (c i) j -> p c j i", i=RUN),
                in_=raw.rearrange("p j (c i) -> p c j i", i=RUN),
            )
            return rounded

        def quantize(codes, plane, values):
            nc.vector.quantize_mx(out=codes.bitcast(FP8X4), scales=plane, in_=values.rearrange("p c j -> p (c j)"))

        def quantize_w(first, rounded):
            columns = slice(first, first + rounded.shape[1])
            quantize(w_codes[:, columns], w_plane[:, columns], rounded[:])

        def product(acc, lhsT, lhsT_scale, rhs, rhs_scale):
            nc.tensor.matmul_mx(
                out=acc, lhsT=lhsT, lhsT_scale=lhsT_scale, rhs=rhs, rhs_scale=rhs_scale, start=True, stop=True
            )

        def light(b, first, count, bank, copy):
            rows = slice(b * P, (b + 1) * P)
            tokens = slice(first, first + count)
            acc = psum.tile([P, count], F32, name="light_acc", tag=bank)
            done = 0
            for width in WIDTHS:
                if count - done >= width:
                    part = slice(first + done, first + done + width)
                    product(
                        acc[:, done : done + width],
                        w_codes[:, rows].bitcast(FP8X4),
                        w_plane[:, rows],
                        x_codes[:, part].bitcast(FP8X4),
                        x_plane[:, part],
                    )
                    done = done + width
            copy(out=windows[b][:, tokens], in_=acc[:])

        def hidden(first, words, bank, target, ts=range(PACK)):
            count = words.shape[1]
            acc = psum.tile([P, len(ts), count], F32, name="hidden_acc", tag=bank)
            for column, t in enumerate(ts):
                product(
                    acc[:, column, :],
                    w1_codes[t // 2][:, 2 * (t % 2) * P : 2 * (t % 2 + 1) * P].bitcast(FP4X4),
                    w1_plane[:, t * P : (t + 1) * P],
                    words.bitcast(FP8X4),
                    slot_plane[:, first : first + count],
                )
            nc.scalar.activation(out=target, in_=acc[:].rearrange("p t s -> p s t"), func=ACT.Relu)

        def heavy(bands, bank):
            acc = psum.tile([P, BANK], F32, name="z_acc", tag=bank)
            for place, b in enumerate(bands):
                product(
                    acc[:, place * HALF : (place + 1) * HALF],
                    w2_codes[:, 2 * b * P : 2 * (b + 1) * P].bitcast(FP4X4),
                    w2_plane[:, b * P : (b + 1) * P],
                    h_codes[:].bitcast(FP8X4),
                    h_plane[:],
                )
            return acc

        def store(b, queue):
            queue.dma_start(out=out[b * P : (b + 1) * P, :], in_=windows[b][:])

        for u in range(2):
            nc.scalar.copy(
                out=w1_codes[u][:].bitcast(U16).rearrange("p (t m) -> p t m", t=2),
                in_=w1_raw[:].bitcast(U16).rearrange("p (m t) -> p t m", t=PACK)[:, 2 * u : 2 * u + 2, :],
            )
        nc.vector.tensor_copy(slot_plane[:], x_plane[:].indirect(offsets[:]))
        words = gather_words("first_words", 0)
        for first, last in ((0, 1), (1, 2), (2, PACK)):
            nc.vector.tensor_copy(
                out=w1_plane[:].rearrange("p (t m) -> p t m", t=PACK)[:, first:last, :],
                in_=w1_raw_plane[:].rearrange("p (m t) -> p t m", t=PACK)[:, first:last, :],
            )
        w2_plane = w1_raw[:, :N]
        load_scale_rows(w2_plane, w2_scales[0], [nc.scalar, nc.scalar, nc.sync, nc.sync])
        later_words = gather_words("later_words", HALF, tag="w1_raw_plane")

        rounded_early = [round_w("rounded%d" % b, w_early[:, :, b * P : (b + 1) * P]) for b in (0, 1)]
        for b in (0, 1):
            quantize_w(b * P, rounded_early[b])

        pairs = tile("relu_pairs", [P, 2, CHUNK, 2], F32)
        hidden(0, words[:, :CHUNK], "bank0", pairs[:, 0], (0, 1))
        hidden(0, words[:, :CHUNK], "bank4", pairs[:, 1], (2, 3))
        hidden(CHUNK, words[:, CHUNK:], "bank1", relu[:])
        nc.scalar.activation(out=h[:, HALF - HELP :, :], in_=relu[:, CHUNK - HELP :, :], func=ACT.Square)
        later_pairs = tile("later_pairs", [P, 2, HALF, 2], F32)
        hidden(HALF, later_words[:], "bank2", later_pairs[:, 0], (0, 1))
        hidden(HALF, later_words[:], "bank3", later_pairs[:, 1], (2, 3))

        by_slot = pairs[:].rearrange("p u s e -> p s u e")
        nc.vector.tensor_tensor(h[:, :CHUNK, :].rearrange("p s (u e) -> p s u e", e=2), by_slot, by_slot, ALU.mult)
        rounded_late = round_w("rounded_late", w_late[:])
        rest = relu[:, : CHUNK - HELP, :]
        nc.vector.tensor_tensor(h[:, CHUNK : HALF - HELP, :], rest, rest, ALU.mult)
        quantize_w(2 * P, rounded_late)
        quantize(h_codes[:], h_plane[:], h[:])
        late = later_pairs[:].rearrange("p u s e -> p s u e")
        nc.gpsimd.tensor_tensor(h[:].rearrange("p s (u e) -> p s u e", e=2), late, late, ALU.mult)

        z = [tile("z%d" % b, [P, S], F32) for b in range(BANDS)]

        def take_z(bands, u, bank, copy):
            acc = heavy(bands, bank)
            for place, b in enumerate(bands):
                copy(out=z[b][:, u * HALF : (u + 1) * HALF], in_=acc[:, place * HALF : (place + 1) * HALF])

        def scatter_on_scalar(b, first, last):
            nc.scalar.activation(windows[b][:].indirect(entries(first, last)), z[b][:, first:last], ACT.Copy)

        def scatter_on_vector(b, first, last):
            nc.vector.tensor_copy(windows[b][:].indirect(entries(first, last)), z[b][:, first:last])

        light(0, 0, BANK, "bank5", on_scalar)
        light(1, 0, BANK, "bank6", on_vector)
        light(0, BANK, BANK, "bank7", on_scalar)
        light(1, BANK, BANK, "bank0", on_vector)
        light(2, 0, BANK, "bank3", on_scalar)
        light(2, BANK, BANK, "bank2", on_vector)
        take_z((0, 1), 0, "bank4", on_scalar)
        take_z((2, 3), 0, "bank1", on_vector)
        scatter_on_scalar(0, 0, HALF)
        scatter_on_vector(2, 0, CHUNK)

        quantize(h_codes[:], h_plane[:], h[:])
        light(3, 0, SPLIT, "bank4", on_scalar)
        light(3, BANK, BANK, "bank1", on_vector)
        light(3, SPLIT, BANK - SPLIT, "bank2", on_vector)
        scatter_on_scalar(1, 0, CHUNK)
        take_z((2, 3), 1, "bank5", on_vector)
        take_z((0, 1), 1, "bank7", on_scalar)

        scatter_on_scalar(0, HALF, S)
        store(0, nc.scalar)
        scatter_on_scalar(1, CHUNK, S)
        for b, first in ((2, CHUNK), (3, 0)):
            scatter_on_vector(b, first, S)
            store(b, nc.sync)
        store(1, nc.scalar)
